import numpy as np
import ml_dtypes


def mxq(x, axis, fmt="e4m3"):
    dtype, down = {"e4m3": (ml_dtypes.float8_e4m3fn, 7), "e5m2": (ml_dtypes.float8_e5m2, 14)}[fmt]
    v = np.moveaxis(np.asarray(x, np.float32).astype(ml_dtypes.bfloat16).astype(np.float64), axis, -1)
    blocks = v.reshape(v.shape[:-1] + (-1, 32))
    amax = np.abs(blocks).max(-1, keepdims=True)
    byte = np.maximum(np.where(amax > 0, np.frexp(amax)[1] - 1 + 127, 0) - down, 1)
    scale = np.exp2(byte - 127.0)
    codes = (blocks / scale).astype(np.float32).astype(dtype).astype(np.float64)
    return np.moveaxis((codes * scale).reshape(v.shape), -1, axis)


WIDE = False


def mx_kscale(k):
    if not WIDE:
        return np.ones(k)
    levels = np.array([10, -10, 5, -5, 0])
    if k % 512:
        return np.exp2(np.random.permutation(np.resize(levels, k // 32))).repeat(32)
    a = np.empty((k // 512, 16))
    for p in range(k // 512):
        a[p, :8] = np.random.permutation(np.resize(levels, 8))
        for g in range(8):
            far = levels[np.abs(levels - a[p, g]) >= 10]
            a[p, g + 8] = far[np.random.randint(len(far))]
    return np.exp2(a.ravel()).repeat(32)


BF16 = ml_dtypes.bfloat16


def bf(x):
    return np.asarray(x, np.float32).astype(BF16)


def f64(x):
    return np.asarray(x).astype(np.float64)


E2M1 = np.array([0.0, 0.5, 1.0, 1.5, 2.0, 3.0, 4.0, 6.0, -0.0, -0.5, -1.0, -1.5, -2.0, -3.0, -4.0, -6.0])


def pack_weight(w, fmt):
    k, n = w.shape
    w = f64(bf(w)).reshape(k // 32, 32, n)
    amax = np.abs(w).max(1)
    if fmt == "e4m3":
        byte = np.frexp(amax)[1] - 1 + 127 - 7
    else:
        mant, ex = np.frexp(amax / 6.0)
        byte = np.where(mant > 0.5, ex, ex - 1) + 127
    byte = np.clip(np.where(amax > 0, byte, 1), 1, 254)
    scaled = (w * np.exp2(127.0 - byte)[:, None, :]).reshape(k, n).astype(np.float32)
    by_word = np.ascontiguousarray(scaled.reshape(k // 512, 128, 4, n).transpose(0, 1, 3, 2))
    if fmt == "e4m3":
        words = by_word.astype(ml_dtypes.float8_e4m3fn).view(np.uint8)
    else:
        c = by_word.astype(ml_dtypes.float4_e2m1fn).view(np.uint8) & 0xF
        words = c[..., 0::2] | (c[..., 1::2] << 4)
    return np.ascontiguousarray(words), np.ascontiguousarray(byte.astype(np.uint8).reshape(k // 512, 16, n))


def unpack_weight(words, scales, fmt):
    g, p, n, _ = words.shape
    if fmt == "e4m3":
        vals = np.ascontiguousarray(words).view(ml_dtypes.float8_e4m3fn).astype(np.float64)
    else:
        nib = np.empty((g, p, n, 4), np.uint8)
        nib[..., 0::2] = words & 0xF
        nib[..., 1::2] = words >> 4
        vals = E2M1[nib]
    vals = vals * np.repeat(np.exp2(scales.astype(np.float64) - 127.0), 8, axis=1)[..., None]
    return vals.transpose(0, 1, 3, 2).reshape(g * 512, n)
def pack4(w):
    words, scales = pack_weight(w, "e2m1")
    return words.reshape(words.shape[0], 128, -1), scales


def unpack4(words, scales):
    return unpack_weight(words.reshape(words.shape[0], 128, -1, 2), scales, "e2m1")


T, A, E, P, R = 512, 512, 2048, 1024, 1024


def draw0():
    s = mx_kscale(A)
    u = mx_kscale(P)
    t = mx_kscale(E)
    resp = np.random.standard_normal((P, E)) / np.sqrt(P) / u[:, None] / t
    resp_words, resp_scales = pack4(resp)
    return {"sig": bf(np.random.standard_normal((T, A)) * s),
            "inc": bf(np.random.standard_normal((A, E)) / np.sqrt(A) / s[:, None]),
            "bias": bf(0.3 * np.random.standard_normal(E)),
            "gain": bf((1 + 0.2 * np.random.standard_normal(E)) * t),
            "coef": bf(np.random.standard_normal((R, P)) * E ** -0.25 * u),
            "resp_words": resp_words,
            "resp_scales": resp_scales}


def core(sig, inc, bias, gain, coef, resp_words, resp_scales):
    field = mxq(f64(sig), 1, "e4m3") @ mxq(f64(inc), 0, "e4m3")
    refl = f64(gain) * np.tanh(field + f64(bias))
    outgoing = mxq(f64(coef), 1, "e4m3") @ unpack4(resp_words, resp_scales)
    return mxq(refl, 1, "e4m3") @ mxq(outgoing, 1, "e4m3").T


def e4m3fn_bytes(y):
    return np.clip(np.asarray(y, np.float64), -448.0, 448.0).astype(np.float32).astype(ml_dtypes.float8_e4m3fn).view(np.uint8)


def e4m3fn_values(b):
    return np.asarray(b, np.uint8).view(ml_dtypes.float8_e4m3fn).astype(np.float64)


def setup_inputs():
    d = draw0()
    x0 = np.asarray(d['inc']).astype(np.float64)
    s = (np.max(np.abs(x0), axis=(1,), keepdims=True) / 448.0).astype(np.float32)
    out = {}
    for k, v in d.items():
        if k == 'inc':
            out['inc_bytes'] = e4m3fn_bytes(x0 / s.astype(np.float64))
            out['inc_scale'] = s
        else:
            out[k] = v
    return out


def reference(sig, inc_bytes, inc_scale, bias, gain, coef, resp_words, resp_scales):
    return core(sig, e4m3fn_values(inc_bytes) * inc_scale.astype(np.float64), bias, gain, coef, resp_words, resp_scales)

@@ -1,0 +1,425 @@
+from contextlib import ExitStack
+
+import concourse.mybir as mybir
+from concourse.masks import make_identity
+
+T, A, E, PATHS, R = 512, 512, 2048, 1024, 1024
+FLOPS = 2 * (T * A * E + R * PATHS * E + T * E * R)
+
+F32 = mybir.dt.float32
+BF16 = mybir.dt.bfloat16
+I32 = mybir.dt.int32
+U32 = mybir.dt.uint32
+U8 = mybir.dt.uint8
+FP8 = mybir.dt.float8_e4m3fn
+FP8X4 = mybir.dt.float8_e4m3fn_x4
+FP4X4 = mybir.dt.float4_e2m1fn_x4
+MULT = mybir.AluOpType.mult
+TANH = mybir.ActivationFunctionType.Tanh
+
+P = 128
+GROUPS = E // 512
+N_COEF = R // 128
+HALF_R = 512
+
+
+def tile_active_surface_link_s11_kernel(
+    tc, sig, inc_bytes, inc_scale, bias, gain, coef, resp_words, resp_scales, out
+):
+    nc = tc.nc
+    with ExitStack() as ctx:
+        keep = ctx.enter_context(tc.tile_pool(name="keep", bufs=1))
+        work = ctx.enter_context(tc.tile_pool(name="work", bufs=2))
+        psum = ctx.enter_context(tc.psum_pool(name="psum", bufs=8))
+        ctx.enter_context(tc.manual_schedule())
+
+        def kept(name, shape, dtype):
+            return keep.tile(shape, dtype, name=name, tag=name, align_bytes=64)
+
+        coef_raw = [kept("coef_raw%d" % n, [P, PATHS], BF16) for n in range(N_COEF)]
+        coef_codes = [kept("coef_codes%d" % n, [P, 2, 128], U32) for n in range(N_COEF)]
+        coef_scales = [kept("coef_scales%d" % n, [P, 2, 128], U8) for n in range(N_COEF)]
+        resp_raw = [kept("resp_raw%d" % g, [P, 2, 1024], U8) for g in range(GROUPS)]
+        resp_perm = [kept("resp_perm%d" % g, [P, 2, 1024], U8) for g in range(GROUPS)]
+        rs_raw = kept("rs_raw", [P, 2, E], U8)
+        rs_perm = kept("rs_perm", [P, 2, E], U8)
+        inc_b = [kept("inc_b%d" % g, [P, 4, 512], U8) for g in range(GROUPS)]
+        inc_sc = kept("inc_sc", [P, 4], F32)
+        inc_codes = [kept("inc_codes%d" % g, [P, 512], U32) for g in range(GROUPS)]
+        inc_scales = [kept("inc_scales%d" % g, [P, 512], U8) for g in range(GROUPS)]
+        sig_raw = kept("sig_raw", [P, 4, A], BF16)
+        sig_grp = kept("sig_grp", [P, T, 4], BF16)
+        sig_codes = kept("sig_codes", [P, T], U32)
+        sig_scales = kept("sig_scales", [P, T], U8)
+        refl_codes = [kept("refl_codes%d" % g, [P, T], U32) for g in range(GROUPS)]
+        refl_scales = [kept("refl_scales%d" % g, [P, T], U8) for g in range(GROUPS)]
+        outg_codes = [[kept("outg_codes%d_%d" % (h, g), [P, HALF_R], U32) for g in range(GROUPS)] for h in range(2)]
+        outg_scales = [[kept("outg_scales%d_%d" % (h, g), [P, HALF_R], U8) for g in range(GROUPS)] for h in range(2)]
+        ident = kept("ident", [P, P], F32)
+        ident_b = kept("ident_b", [P, P], BF16)
+        vec_b = kept("vec_b", [P, 512], BF16)
+        vec_t = kept("vec_t", [P, GROUPS, 8], F32)
+        dummy = kept("dummy", [P, 1], F32)
+        zeros = kept("zeros", [P, 512], BF16)
+
+        nc.vector.memset(rs_raw[:].rearrange("p g e -> p (g e)").bitcast(I32), 0)
+        nc.vector.memset(zeros[:], 0.0)
+        nc.vector.memset(dummy[:], 0.0)
+        make_identity(nc, ident[:])
+        nc.gpsimd.memset(vec_b[:], 0.0)
+        make_identity(nc, ident_b[:])
+        nc.scalar.activation(dummy[:], dummy[:], TANH)
+
+        def load_coef(n):
+            nc.sync.dma_start(out=coef_raw[n][:], in_=coef[128 * n : 128 * (n + 1), :])
+
+        def load_resp(grp):
+            nc.sync.dma_start(
+                out=resp_raw[grp][:].bitcast(I32),
+                in_=resp_words[:, :, 1024 * grp : 1024 * (grp + 1)].rearrange("g p b -> p g b").bitcast(I32),
+            )
+
+        def load_inc(grp):
+            cols = slice(512 * grp, 512 * (grp + 1))
+            nc.sync.dma_start(out=inc_b[grp][:], in_=inc_bytes[:, cols].rearrange("(p j) e -> p j e", j=4))
+
+        load_coef(0)
+        load_coef(1)
+        for q in range(4):
+            nc.sync.dma_start(
+                out=rs_raw[32 * q : 32 * q + 4, :, :].bitcast(I32),
+                in_=resp_scales[:, 4 * q : 4 * q + 4, :].rearrange("g q e -> q g e").bitcast(I32),
+            )
+        load_resp(0)
+        load_resp(1)
+        nc.sync.dma_start(out=inc_sc[:], in_=inc_scale.rearrange("(p j) o -> p (j o)", j=4))
+        load_inc(0)
+        load_resp(2)
+        load_resp(3)
+        load_coef(2)
+        load_coef(3)
+        nc.sync.dma_start(out=sig_raw[:], in_=sig.rearrange("(n p) a -> p n a", p=P))
+        for v, vec in enumerate((bias, gain)):
+            nc.sync.dma_start(
+                out=vec_b[4 * v : 4 * v + 4, :].rearrange("t (b i) -> t b i", i=8),
+                in_=vec.rearrange("(b t i) -> t b i", t=4, i=8),
+            )
+        load_inc(1)
+        load_inc(2)
+        load_inc(3)
+        load_coef(4)
+        load_coef(5)
+        load_coef(6)
+        load_coef(7)
+
+        def warm_up(count):
+            bank = psum.tile([P, 512], F32, name="bank", tag="bank")
+            for i in range(count):
+                nc.tensor.matmul(bank[:], lhsT=zeros[:, 0:P], rhs=zeros[:], start=True, stop=True)
+
+        coef_bank, coef_grp = {}, {}
+
+        def t_coef(n):
+            bank = psum.tile([P, 512], F32, name="bank", tag="bank")
+            words = coef_raw[n][:].bitcast(F32)
+            for g in range(2):
+                for u in range(2):
+                    j = 2 * g + u
+                    nc.tensor.transpose(
+                        bank[:, 128 * j : 128 * (j + 1)], words[:, 256 * g + u : 256 * (g + 1) : 2], ident[:]
+                    )
+            coef_bank[n] = bank
+
+        def copy(engine, dst, src):
+            if engine == "v":
+                nc.vector.tensor_copy(out=dst, in_=src)
+            else:
+                nc.scalar.copy(out=dst, in_=src)
+
+        def c_coef(n, engine):
+            grp = work.tile([P, 2, 128, 4], BF16, name="coef_grp", tag="coef_grp", bufs=4, align_bytes=64)
+            coef_grp[n] = grp
+            copy(
+                engine,
+                grp[:].rearrange("p g r t -> p (g r t)").bitcast(F32).rearrange("p (g r u) -> p g r u", g=2, u=2),
+                coef_bank[n][:].rearrange("p (g u r) -> p g r u", g=2, u=2),
+            )
+
+        def q_coef(n):
+            nc.vector.quantize_mx(
+                out=coef_codes[n][:].rearrange("p g r -> p (g r)").bitcast(FP8X4),
+                scales=coef_scales[n][:].rearrange("p g r -> p (g r)"),
+                in_=coef_grp[n][:].rearrange("p g r t -> p (g r t)"),
+            )
+
+        sig_bank = {}
+
+        def t_sig(pair):
+            bank = psum.tile([P, 512], F32, name="bank", tag="bank")
+            for i in range(2):
+                words = sig_raw[:, 2 * pair + i, :].bitcast(F32)
+                for u in range(2):
+                    j = 2 * i + u
+                    nc.tensor.transpose(bank[:, 128 * j : 128 * (j + 1)], words[:, u:256:2], ident[:])
+            sig_bank[pair] = bank
+
+        def c_sig(pair, engine):
+            dst = sig_grp[:, 256 * pair : 256 * (pair + 1), :].rearrange("p r t -> p (r t)").bitcast(F32)
+            copy(
+                engine,
+                dst.rearrange("p (i r u) -> p i r u", i=2, u=2),
+                sig_bank[pair][:].rearrange("p (i u r) -> p i r u", i=2, u=2),
+            )
+
+        def q_sig():
+            nc.vector.quantize_mx(
+                out=sig_codes[:].bitcast(FP8X4), scales=sig_scales[:], in_=sig_grp[:].rearrange("p r t -> p (r t)")
+            )
+
+        def perm_scales(g):
+            nc.vector.tensor_copy(
+                out=rs_perm[:, g, :].bitcast(I32).rearrange("p (t b w) -> p t b w", t=4, w=2),
+                in_=rs_raw[:, g, :].bitcast(I32).rearrange("p (b t w) -> p t b w", t=4, w=2),
+            )
+
+        def perm_resp(grp):
+            for g in range(2):
+                nc.vector.tensor_copy(
+                    out=resp_perm[grp][:, g, :].bitcast(I32).rearrange("p (t b w) -> p t b w", t=4, w=4),
+                    in_=resp_raw[grp][:, g, :].bitcast(I32).rearrange("p (b t w) -> p t b w", t=4, w=4),
+                )
+
+        def vectors():
+            bank = psum.tile([P, 8, P], BF16, name="bank", tag="bank")
+            for grp in range(GROUPS):
+                cols = slice(128 * grp, 128 * (grp + 1))
+                nc.tensor.transpose(bank[:, grp, :], vec_b[:, cols], ident_b[:])
+            nc.vector.tensor_copy(out=vec_t[:], in_=bank[:, 0:GROUPS, 0:8])
+
+        inc_wid, inc_grp = {}, {}
+
+        def widen(grp):
+            wid = work.tile([P, 4, 512], BF16, name="inc_wid", tag="inc_wid", align_bytes=64)
+            inc_wid[grp] = wid
+            for j in range(4):
+                nc.vector.tensor_scalar(
+                    out=wid[:, j, :].rearrange("p (t q i) -> p q t i", t=4, i=8),
+                    in0=inc_b[grp][:, j, :].bitcast(FP8).rearrange("p (q t i) -> p q t i", t=4, i=8),
+                    scalar1=inc_sc[:, j : j + 1],
+                    scalar2=None,
+                    op0=MULT,
+                )
+
+        def interleave(grp):
+            g4 = work.tile([P, 512, 4], BF16, name="inc_grp", tag="inc_grp", align_bytes=64)
+            inc_grp[grp] = g4
+            nc.vector.tensor_copy(
+                out=g4[:].rearrange("p (c i) j -> p c j i", i=4),
+                in_=inc_wid[grp][:].rearrange("p j (c i) -> p c j i", i=4),
+            )
+
+        def q_inc(grp):
+            nc.vector.quantize_mx(
+                out=inc_codes[grp][:].bitcast(FP8X4),
+                scales=inc_scales[grp][:],
+                in_=inc_grp[grp][:].rearrange("p c j -> p (c j)"),
+            )
+
+        outg = {}
+
+        def outgoing(n, grp, engine):
+            h = n // 4
+            if (h, grp) not in outg:
+                outg[(h, grp)] = work.tile(
+                    [P, HALF_R, 4], BF16, name="outg", tag="outg", bufs=6, align_bytes=64
+                )
+            bank = psum.tile([P, 512], F32, name="bank", tag="bank")
+            for t in range(4):
+                lo = 256 * t
+                so = 512 * t + 128 * grp
+                for g in range(2):
+                    nc.tensor.matmul_mx(
+                        out=bank[:, 128 * t : 128 * (t + 1)],
+                        lhsT=resp_perm[grp][:, g, lo : lo + 256].bitcast(FP4X4),
+                        lhsT_scale=rs_perm[:, g, so : so + 128],
+                        rhs=coef_codes[n][:, g, :].bitcast(FP8X4),
+                        rhs_scale=coef_scales[n][:, g, :],
+                        start=(g == 0),
+                        stop=(g == 1),
+                    )
+            r0 = 128 * (n % 4)
+            copy(engine, outg[(h, grp)][:, r0 : r0 + 128, :], bank[:].rearrange("p (t r) -> p r t", t=4))
+
+        def q_outg(h, grp):
+            nc.vector.quantize_mx(
+                out=outg_codes[h][grp][:].bitcast(FP8X4),
+                scales=outg_scales[h][grp][:],
+                in_=outg[(h, grp)][:].rearrange("p r t -> p (r t)"),
+            )
+
+        refl_tanh, refl_grp = {}, {}
+
+        def field(grp):
+            th = work.tile([P, 4, T], F32, name="th", tag="th", bufs=3, align_bytes=64)
+            refl_tanh[grp] = th
+            for t in range(4):
+                bank = psum.tile([P, 512], F32, name="bank", tag="bank")
+                nc.tensor.matmul_mx(
+                    out=bank[:],
+                    lhsT=inc_codes[grp][:, 128 * t : 128 * (t + 1)].bitcast(FP8X4),
+                    lhsT_scale=inc_scales[grp][:, 128 * t : 128 * (t + 1)],
+                    rhs=sig_codes[:].bitcast(FP8X4),
+                    rhs_scale=sig_scales[:],
+                    start=True,
+                    stop=True,
+                )
+                nc.scalar.activation(th[:, t, :], bank[:], TANH, bias=vec_t[:, grp, t : t + 1])
+
+        def apply_gain(grp):
+            rf = work.tile([P, T, 4], BF16, name="refl", tag="refl", bufs=2, align_bytes=64)
+            refl_grp[grp] = rf
+            nc.vector.tensor_tensor(
+                out=rf[:].rearrange("p (c i) t -> p c t i", i=4),
+                in0=refl_tanh[grp][:].rearrange("p t (c i) -> p c t i", i=4),
+                in1=vec_t[:, grp, 4:8].unsqueeze(1).unsqueeze(3).to_broadcast([P, T // 4, 4, 4]),
+                op=MULT,
+            )
+
+        def q_refl(grp):
+            nc.vector.quantize_mx(
+                out=refl_codes[grp][:].bitcast(FP8X4),
+                scales=refl_scales[grp][:],
+                in_=refl_grp[grp][:].rearrange("p n t -> p (n t)"),
+            )
+
+        def final_pass(h, m, grp, bank, recv=slice(0, HALF_R)):
+            cols = slice(128 * m, 128 * (m + 1))
+            nc.tensor.matmul_mx(
+                out=bank[:, recv],
+                lhsT=refl_codes[grp][:, cols].bitcast(FP8X4),
+                lhsT_scale=refl_scales[grp][:, cols],
+                rhs=outg_codes[h][grp][:, recv].bitcast(FP8X4),
+                rhs_scale=outg_scales[h][grp][:, recv],
+                start=(grp == 0),
+                stop=(grp == GROUPS - 1),
+            )
+
+        def store(h, m, bank, engine, recv=slice(0, HALF_R)):
+            res = work.tile([P, HALF_R], F32, name="res", tag="res", bufs=8, align_bytes=64)
+            copy(engine, res[:, recv], bank[:, recv])
+            nc.sync.dma_start(
+                out=out[128 * m : 128 * (m + 1), HALF_R * h + recv.start : HALF_R * h + recv.stop], in_=res[:, recv]
+            )
+
+        warm_up(4)
+        t_coef(0)
+        t_coef(1)
+        warm_up(3)
+        c_coef(0, "v")
+        c_coef(1, "s")
+        q_coef(0)
+        perm_scales(0)
+        perm_scales(1)
+        q_coef(1)
+        perm_resp(0)
+        outgoing(0, 0, "s")
+        outgoing(1, 0, "s")
+        perm_resp(1)
+        widen(0)
+        outgoing(0, 1, "s")
+        outgoing(1, 1, "s")
+        perm_resp(2)
+        interleave(0)
+        outgoing(0, 2, "s")
+        outgoing(1, 2, "s")
+        perm_resp(3)
+        t_coef(2)
+        t_coef(3)
+        widen(1)
+        q_inc(0)
+        c_coef(2, "s")
+        c_coef(3, "s")
+        outgoing(0, 3, "s")
+        q_coef(2)
+        interleave(1)
+        outgoing(1, 3, "s")
+        q_coef(3)
+        t_sig(0)
+        t_sig(1)
+        vectors()
+        c_sig(0, "s")
+        c_sig(1, "s")
+        widen(2)
+        q_inc(1)
+        q_sig()
+        for grp in range(4):
+            outgoing(2, grp, "s")
+        interleave(2)
+        field(0)
+        t_coef(4)
+        t_coef(5)
+        widen(3)
+        q_inc(2)
+        c_coef(4, "s")
+        c_coef(5, "s")
+        outgoing(3, 0, "s")
+        t_coef(6)
+        t_coef(7)
+        c_coef(6, "s")
+        c_coef(7, "s")
+        q_coef(4)
+        q_coef(5)
+        apply_gain(0)
+        outgoing(3, 1, "s")
+        q_coef(6)
+        q_coef(7)
+        interleave(3)
+        q_refl(0)
+        q_inc(3)
+        for grp in range(2, 4):
+            outgoing(3, grp, "s")
+        field(1)
+        q_outg(0, 0)
+        q_outg(0, 1)
+        for n in range(4, 8):
+            outgoing(n, 0, "s")
+        apply_gain(1)
+        q_outg(0, 2)
+        q_outg(0, 3)
+        q_refl(1)
+        field(2)
+        for n in range(4, 8):
+            outgoing(n, 1, "s")
+        q_outg(1, 0)
+        apply_gain(2)
+        field(3)
+        q_refl(2)
+        fin = [psum.tile([P, 512], F32, name="bank", tag="bank") for m in range(4)]
+        for grp in (0, 1):
+            for m in range(4):
+                final_pass(0, m, grp, fin[m])
+        q_outg(1, 1)
+        for n in range(4, 8):
+            outgoing(n, 2, "s")
+        apply_gain(3)
+        q_outg(1, 2)
+        q_refl(3)
+        for n in range(4, 8):
+            outgoing(n, 3, "v" if n % 2 else "s")
+        q_outg(1, 3)
+        for m in range(4):
+            for grp in (2, 3):
+                final_pass(0, m, grp, fin[m])
+        for m in range(4):
+            store(0, m, fin[m], "v" if m % 2 else "s")
+        for m in range(3):
+            bank = psum.tile([P, 512], F32, name="bank", tag="bank")
+            for grp in range(GROUPS):
+                final_pass(1, m, grp, bank)
+            store(1, m, bank, "v" if m % 2 else "s")
+        for part in range(2):
+            bank = psum.tile([P, 512], F32, name="bank", tag="bank")
+            cols = slice(256 * part, 256 * (part + 1))
+            for grp in range(GROUPS):
+                final_pass(1, 3, grp, bank, cols)
+            store(1, 3, bank, "s" if part else "v", cols)

@@ -21,6 +21,7 @@ P = 128
 GROUPS = E // 512
 N_COEF = R // 128
 HALF_R = 512
+OUTG_BUFS = 6
 
 
 def tile_active_surface_link_s11_kernel(
@@ -30,19 +31,20 @@ def tile_active_surface_link_s11_kernel(
     with ExitStack() as ctx:
         keep = ctx.enter_context(tc.tile_pool(name="keep", bufs=1))
         work = ctx.enter_context(tc.tile_pool(name="work", bufs=2))
-        psum = ctx.enter_context(tc.psum_pool(name="psum", bufs=8))
+        psum = ctx.enter_context(tc.psum_pool(name="psum", bufs=1))
         ctx.enter_context(tc.manual_schedule())
 
         def kept(name, shape, dtype):
             return keep.tile(shape, dtype, name=name, tag=name, align_bytes=64)
 
         coef_raw = [kept("coef_raw%d" % n, [P, PATHS], BF16) for n in range(N_COEF)]
-        coef_codes = [kept("coef_codes%d" % n, [P, 2, 128], U32) for n in range(N_COEF)]
-        coef_scales = [kept("coef_scales%d" % n, [P, 2, 128], U8) for n in range(N_COEF)]
+        coef_codes = [[kept("coef_codes%d_%d" % (h, g), [P, HALF_R], U32) for g in range(2)] for h in range(2)]
+        coef_scales = [[kept("coef_scales%d_%d" % (h, g), [P, HALF_R], U8) for g in range(2)] for h in range(2)]
         resp_raw = [kept("resp_raw%d" % g, [P, 2, 1024], U8) for g in range(GROUPS)]
         resp_perm = [kept("resp_perm%d" % g, [P, 2, 1024], U8) for g in range(GROUPS)]
         rs_raw = kept("rs_raw", [P, 2, E], U8)
-        rs_perm = kept("rs_perm", [P, 2, E], U8)
+        rs_first = kept("rs_first", [P, 2, 512], U8)
+        rs_rest = kept("rs_rest", [P, 2, E - 512], U8)
         inc_b = [kept("inc_b%d" % g, [P, 4, 512], U8) for g in range(GROUPS)]
         inc_sc = kept("inc_sc", [P, 4], F32)
         inc_codes = [kept("inc_codes%d" % g, [P, 512], U32) for g in range(GROUPS)]
@@ -62,9 +64,17 @@ def tile_active_surface_link_s11_kernel(
         dummy = kept("dummy", [P, 1], F32)
         zeros = kept("zeros", [P, 512], BF16)
 
-        nc.vector.memset(rs_raw[:].rearrange("p g e -> p (g e)").bitcast(I32), 0)
+        ring = list(range(8))
+
+        def take_bank(shape=(P, 512), dtype=F32, hold=False):
+            b = ring.pop(0)
+            if not hold:
+                ring.append(b)
+            return b, psum.tile(list(shape), dtype, name="bank%d" % b, tag="bank%d" % b)
+
         nc.vector.memset(zeros[:], 0.0)
-        nc.vector.memset(dummy[:], 0.0)
+        nc.vector.memset(rs_raw[:].rearrange("p g e -> p (g e)").bitcast(I32), 0)
+        nc.gpsimd.memset(dummy[:], 0.0)
         make_identity(nc, ident[:])
         nc.gpsimd.memset(vec_b[:], 0.0)
         make_identity(nc, ident_b[:])
@@ -72,6 +82,13 @@ def tile_active_surface_link_s11_kernel(
 
         def load_coef(n):
             nc.sync.dma_start(out=coef_raw[n][:], in_=coef[128 * n : 128 * (n + 1), :])
+
+        def load_scales():
+            for q in range(4):
+                nc.sync.dma_start(
+                    out=rs_raw[32 * q : 32 * q + 4, :, :].bitcast(I32),
+                    in_=resp_scales[:, 4 * q : 4 * q + 4, :].rearrange("g q e -> q g e").bitcast(I32),
+                )
 
         def load_resp(grp):
             nc.sync.dma_start(
@@ -83,44 +100,34 @@ def tile_active_surface_link_s11_kernel(
             cols = slice(512 * grp, 512 * (grp + 1))
             nc.sync.dma_start(out=inc_b[grp][:], in_=inc_bytes[:, cols].rearrange("(p j) e -> p j e", j=4))
 
-        load_coef(0)
-        load_coef(1)
-        for q in range(4):
-            nc.sync.dma_start(
-                out=rs_raw[32 * q : 32 * q + 4, :, :].bitcast(I32),
-                in_=resp_scales[:, 4 * q : 4 * q + 4, :].rearrange("g q e -> q g e").bitcast(I32),
-            )
-        load_resp(0)
-        load_resp(1)
-        nc.sync.dma_start(out=inc_sc[:], in_=inc_scale.rearrange("(p j) o -> p (j o)", j=4))
-        load_inc(0)
-        load_resp(2)
-        load_resp(3)
-        load_coef(2)
-        load_coef(3)
-        nc.sync.dma_start(out=sig_raw[:], in_=sig.rearrange("(n p) a -> p n a", p=P))
-        for v, vec in enumerate((bias, gain)):
-            nc.sync.dma_start(
-                out=vec_b[4 * v : 4 * v + 4, :].rearrange("t (b i) -> t b i", i=8),
-                in_=vec.rearrange("(b t i) -> t b i", t=4, i=8),
-            )
-        load_inc(1)
-        load_inc(2)
-        load_inc(3)
-        load_coef(4)
-        load_coef(5)
-        load_coef(6)
-        load_coef(7)
+        def load_inc_scale():
+            nc.sync.dma_start(out=inc_sc[:], in_=inc_scale.rearrange("(p j) o -> p (j o)", j=4))
+
+        def load_sig():
+            nc.sync.dma_start(out=sig_raw[:], in_=sig.rearrange("(p n) a -> p n a", n=4))
+
+        def load_vectors():
+            for v, vec in enumerate((bias, gain)):
+                nc.sync.dma_start(
+                    out=vec_b[4 * v : 4 * v + 4, :].rearrange("t (b i) -> t b i", i=8),
+                    in_=vec.rearrange("(b t i) -> t b i", t=4, i=8),
+                )
 
         def warm_up(count):
-            bank = psum.tile([P, 512], F32, name="bank", tag="bank")
+            b, bank = take_bank()
             for i in range(count):
                 nc.tensor.matmul(bank[:], lhsT=zeros[:, 0:P], rhs=zeros[:], start=True, stop=True)
+
+        def copy(engine, dst, src):
+            if engine == "v":
+                nc.vector.tensor_copy(out=dst, in_=src)
+            else:
+                nc.scalar.copy(out=dst, in_=src)
 
         coef_bank, coef_grp = {}, {}
 
         def t_coef(n):
-            bank = psum.tile([P, 512], F32, name="bank", tag="bank")
+            b, bank = take_bank()
             words = coef_raw[n][:].bitcast(F32)
             for g in range(2):
                 for u in range(2):
@@ -130,32 +137,33 @@ def tile_active_surface_link_s11_kernel(
                     )
             coef_bank[n] = bank
 
-        def copy(engine, dst, src):
-            if engine == "v":
-                nc.vector.tensor_copy(out=dst, in_=src)
-            else:
-                nc.scalar.copy(out=dst, in_=src)
-
         def c_coef(n, engine):
-            grp = work.tile([P, 2, 128, 4], BF16, name="coef_grp", tag="coef_grp", bufs=4, align_bytes=64)
-            coef_grp[n] = grp
+            pair = n // 2
+            if pair not in coef_grp:
+                coef_grp[pair] = work.tile([P, 2, 256, 4], BF16, name="coef_grp", tag="coef_grp", align_bytes=64)
+            words = coef_grp[pair][:].rearrange("p g r t -> p (g r t)").bitcast(F32)
+            r0 = 128 * (n % 2)
             copy(
                 engine,
-                grp[:].rearrange("p g r t -> p (g r t)").bitcast(F32).rearrange("p (g r u) -> p g r u", g=2, u=2),
+                words.rearrange("p (g r u) -> p g r u", g=2, u=2)[:, :, r0 : r0 + 128, :],
                 coef_bank[n][:].rearrange("p (g u r) -> p g r u", g=2, u=2),
             )
 
-        def q_coef(n):
-            nc.vector.quantize_mx(
-                out=coef_codes[n][:].rearrange("p g r -> p (g r)").bitcast(FP8X4),
-                scales=coef_scales[n][:].rearrange("p g r -> p (g r)"),
-                in_=coef_grp[n][:].rearrange("p g r t -> p (g r t)"),
-            )
+        def q_coef(n, count=1):
+            r0 = 128 * (n % 2)
+            c0 = 128 * (n % 4)
+            w = 128 * count
+            for g in range(2):
+                nc.vector.quantize_mx(
+                    out=coef_codes[n // 4][g][:, c0 : c0 + w].bitcast(FP8X4),
+                    scales=coef_scales[n // 4][g][:, c0 : c0 + w],
+                    in_=coef_grp[n // 2][:, g, r0 : r0 + w, :].rearrange("p r t -> p (r t)"),
+                )
 
         sig_bank = {}
 
         def t_sig(pair):
-            bank = psum.tile([P, 512], F32, name="bank", tag="bank")
+            b, bank = take_bank()
             for i in range(2):
                 words = sig_raw[:, 2 * pair + i, :].bitcast(F32)
                 for u in range(2):
@@ -176,25 +184,35 @@ def tile_active_surface_link_s11_kernel(
                 out=sig_codes[:].bitcast(FP8X4), scales=sig_scales[:], in_=sig_grp[:].rearrange("p r t -> p (r t)")
             )
 
-        def perm_scales(g):
+        def sort_scales(dst, cols):
             nc.vector.tensor_copy(
-                out=rs_perm[:, g, :].bitcast(I32).rearrange("p (t b w) -> p t b w", t=4, w=2),
-                in_=rs_raw[:, g, :].bitcast(I32).rearrange("p (b t w) -> p t b w", t=4, w=2),
+                out=dst[:].rearrange("p g e -> p (g e)").bitcast(I32).rearrange("p (g t b w) -> p g t b w", g=2, t=4, w=2),
+                in_=rs_raw[:, :, cols].bitcast(I32).rearrange("p g (b t w) -> p g t b w", t=4, w=2),
             )
 
-        def perm_resp(grp):
-            for g in range(2):
-                nc.vector.tensor_copy(
-                    out=resp_perm[grp][:, g, :].bitcast(I32).rearrange("p (t b w) -> p t b w", t=4, w=4),
-                    in_=resp_raw[grp][:, g, :].bitcast(I32).rearrange("p (b t w) -> p t b w", t=4, w=4),
-                )
+        def resp_scale(grp, g, t):
+            if grp == 0:
+                return rs_first[:, g, 128 * t : 128 * (t + 1)]
+            so = 384 * t + 128 * (grp - 1)
+            return rs_rest[:, g, so : so + 128]
 
-        def vectors():
-            bank = psum.tile([P, 8, P], BF16, name="bank", tag="bank")
+        def perm_resp(grp):
+            nc.vector.tensor_copy(
+                out=resp_perm[grp][:].bitcast(I32).rearrange("p g (t b w) -> p g t b w", t=4, w=4),
+                in_=resp_raw[grp][:].bitcast(I32).rearrange("p g (b t w) -> p g t b w", t=4, w=4),
+            )
+
+        vec_bank = {}
+
+        def t_vectors():
+            b, bank = take_bank((P, 8, P), BF16)
             for grp in range(GROUPS):
                 cols = slice(128 * grp, 128 * (grp + 1))
                 nc.tensor.transpose(bank[:, grp, :], vec_b[:, cols], ident_b[:])
-            nc.vector.tensor_copy(out=vec_t[:], in_=bank[:, 0:GROUPS, 0:8])
+            vec_bank[0] = bank
+
+        def c_vectors(engine):
+            copy(engine, vec_t[:], vec_bank[0][:, 0:GROUPS, 0:8])
 
         inc_wid, inc_grp = {}, {}
 
@@ -210,13 +228,16 @@ def tile_active_surface_link_s11_kernel(
                     op0=MULT,
                 )
 
-        def interleave(grp):
-            g4 = work.tile([P, 512, 4], BF16, name="inc_grp", tag="inc_grp", align_bytes=64)
-            inc_grp[grp] = g4
+        def interleave_planes(dst, planes, cols=slice(0, 512)):
             nc.vector.tensor_copy(
-                out=g4[:].rearrange("p (c i) j -> p c j i", i=4),
-                in_=inc_wid[grp][:].rearrange("p j (c i) -> p c j i", i=4),
+                out=dst[:, cols, :].rearrange("p (c i) j -> p c j i", i=4),
+                in_=planes[:, :, cols].rearrange("p j (c i) -> p c j i", i=4),
             )
+
+        def interleave(grp, cols=slice(0, 512)):
+            if grp not in inc_grp:
+                inc_grp[grp] = work.tile([P, 512, 4], BF16, name="inc_grp", tag="inc_grp", align_bytes=64)
+            interleave_planes(inc_grp[grp], inc_wid[grp], cols)
 
         def q_inc(grp):
             nc.vector.quantize_mx(
@@ -225,30 +246,53 @@ def tile_active_surface_link_s11_kernel(
                 in_=inc_grp[grp][:].rearrange("p c j -> p (c j)"),
             )
 
-        outg = {}
+        outg, outg_bank, planes = {}, {}, {}
 
-        def outgoing(n, grp, engine):
-            h = n // 4
+        def outg_tile(h, grp):
             if (h, grp) not in outg:
-                outg[(h, grp)] = work.tile(
-                    [P, HALF_R, 4], BF16, name="outg", tag="outg", bufs=6, align_bytes=64
+                outg[(h, grp)] = work.tile([P, HALF_R, 4], BF16, name="outg", tag="outg", bufs=OUTG_BUFS, align_bytes=64)
+            return outg[(h, grp)]
+
+        def resp_pass(dst, grp, t, h, recv):
+            for g in range(2):
+                nc.tensor.matmul_mx(
+                    out=dst,
+                    lhsT=resp_perm[grp][:, g, 256 * t : 256 * (t + 1)].bitcast(FP4X4),
+                    lhsT_scale=resp_scale(grp, g, t),
+                    rhs=coef_codes[h][g][:, recv].bitcast(FP8X4),
+                    rhs_scale=coef_scales[h][g][:, recv],
+                    start=(g == 0),
+                    stop=(g == 1),
                 )
-            bank = psum.tile([P, 512], F32, name="bank", tag="bank")
-            for t in range(4):
-                lo = 256 * t
-                so = 512 * t + 128 * grp
-                for g in range(2):
-                    nc.tensor.matmul_mx(
-                        out=bank[:, 128 * t : 128 * (t + 1)],
-                        lhsT=resp_perm[grp][:, g, lo : lo + 256].bitcast(FP4X4),
-                        lhsT_scale=rs_perm[:, g, so : so + 128],
-                        rhs=coef_codes[n][:, g, :].bitcast(FP8X4),
-                        rhs_scale=coef_scales[n][:, g, :],
-                        start=(g == 0),
-                        stop=(g == 1),
-                    )
+
+        def outgoing(n, grp):
+            b, bank = take_bank()
             r0 = 128 * (n % 4)
-            copy(engine, outg[(h, grp)][:, r0 : r0 + 128, :], bank[:].rearrange("p (t r) -> p r t", t=4))
+            for t in range(4):
+                resp_pass(bank[:, 128 * t : 128 * (t + 1)], grp, t, n // 4, slice(r0, r0 + 128))
+            outg_bank[(n, grp)] = bank
+
+        def c_outg(n, grp, engine):
+            r0 = 128 * (n % 4)
+            copy(
+                engine,
+                outg_tile(n // 4, grp)[:, r0 : r0 + 128, :],
+                outg_bank[(n, grp)][:].rearrange("p (t r) -> p r t", t=4),
+            )
+
+        def og(n, grp, engine="s"):
+            outgoing(n, grp)
+            c_outg(n, grp, engine)
+
+        def outgoing_wide(h, grp, t, engine):
+            b, bank = take_bank()
+            resp_pass(bank[:], grp, t, h, slice(0, HALF_R))
+            if (h, grp) not in planes:
+                planes[(h, grp)] = work.tile([P, 4, HALF_R], BF16, name="inc_wid", tag="inc_wid", align_bytes=64)
+            copy(engine, planes[(h, grp)][:, t, :], bank[:])
+
+        def interleave_outg(h, grp):
+            interleave_planes(outg_tile(h, grp), planes[(h, grp)])
 
         def q_outg(h, grp):
             nc.vector.quantize_mx(
@@ -263,7 +307,7 @@ def tile_active_surface_link_s11_kernel(
             th = work.tile([P, 4, T], F32, name="th", tag="th", bufs=3, align_bytes=64)
             refl_tanh[grp] = th
             for t in range(4):
-                bank = psum.tile([P, 512], F32, name="bank", tag="bank")
+                b, bank = take_bank()
                 nc.tensor.matmul_mx(
                     out=bank[:],
                     lhsT=inc_codes[grp][:, 128 * t : 128 * (t + 1)].bitcast(FP8X4),
@@ -292,10 +336,16 @@ def tile_active_surface_link_s11_kernel(
                 in_=refl_grp[grp][:].rearrange("p n t -> p (n t)"),
             )
 
-        def final_pass(h, m, grp, bank, recv=slice(0, HALF_R)):
+        fin = {}
+        out_rows = out.rearrange("(p n) r -> n p r", n=4)
+
+        def final_pass(h, m, grp, recv=slice(0, HALF_R)):
+            key = (h, m, recv.start)
+            if key not in fin:
+                fin[key] = take_bank(hold=True)
             cols = slice(128 * m, 128 * (m + 1))
             nc.tensor.matmul_mx(
-                out=bank[:, recv],
+                out=fin[key][1][:, recv],
                 lhsT=refl_codes[grp][:, cols].bitcast(FP8X4),
                 lhsT_scale=refl_scales[grp][:, cols],
                 rhs=outg_codes[h][grp][:, recv].bitcast(FP8X4),
@@ -304,122 +354,159 @@ def tile_active_surface_link_s11_kernel(
                 stop=(grp == GROUPS - 1),
             )
 
-        def store(h, m, bank, engine, recv=slice(0, HALF_R)):
+        def final(h, grp):
+            for m in range(4):
+                final_pass(h, m, grp)
+
+        def store(h, m, engine, recv=slice(0, HALF_R)):
+            b, bank = fin[(h, m, recv.start)]
             res = work.tile([P, HALF_R], F32, name="res", tag="res", bufs=8, align_bytes=64)
             copy(engine, res[:, recv], bank[:, recv])
             nc.sync.dma_start(
-                out=out[128 * m : 128 * (m + 1), HALF_R * h + recv.start : HALF_R * h + recv.stop], in_=res[:, recv]
+                out=out_rows[m][:, HALF_R * h + recv.start : HALF_R * h + recv.stop], in_=res[:, recv]
             )
+            ring.append(b)
+
+        load_inc_scale()
+        load_inc(0)
+        load_coef(0)
+        load_scales()
+        load_resp(0)
+        load_coef(1)
+        load_vectors()
+        load_resp(1)
+        load_sig()
+        load_resp(2)
+        load_inc(1)
+        load_coef(2)
+        load_coef(3)
+        load_resp(3)
+        load_inc(2)
+        load_coef(4)
+        load_coef(5)
+        load_inc(3)
+        load_coef(6)
+        load_coef(7)
 
         warm_up(4)
         t_coef(0)
-        t_coef(1)
-        warm_up(3)
-        c_coef(0, "v")
-        c_coef(1, "s")
-        q_coef(0)
-        perm_scales(0)
-        perm_scales(1)
-        q_coef(1)
-        perm_resp(0)
-        outgoing(0, 0, "s")
-        outgoing(1, 0, "s")
-        perm_resp(1)
+        warm_up(4)
+        c_coef(0, "s")
         widen(0)
-        outgoing(0, 1, "s")
-        outgoing(1, 1, "s")
-        perm_resp(2)
-        interleave(0)
-        outgoing(0, 2, "s")
-        outgoing(1, 2, "s")
-        perm_resp(3)
-        t_coef(2)
-        t_coef(3)
-        widen(1)
+        interleave(0, slice(0, 256))
+        sort_scales(rs_first, slice(0, 512))
+        q_coef(0)
+        t_coef(1)
+        t_vectors()
+        c_coef(1, "s")
+        c_vectors("s")
+        perm_resp(0)
+        sort_scales(rs_rest, slice(512, E))
+        perm_resp(1)
+        interleave(0, slice(256, 512))
+        q_coef(1)
+        og(0, 0)
+        og(0, 1)
         q_inc(0)
-        c_coef(2, "s")
-        c_coef(3, "s")
-        outgoing(0, 3, "s")
-        q_coef(2)
-        interleave(1)
-        outgoing(1, 3, "s")
-        q_coef(3)
+        og(1, 0)
         t_sig(0)
         t_sig(1)
-        vectors()
         c_sig(0, "s")
         c_sig(1, "s")
-        widen(2)
-        q_inc(1)
+        perm_resp(2)
+        widen(1)
+        og(1, 1)
+        og(0, 2)
+        interleave(1)
         q_sig()
-        for grp in range(4):
-            outgoing(2, grp, "s")
-        interleave(2)
+        t_coef(2)
+        t_coef(3)
+        c_coef(2, "s")
+        c_coef(3, "s")
+        perm_resp(3)
+        q_inc(1)
         field(0)
+        og(1, 2)
+        og(0, 3)
+        widen(2)
+        q_coef(2, 2)
+        interleave(2)
+        og(1, 3)
+        og(2, 0)
+        og(3, 0)
+        apply_gain(0)
+        q_inc(2)
+        field(1)
+        og(2, 1)
+        og(3, 1)
+        q_refl(0)
+        q_outg(0, 0)
+        widen(3)
         t_coef(4)
         t_coef(5)
-        widen(3)
-        q_inc(2)
         c_coef(4, "s")
         c_coef(5, "s")
-        outgoing(3, 0, "s")
+        og(2, 2)
+        final(0, 0)
+        apply_gain(1)
+        q_outg(0, 1)
+        og(3, 2)
+        og(2, 3)
+        q_coef(4, 2)
+        q_refl(1)
         t_coef(6)
         t_coef(7)
         c_coef(6, "s")
-        c_coef(7, "s")
-        q_coef(4)
-        q_coef(5)
-        apply_gain(0)
-        outgoing(3, 1, "s")
-        q_coef(6)
-        q_coef(7)
-        interleave(3)
-        q_refl(0)
-        q_inc(3)
-        for grp in range(2, 4):
-            outgoing(3, grp, "s")
-        field(1)
-        q_outg(0, 0)
-        q_outg(0, 1)
-        for n in range(4, 8):
-            outgoing(n, 0, "s")
-        apply_gain(1)
-        q_outg(0, 2)
-        q_outg(0, 3)
-        q_refl(1)
+        c_coef(7, "v")
+        og(3, 3)
         field(2)
-        for n in range(4, 8):
-            outgoing(n, 1, "s")
-        q_outg(1, 0)
+        final(0, 1)
+        interleave(3)
+        q_coef(6, 2)
+        q_outg(0, 2)
+        q_inc(3)
+        og(4, 0)
+        og(5, 0)
         apply_gain(2)
-        field(3)
+        og(6, 0)
+        q_outg(0, 3)
         q_refl(2)
-        fin = [psum.tile([P, 512], F32, name="bank", tag="bank") for m in range(4)]
-        for grp in (0, 1):
-            for m in range(4):
-                final_pass(0, m, grp, fin[m])
-        q_outg(1, 1)
-        for n in range(4, 8):
-            outgoing(n, 2, "s")
+        og(7, 0)
+        field(3)
+        final(0, 2)
+        for t in range(4):
+            outgoing_wide(1, 1, t, "s")
         apply_gain(3)
-        q_outg(1, 2)
+        q_outg(1, 0)
         q_refl(3)
-        for n in range(4, 8):
-            outgoing(n, 3, "v" if n % 2 else "s")
+        interleave_outg(1, 1)
+        for t in range(4):
+            outgoing_wide(1, 2, t, "s")
+        q_outg(1, 1)
+        final(0, 3)
+        interleave_outg(1, 2)
+        og(4, 3)
+        store(0, 0, "v")
+        og(5, 3)
+        q_outg(1, 2)
+        og(6, 3)
+        og(7, 3, "v")
+        store(0, 1, "s")
+        for m in range(2):
+            for grp in range(3):
+                final_pass(1, m, grp)
         q_outg(1, 3)
-        for m in range(4):
-            for grp in (2, 3):
-                final_pass(0, m, grp, fin[m])
-        for m in range(4):
-            store(0, m, fin[m], "v" if m % 2 else "s")
-        for m in range(3):
-            bank = psum.tile([P, 512], F32, name="bank", tag="bank")
-            for grp in range(GROUPS):
-                final_pass(1, m, grp, bank)
-            store(1, m, bank, "v" if m % 2 else "s")
+        store(0, 2, "s")
+        store(0, 3, "v")
+
+        for m in range(2):
+            final_pass(1, m, 3)
+            store(1, m, "sv"[m % 2])
+        for grp in range(GROUPS):
+            final_pass(1, 2, grp)
+        store(1, 2, "s")
         for part in range(2):
-            bank = psum.tile([P, 512], F32, name="bank", tag="bank")
             cols = slice(256 * part, 256 * (part + 1))
             for grp in range(GROUPS):
-                final_pass(1, 3, grp, bank, cols)
-            store(1, 3, bank, "s" if part else "v", cols)
+                final_pass(1, 3, grp, cols)
+            store(1, 3, "vs"[part], cols)

@@ -15,13 +15,16 @@ FP8 = mybir.dt.float8_e4m3fn
 FP8X4 = mybir.dt.float8_e4m3fn_x4
 FP4X4 = mybir.dt.float4_e2m1fn_x4
 MULT = mybir.AluOpType.mult
+COPY = mybir.ActivationFunctionType.Copy
 TANH = mybir.ActivationFunctionType.Tanh
 
 P = 128
 GROUPS = E // 512
 N_COEF = R // 128
 HALF_R = 512
-OUTG_BUFS = 6
+OUTG_BUFS = 3
+WID_BUFS = 2
+RESP_LOADS = ((0, 1), (1, 1), (2, 2))
 
 
 def tile_active_surface_link_s11_kernel(
@@ -38,10 +41,10 @@ def tile_active_surface_link_s11_kernel(
             return keep.tile(shape, dtype, name=name, tag=name, align_bytes=64)
 
         coef_raw = [kept("coef_raw%d" % n, [P, PATHS], BF16) for n in range(N_COEF)]
-        coef_codes = [[kept("coef_codes%d_%d" % (h, g), [P, HALF_R], U32) for g in range(2)] for h in range(2)]
-        coef_scales = [[kept("coef_scales%d_%d" % (h, g), [P, HALF_R], U8) for g in range(2)] for h in range(2)]
-        resp_raw = [kept("resp_raw%d" % g, [P, 2, 1024], U8) for g in range(GROUPS)]
-        resp_perm = [kept("resp_perm%d" % g, [P, 2, 1024], U8) for g in range(GROUPS)]
+        coef_codes = [kept("coef_codes%d_x" % n, [P, 512], U32) for n in range(N_COEF // 2)]
+        coef_scales = [kept("coef_scales%d" % n, [P, 512], U8) for n in range(N_COEF // 2)]
+        resp_raw = [kept("resp_raw%d" % k, [P, 2, 1024 * w], U8) for k, (g0, w) in enumerate(RESP_LOADS)]
+        resp_perm = [kept("resp_perm%d" % k, [P, 2, 1024 * w], U8) for k, (g0, w) in enumerate(RESP_LOADS)]
         rs_raw = kept("rs_raw", [P, 2, E], U8)
         rs_first = kept("rs_first", [P, 2, 512], U8)
         rs_rest = kept("rs_rest", [P, 2, E - 512], U8)
@@ -55,8 +58,8 @@ def tile_active_surface_link_s11_kernel(
         sig_scales = kept("sig_scales", [P, T], U8)
         refl_codes = [kept("refl_codes%d" % g, [P, T], U32) for g in range(GROUPS)]
         refl_scales = [kept("refl_scales%d" % g, [P, T], U8) for g in range(GROUPS)]
-        outg_codes = [[kept("outg_codes%d_%d" % (h, g), [P, HALF_R], U32) for g in range(GROUPS)] for h in range(2)]
-        outg_scales = [[kept("outg_scales%d_%d" % (h, g), [P, HALF_R], U8) for g in range(GROUPS)] for h in range(2)]
+        outg_codes = [[kept("outg_codes%d_%d" % (h, k), [P, 2 * HALF_R], U32) for k in range(2)] for h in range(2)]
+        outg_scales = [[kept("outg_scales%d_%d" % (h, k), [P, 2 * HALF_R], U8) for k in range(2)] for h in range(2)]
         ident = kept("ident", [P, P], F32)
         ident_b = kept("ident_b", [P, P], BF16)
         vec_b = kept("vec_b", [P, 512], BF16)
@@ -90,10 +93,11 @@ def tile_active_surface_link_s11_kernel(
                     in_=resp_scales[:, 4 * q : 4 * q + 4, :].rearrange("g q e -> q g e").bitcast(I32),
                 )
 
-        def load_resp(grp):
+        def load_resp(k):
+            g0, w = RESP_LOADS[k]
             nc.sync.dma_start(
-                out=resp_raw[grp][:].bitcast(I32),
-                in_=resp_words[:, :, 1024 * grp : 1024 * (grp + 1)].rearrange("g p b -> p g b").bitcast(I32),
+                out=resp_raw[k][:].bitcast(I32),
+                in_=resp_words[:, :, 1024 * g0 : 1024 * (g0 + w)].rearrange("g p b -> p g b").bitcast(I32),
             )
 
         def load_inc(grp):
@@ -140,25 +144,21 @@ def tile_active_surface_link_s11_kernel(
         def c_coef(n, engine):
             pair = n // 2
             if pair not in coef_grp:
-                coef_grp[pair] = work.tile([P, 2, 256, 4], BF16, name="coef_grp", tag="coef_grp", align_bytes=64)
-            words = coef_grp[pair][:].rearrange("p g r t -> p (g r t)").bitcast(F32)
-            r0 = 128 * (n % 2)
+                coef_grp[pair] = work.tile([P, 2048], BF16, name="coef_grp", tag="coef_grp", align_bytes=64)
+            lo = 1024 * (n % 2)
             copy(
                 engine,
-                words.rearrange("p (g r u) -> p g r u", g=2, u=2)[:, :, r0 : r0 + 128, :],
+                coef_grp[pair][:, lo : lo + 1024].bitcast(F32).rearrange("p (g r u) -> p g r u", g=2, u=2),
                 coef_bank[n][:].rearrange("p (g u r) -> p g r u", g=2, u=2),
             )
 
         def q_coef(n, count=1):
-            r0 = 128 * (n % 2)
-            c0 = 128 * (n % 4)
-            w = 128 * count
-            for g in range(2):
-                nc.vector.quantize_mx(
-                    out=coef_codes[n // 4][g][:, c0 : c0 + w].bitcast(FP8X4),
-                    scales=coef_scales[n // 4][g][:, c0 : c0 + w],
-                    in_=coef_grp[n // 2][:, g, r0 : r0 + w, :].rearrange("p r t -> p (r t)"),
-                )
+            cols = slice(256 * (n % 2), 256 * (n % 2 + count))
+            nc.vector.quantize_mx(
+                out=coef_codes[n // 2][:, cols].bitcast(FP8X4),
+                scales=coef_scales[n // 2][:, cols],
+                in_=coef_grp[n // 2][:, 4 * cols.start : 4 * cols.stop],
+            )
 
         sig_bank = {}
 
@@ -196,11 +196,17 @@ def tile_active_surface_link_s11_kernel(
             so = 384 * t + 128 * (grp - 1)
             return rs_rest[:, g, so : so + 128]
 
-        def perm_resp(grp):
+        def perm_resp(k):
             nc.vector.tensor_copy(
-                out=resp_perm[grp][:].bitcast(I32).rearrange("p g (t b w) -> p g t b w", t=4, w=4),
-                in_=resp_raw[grp][:].bitcast(I32).rearrange("p g (b t w) -> p g t b w", t=4, w=4),
+                out=resp_perm[k][:].bitcast(I32).rearrange("p g (t b w) -> p g t b w", t=4, w=4),
+                in_=resp_raw[k][:].bitcast(I32).rearrange("p g (b t w) -> p g t b w", t=4, w=4),
             )
+
+        def resp_slice(grp, g, t):
+            k = max(i for i, (g0, w) in enumerate(RESP_LOADS) if g0 <= grp)
+            g0, w = RESP_LOADS[k]
+            lo = 256 * (w * t + grp - g0)
+            return resp_perm[k][:, g, lo : lo + 256].bitcast(FP4X4)
 
         vec_bank = {}
 
@@ -214,30 +220,48 @@ def tile_active_surface_link_s11_kernel(
         def c_vectors(engine):
             copy(engine, vec_t[:], vec_bank[0][:, 0:GROUPS, 0:8])
 
-        inc_wid, inc_grp = {}, {}
+        inc_wid, inc_grp, plain = {}, {}, set()
 
-        def widen(grp):
-            wid = work.tile([P, 4, 512], BF16, name="inc_wid", tag="inc_wid", align_bytes=64)
+        def widen(grp, engines="vvvv"):
+            wid = work.tile([P, 4, 512], BF16, name="inc_wid", tag="inc_wid", bufs=WID_BUFS, align_bytes=64)
             inc_wid[grp] = wid
+            if "s" in engines:
+                plain.add(grp)
             for j in range(4):
+                if engines[j] != "-":
+                    widen_row(grp, j, engines[j])
+
+        def widen_row(grp, j, engine):
+            src = inc_b[grp][:, j, :].bitcast(FP8)
+            dst = inc_wid[grp][:, j, :]
+            if engine == "s":
+                nc.scalar.activation(dst, src, COPY, scale=inc_sc[:, j : j + 1])
+            elif grp in plain:
+                nc.vector.tensor_scalar(out=dst, in0=src, scalar1=inc_sc[:, j : j + 1], scalar2=None, op0=MULT)
+            else:
                 nc.vector.tensor_scalar(
-                    out=wid[:, j, :].rearrange("p (t q i) -> p q t i", t=4, i=8),
-                    in0=inc_b[grp][:, j, :].bitcast(FP8).rearrange("p (q t i) -> p q t i", t=4, i=8),
+                    out=dst.rearrange("p (t q i) -> p q t i", t=4, i=8),
+                    in0=src.rearrange("p (q t i) -> p q t i", t=4, i=8),
                     scalar1=inc_sc[:, j : j + 1],
                     scalar2=None,
                     op0=MULT,
                 )
 
-        def interleave_planes(dst, planes, cols=slice(0, 512)):
-            nc.vector.tensor_copy(
-                out=dst[:, cols, :].rearrange("p (c i) j -> p c j i", i=4),
-                in_=planes[:, :, cols].rearrange("p j (c i) -> p c j i", i=4),
-            )
-
-        def interleave(grp, cols=slice(0, 512)):
+        def interleave(grp, half=None):
             if grp not in inc_grp:
                 inc_grp[grp] = work.tile([P, 512, 4], BF16, name="inc_grp", tag="inc_grp", align_bytes=64)
-            interleave_planes(inc_grp[grp], inc_wid[grp], cols)
+            if grp in plain:
+                slots = slice(0, 4) if half is None else slice(2 * half, 2 * half + 2)
+                nc.vector.tensor_copy(
+                    out=inc_grp[grp][:].rearrange("p (t q i) j -> p t q i j", t=4, i=8)[:, slots],
+                    in_=inc_wid[grp][:].rearrange("p j (q t i) -> p t q i j", t=4, i=8)[:, slots],
+                )
+            else:
+                cols = slice(0, 512) if half is None else slice(256 * half, 256 * (half + 1))
+                nc.vector.tensor_copy(
+                    out=inc_grp[grp][:, cols, :].rearrange("p (c i) j -> p c j i", i=4),
+                    in_=inc_wid[grp][:, :, cols].rearrange("p j (c i) -> p c j i", i=4),
+                )
 
         def q_inc(grp):
             nc.vector.quantize_mx(
@@ -246,59 +270,41 @@ def tile_active_surface_link_s11_kernel(
                 in_=inc_grp[grp][:].rearrange("p c j -> p (c j)"),
             )
 
-        outg, outg_bank, planes = {}, {}, {}
-
-        def outg_tile(h, grp):
-            if (h, grp) not in outg:
-                outg[(h, grp)] = work.tile([P, HALF_R, 4], BF16, name="outg", tag="outg", bufs=OUTG_BUFS, align_bytes=64)
-            return outg[(h, grp)]
-
-        def resp_pass(dst, grp, t, h, recv):
-            for g in range(2):
-                nc.tensor.matmul_mx(
-                    out=dst,
-                    lhsT=resp_perm[grp][:, g, 256 * t : 256 * (t + 1)].bitcast(FP4X4),
-                    lhsT_scale=resp_scale(grp, g, t),
-                    rhs=coef_codes[h][g][:, recv].bitcast(FP8X4),
-                    rhs_scale=coef_scales[h][g][:, recv],
-                    start=(g == 0),
-                    stop=(g == 1),
-                )
+        outg, outg_bank = {}, {}
 
         def outgoing(n, grp):
             b, bank = take_bank()
-            r0 = 128 * (n % 4)
             for t in range(4):
-                resp_pass(bank[:, 128 * t : 128 * (t + 1)], grp, t, n // 4, slice(r0, r0 + 128))
+                for g in range(2):
+                    cols = slice(256 * (n % 2) + 128 * g, 256 * (n % 2) + 128 * (g + 1))
+                    nc.tensor.matmul_mx(
+                        out=bank[:, 128 * t : 128 * (t + 1)],
+                        lhsT=resp_slice(grp, g, t),
+                        lhsT_scale=resp_scale(grp, g, t),
+                        rhs=coef_codes[n // 2][:, cols].bitcast(FP8X4),
+                        rhs_scale=coef_scales[n // 2][:, cols],
+                        start=(g == 0),
+                        stop=(g == 1),
+                    )
             outg_bank[(n, grp)] = bank
 
         def c_outg(n, grp, engine):
-            r0 = 128 * (n % 4)
-            copy(
-                engine,
-                outg_tile(n // 4, grp)[:, r0 : r0 + 128, :],
-                outg_bank[(n, grp)][:].rearrange("p (t r) -> p r t", t=4),
-            )
+            key = (n // 4, grp // 2)
+            if key not in outg:
+                outg[key] = work.tile([P, 2 * HALF_R, 4], BF16, name="outg", tag="outg", bufs=OUTG_BUFS, align_bytes=64)
+            r0 = HALF_R * (grp % 2) + 128 * (n % 4)
+            copy(engine, outg[key][:, r0 : r0 + 128, :], outg_bank[(n, grp)][:].rearrange("p (t r) -> p r t", t=4))
 
         def og(n, grp, engine="s"):
             outgoing(n, grp)
             c_outg(n, grp, engine)
 
-        def outgoing_wide(h, grp, t, engine):
-            b, bank = take_bank()
-            resp_pass(bank[:], grp, t, h, slice(0, HALF_R))
-            if (h, grp) not in planes:
-                planes[(h, grp)] = work.tile([P, 4, HALF_R], BF16, name="inc_wid", tag="inc_wid", align_bytes=64)
-            copy(engine, planes[(h, grp)][:, t, :], bank[:])
-
-        def interleave_outg(h, grp):
-            interleave_planes(outg_tile(h, grp), planes[(h, grp)])
-
-        def q_outg(h, grp):
+        def q_outg(h, grp, count=1):
+            cols = slice(HALF_R * (grp % 2), HALF_R * (grp % 2 + count))
             nc.vector.quantize_mx(
-                out=outg_codes[h][grp][:].bitcast(FP8X4),
-                scales=outg_scales[h][grp][:],
-                in_=outg[(h, grp)][:].rearrange("p r t -> p (r t)"),
+                out=outg_codes[h][grp // 2][:, cols].bitcast(FP8X4),
+                scales=outg_scales[h][grp // 2][:, cols],
+                in_=outg[(h, grp // 2)][:, cols, :].rearrange("p r t -> p (r t)"),
             )
 
         refl_tanh, refl_grp = {}, {}
@@ -344,12 +350,13 @@ def tile_active_surface_link_s11_kernel(
             if key not in fin:
                 fin[key] = take_bank(hold=True)
             cols = slice(128 * m, 128 * (m + 1))
+            moving = slice(HALF_R * (grp % 2) + recv.start, HALF_R * (grp % 2) + recv.stop)
             nc.tensor.matmul_mx(
                 out=fin[key][1][:, recv],
                 lhsT=refl_codes[grp][:, cols].bitcast(FP8X4),
                 lhsT_scale=refl_scales[grp][:, cols],
-                rhs=outg_codes[h][grp][:, recv].bitcast(FP8X4),
-                rhs_scale=outg_scales[h][grp][:, recv],
+                rhs=outg_codes[h][grp // 2][:, moving].bitcast(FP8X4),
+                rhs_scale=outg_scales[h][grp // 2][:, moving],
                 start=(grp == 0),
                 stop=(grp == GROUPS - 1),
             )
@@ -373,14 +380,13 @@ def tile_active_surface_link_s11_kernel(
         load_scales()
         load_resp(0)
         load_coef(1)
-        load_vectors()
         load_resp(1)
         load_sig()
+        load_vectors()
         load_resp(2)
         load_inc(1)
         load_coef(2)
         load_coef(3)
-        load_resp(3)
         load_inc(2)
         load_coef(4)
         load_coef(5)
@@ -391,113 +397,111 @@ def tile_active_surface_link_s11_kernel(
         warm_up(4)
         t_coef(0)
         warm_up(4)
+        widen(0, "vvss")
         c_coef(0, "s")
-        widen(0)
-        interleave(0, slice(0, 256))
+        interleave(0, 0)
         sort_scales(rs_first, slice(0, 512))
         q_coef(0)
         t_coef(1)
-        t_vectors()
         c_coef(1, "s")
-        c_vectors("s")
         perm_resp(0)
-        sort_scales(rs_rest, slice(512, E))
         perm_resp(1)
-        interleave(0, slice(256, 512))
+        sort_scales(rs_rest, slice(512, E))
         q_coef(1)
+        interleave(0, 1)
         og(0, 0)
         og(0, 1)
-        q_inc(0)
         og(1, 0)
+        og(1, 1)
         t_sig(0)
         t_sig(1)
+        t_vectors()
         c_sig(0, "s")
         c_sig(1, "s")
+        c_vectors("s")
         perm_resp(2)
+        q_inc(0)
         widen(1)
-        og(1, 1)
         og(0, 2)
-        interleave(1)
-        q_sig()
+        og(1, 2)
         t_coef(2)
         t_coef(3)
         c_coef(2, "s")
         c_coef(3, "s")
-        perm_resp(3)
-        q_inc(1)
+        q_sig()
+        interleave(1)
         field(0)
-        og(1, 2)
         og(0, 3)
+        og(1, 3)
         widen(2)
         q_coef(2, 2)
+        q_inc(1)
         interleave(2)
-        og(1, 3)
         og(2, 0)
         og(3, 0)
-        apply_gain(0)
-        q_inc(2)
-        field(1)
         og(2, 1)
         og(3, 1)
-        q_refl(0)
-        q_outg(0, 0)
-        widen(3)
+        apply_gain(0)
+        field(1)
         t_coef(4)
         t_coef(5)
         c_coef(4, "s")
         c_coef(5, "s")
+        q_inc(2)
+        q_refl(0)
+        q_outg(0, 0, 2)
         og(2, 2)
-        final(0, 0)
-        apply_gain(1)
-        q_outg(0, 1)
         og(3, 2)
-        og(2, 3)
+        widen(3)
         q_coef(4, 2)
-        q_refl(1)
         t_coef(6)
         t_coef(7)
         c_coef(6, "s")
-        c_coef(7, "v")
+        c_coef(7, "s")
+        final(0, 0)
+        apply_gain(1)
+        og(2, 3)
         og(3, 3)
         field(2)
-        final(0, 1)
         interleave(3)
+        q_refl(1)
         q_coef(6, 2)
-        q_outg(0, 2)
         q_inc(3)
         og(4, 0)
         og(5, 0)
+        og(4, 1)
+        final(0, 1)
+        q_outg(0, 2, 2)
+        og(5, 1)
         apply_gain(2)
         og(6, 0)
-        q_outg(0, 3)
-        q_refl(2)
-        og(7, 0)
         field(3)
+        og(7, 0)
+        q_refl(2)
+        og(6, 1)
+        og(7, 1)
         final(0, 2)
-        for t in range(4):
-            outgoing_wide(1, 1, t, "s")
         apply_gain(3)
-        q_outg(1, 0)
+        og(4, 2)
+        og(5, 2)
+        og(6, 2)
+        q_outg(1, 0, 2)
         q_refl(3)
-        interleave_outg(1, 1)
-        for t in range(4):
-            outgoing_wide(1, 2, t, "s")
-        q_outg(1, 1)
-        final(0, 3)
-        interleave_outg(1, 2)
+        og(7, 2)
         og(4, 3)
-        store(0, 0, "v")
-        og(5, 3)
+        og(5, 3, "v")
         q_outg(1, 2)
         og(6, 3)
         og(7, 3, "v")
-        store(0, 1, "s")
+        final(0, 3)
+        store(0, 0, "s")
         for m in range(2):
             for grp in range(3):
                 final_pass(1, m, grp)
         q_outg(1, 3)
-        store(0, 2, "s")
-        store(0, 3, "v")
+        store(0, 1, "s")
+        store(0, 2, "v")
+        store(0, 3, "s")
 
         for m in range(2):
             final_pass(1, m, 3)

@@ -293,7 +293,11 @@ def tile_active_surface_link_s11_kernel(
             if key not in outg:
                 outg[key] = work.tile([P, 2 * HALF_R, 4], BF16, name="outg", tag="outg", bufs=OUTG_BUFS, align_bytes=64)
             r0 = HALF_R * (grp % 2) + 128 * (n % 4)
-            copy(engine, outg[key][:, r0 : r0 + 128, :], outg_bank[(n, grp)][:].rearrange("p (t r) -> p r t", t=4))
+            copy(
+                engine,
+                outg[key][:, r0 : r0 + 128, :].rearrange("p (c i) t -> p c t i", i=4),
+                outg_bank[(n, grp)][:].rearrange("p (t c i) -> p c t i", t=4, i=4),
+            )
 
         def og(n, grp, engine="s"):
             outgoing(n, grp)
@@ -309,21 +313,24 @@ def tile_active_surface_link_s11_kernel(
 
         refl_tanh, refl_grp = {}, {}
 
+        def field_slot(grp, t):
+            if grp not in refl_tanh:
+                refl_tanh[grp] = work.tile([P, 4, T], F32, name="th", tag="th", bufs=3, align_bytes=64)
+            b, bank = take_bank()
+            nc.tensor.matmul_mx(
+                out=bank[:],
+                lhsT=inc_codes[grp][:, 128 * t : 128 * (t + 1)].bitcast(FP8X4),
+                lhsT_scale=inc_scales[grp][:, 128 * t : 128 * (t + 1)],
+                rhs=sig_codes[:].bitcast(FP8X4),
+                rhs_scale=sig_scales[:],
+                start=True,
+                stop=True,
+            )
+            nc.scalar.activation(refl_tanh[grp][:, t, :], bank[:], TANH, bias=vec_t[:, grp, t : t + 1])
+
         def field(grp):
-            th = work.tile([P, 4, T], F32, name="th", tag="th", bufs=3, align_bytes=64)
-            refl_tanh[grp] = th
             for t in range(4):
-                b, bank = take_bank()
-                nc.tensor.matmul_mx(
-                    out=bank[:],
-                    lhsT=inc_codes[grp][:, 128 * t : 128 * (t + 1)].bitcast(FP8X4),
-                    lhsT_scale=inc_scales[grp][:, 128 * t : 128 * (t + 1)],
-                    rhs=sig_codes[:].bitcast(FP8X4),
-                    rhs_scale=sig_scales[:],
-                    start=True,
-                    stop=True,
-                )
-                nc.scalar.activation(th[:, t, :], bank[:], TANH, bias=vec_t[:, grp, t : t + 1])
+                field_slot(grp, t)
 
         def apply_gain(grp):
             rf = work.tile([P, T, 4], BF16, name="refl", tag="refl", bufs=2, align_bytes=64)
@@ -405,8 +412,8 @@ def tile_active_surface_link_s11_kernel(
         t_coef(1)
         c_coef(1, "s")
         perm_resp(0)
-        perm_resp(1)
         sort_scales(rs_rest, slice(512, E))
+        perm_resp(1)
         q_coef(1)
         interleave(0, 1)
         og(0, 0)
@@ -422,6 +429,7 @@ def tile_active_surface_link_s11_kernel(
         perm_resp(2)
         q_inc(0)
         widen(1)
+
         og(0, 2)
         og(1, 2)
         t_coef(2)
@@ -433,9 +441,9 @@ def tile_active_surface_link_s11_kernel(
         field(0)
         og(0, 3)
         og(1, 3)
-        widen(2)
-        q_coef(2, 2)
         q_inc(1)
+        q_coef(2, 2)
+        widen(2)
         interleave(2)
         og(2, 0)
         og(3, 0)
@@ -450,44 +458,40 @@ def tile_active_surface_link_s11_kernel(
         q_inc(2)
         q_refl(0)
         q_outg(0, 0, 2)
+        q_coef(4, 2)
         og(2, 2)
         og(3, 2)
-        widen(3)
-        q_coef(4, 2)
         t_coef(6)
         t_coef(7)
         c_coef(6, "s")
         c_coef(7, "s")
-        final(0, 0)
+        widen(3)
+        q_coef(6, 2)
         apply_gain(1)
         og(2, 3)
         og(3, 3)
-        field(2)
         interleave(3)
+        for t in range(4):
+            field_slot(2, t)
+            final_pass(0, t, 0)
+            og(4 + t, 0)
         q_refl(1)
-        q_coef(6, 2)
         q_inc(3)
-        og(4, 0)
-        og(5, 0)
-        og(4, 1)
-        final(0, 1)
-        q_outg(0, 2, 2)
-        og(5, 1)
         apply_gain(2)
-        og(6, 0)
-        field(3)
-        og(7, 0)
+        og(4, 1)
+        og(5, 1)
+        for t in range(4):
+            field_slot(3, t)
+            final_pass(0, t, 1)
+            og(*((6, 1), (7, 1), (4, 2), (5, 2))[t])
+        q_outg(0, 2, 2)
         q_refl(2)
-        og(6, 1)
-        og(7, 1)
-        final(0, 2)
         apply_gain(3)
-        og(4, 2)
-        og(5, 2)
-        og(6, 2)
         q_outg(1, 0, 2)
-        q_refl(3)
+        og(6, 2)
         og(7, 2)
+        final(0, 2)
+        q_refl(3)
         og(4, 3)
         og(5, 3, "v")
         q_outg(1, 2)

@@ -25,6 +25,7 @@ HALF_R = 512
 OUTG_BUFS = 3
 WID_BUFS = 2
 RESP_LOADS = ((0, 1), (1, 1), (2, 2))
+INC_LOADS = ((0, 1), (1, 1), (2, 2))
 
 
 def tile_active_surface_link_s11_kernel(
@@ -45,10 +46,10 @@ def tile_active_surface_link_s11_kernel(
         coef_scales = [kept("coef_scales%d" % n, [P, 512], U8) for n in range(N_COEF // 2)]
         resp_raw = [kept("resp_raw%d" % k, [P, 2, 1024 * w], U8) for k, (g0, w) in enumerate(RESP_LOADS)]
         resp_perm = [kept("resp_perm%d" % k, [P, 2, 1024 * w], U8) for k, (g0, w) in enumerate(RESP_LOADS)]
-        rs_raw = kept("rs_raw", [P, 2, E], U8)
+        rs_raw = [kept("rs_raw0", [P, 2, 512], U8), kept("rs_raw1", [P, 2, E - 512], U8)]
         rs_first = kept("rs_first", [P, 2, 512], U8)
         rs_rest = kept("rs_rest", [P, 2, E - 512], U8)
-        inc_b = [kept("inc_b%d" % g, [P, 4, 512], U8) for g in range(GROUPS)]
+        inc_b = [kept("inc_b%d" % k, [P, 4, 512 * w], U8) for k, (g0, w) in enumerate(INC_LOADS)]
         inc_sc = kept("inc_sc", [P, 4], F32)
         inc_codes = [kept("inc_codes%d" % g, [P, 512], U32) for g in range(GROUPS)]
         inc_scales = [kept("inc_scales%d" % g, [P, 512], U8) for g in range(GROUPS)]
@@ -75,22 +76,25 @@ def tile_active_surface_link_s11_kernel(
                 ring.append(b)
             return b, psum.tile(list(shape), dtype, name="bank%d" % b, tag="bank%d" % b)
 
+        nc.vector.memset(ident[:], 0.0)
+        nc.vector.memset(dummy[:], 0.0)
+        make_identity(nc, ident[:], nomemset=True)
         nc.vector.memset(zeros[:], 0.0)
-        nc.vector.memset(rs_raw[:].rearrange("p g e -> p (g e)").bitcast(I32), 0)
-        nc.gpsimd.memset(dummy[:], 0.0)
-        make_identity(nc, ident[:])
-        nc.gpsimd.memset(vec_b[:], 0.0)
-        make_identity(nc, ident_b[:])
+        nc.vector.memset(rs_raw[0][:].rearrange("p g e -> p (g e)").bitcast(I32), 0)
+        nc.vector.memset(rs_raw[1][:].rearrange("p g e -> p (g e)").bitcast(I32), 0)
+        nc.vector.memset(vec_b[:], 0.0)
         nc.scalar.activation(dummy[:], dummy[:], TANH)
+        nc.scalar.copy(out=ident_b[:], in_=ident[:])
 
         def load_coef(n):
             nc.sync.dma_start(out=coef_raw[n][:], in_=coef[128 * n : 128 * (n + 1), :])
 
-        def load_scales():
+        def load_scales(k):
+            cols = (slice(0, 512), slice(512, E))[k]
             for q in range(4):
                 nc.sync.dma_start(
-                    out=rs_raw[32 * q : 32 * q + 4, :, :].bitcast(I32),
-                    in_=resp_scales[:, 4 * q : 4 * q + 4, :].rearrange("g q e -> q g e").bitcast(I32),
+                    out=rs_raw[k][32 * q : 32 * q + 4, :, :].bitcast(I32),
+                    in_=resp_scales[:, 4 * q : 4 * q + 4, cols].rearrange("g q e -> q g e").bitcast(I32),
                 )
 
         def load_resp(k):
@@ -100,9 +104,10 @@ def tile_active_surface_link_s11_kernel(
                 in_=resp_words[:, :, 1024 * g0 : 1024 * (g0 + w)].rearrange("g p b -> p g b").bitcast(I32),
             )
 
-        def load_inc(grp):
-            cols = slice(512 * grp, 512 * (grp + 1))
-            nc.sync.dma_start(out=inc_b[grp][:], in_=inc_bytes[:, cols].rearrange("(p j) e -> p j e", j=4))
+        def load_inc(k):
+            g0, w = INC_LOADS[k]
+            cols = slice(512 * g0, 512 * (g0 + w))
+            nc.sync.dma_start(out=inc_b[k][:], in_=inc_bytes[:, cols].rearrange("(p j) e -> p j e", j=4))
 
         def load_inc_scale():
             nc.sync.dma_start(out=inc_sc[:], in_=inc_scale.rearrange("(p j) o -> p (j o)", j=4))
@@ -184,10 +189,11 @@ def tile_active_surface_link_s11_kernel(
                 out=sig_codes[:].bitcast(FP8X4), scales=sig_scales[:], in_=sig_grp[:].rearrange("p r t -> p (r t)")
             )
 
-        def sort_scales(dst, cols):
+        def sort_scales(k):
+            dst = (rs_first, rs_rest)[k]
             nc.vector.tensor_copy(
                 out=dst[:].rearrange("p g e -> p (g e)").bitcast(I32).rearrange("p (g t b w) -> p g t b w", g=2, t=4, w=2),
-                in_=rs_raw[:, :, cols].bitcast(I32).rearrange("p g (b t w) -> p g t b w", t=4, w=2),
+                in_=rs_raw[k][:].bitcast(I32).rearrange("p g (b t w) -> p g t b w", t=4, w=2),
             )
 
         def resp_scale(grp, g, t):
@@ -223,7 +229,7 @@ def tile_active_surface_link_s11_kernel(
         inc_wid, inc_grp, plain = {}, {}, set()
 
         def widen(grp, engines="vvvv"):
-            wid = work.tile([P, 4, 512], BF16, name="inc_wid", tag="inc_wid", bufs=WID_BUFS, align_bytes=64)
+            wid = work.tile([P, 4, 512 * INC_LOADS[grp][1]], BF16, name="inc_wid", tag="inc_wid", bufs=WID_BUFS, align_bytes=64)
             inc_wid[grp] = wid
             if "s" in engines:
                 plain.add(grp)
@@ -257,10 +263,11 @@ def tile_active_surface_link_s11_kernel(
                     in_=inc_wid[grp][:].rearrange("p j (q t i) -> p t q i j", t=4, i=8)[:, slots],
                 )
             else:
-                cols = slice(0, 512) if half is None else slice(256 * half, 256 * (half + 1))
+                k = min(grp, len(INC_LOADS) - 1)
+                g0, w = INC_LOADS[k]
                 nc.vector.tensor_copy(
-                    out=inc_grp[grp][:, cols, :].rearrange("p (c i) j -> p c j i", i=4),
-                    in_=inc_wid[grp][:, :, cols].rearrange("p j (c i) -> p c j i", i=4),
+                    out=inc_grp[grp][:].rearrange("p (t c i) j -> p t c j i", t=4, i=4),
+                    in_=inc_wid[k][:].rearrange("p j (t g c i) -> p g t c j i", t=4, g=w, i=4)[:, grp - g0],
                 )
 
         def q_inc(grp):
@@ -384,71 +391,74 @@ def tile_active_surface_link_s11_kernel(
         load_inc_scale()
         load_inc(0)
         load_coef(0)
-        load_scales()
+        load_scales(0)
         load_resp(0)
         load_coef(1)
+        load_coef(2)
+        load_coef(3)
+        load_scales(1)
         load_resp(1)
+        load_inc(1)
         load_sig()
         load_vectors()
         load_resp(2)
-        load_inc(1)
-        load_coef(2)
-        load_coef(3)
         load_inc(2)
         load_coef(4)
         load_coef(5)
-        load_inc(3)
         load_coef(6)
         load_coef(7)
 
         warm_up(4)
         t_coef(0)
-        warm_up(4)
+        warm_up(3)
         widen(0, "vvss")
         c_coef(0, "s")
+        sort_scales(0)
         interleave(0, 0)
-        sort_scales(rs_first, slice(0, 512))
+        perm_resp(0)
         q_coef(0)
         t_coef(1)
         c_coef(1, "s")
-        perm_resp(0)
-        sort_scales(rs_rest, slice(512, E))
-        perm_resp(1)
-        q_coef(1)
         interleave(0, 1)
+        q_coef(1)
         og(0, 0)
-        og(0, 1)
+        t_coef(2)
+        t_coef(3)
+        c_coef(2, "s")
+        q_inc(0)
+        q_coef(2)
+        c_coef(3, "s")
+        sort_scales(1)
+        perm_resp(1)
+        q_coef(3)
         og(1, 0)
+        og(2, 0)
+        og(0, 1)
         og(1, 1)
+        og(3, 0)
         t_sig(0)
         t_sig(1)
         t_vectors()
         c_sig(0, "s")
         c_sig(1, "s")
         c_vectors("s")
-        perm_resp(2)
-        q_inc(0)
         widen(1)
-
-        og(0, 2)
-        og(1, 2)
-        t_coef(2)
-        t_coef(3)
-        c_coef(2, "s")
-        c_coef(3, "s")
-        q_sig()
         interleave(1)
-        field(0)
-        og(0, 3)
-        og(1, 3)
-        q_inc(1)
-        q_coef(2, 2)
-        widen(2)
-        interleave(2)
-        og(2, 0)
-        og(3, 0)
+        perm_resp(2)
+        q_sig()
         og(2, 1)
         og(3, 1)
+        og(0, 2)
+        field(0)
+        widen(2, "vv--")
+        q_inc(1)
+        widen_row(2, 2, "v")
+        widen_row(2, 3, "v")
+        q_outg(0, 0, 2)
+        interleave(2)
+        og(1, 2)
+        og(2, 2)
+        og(3, 2)
         apply_gain(0)
         field(1)
         t_coef(4)
@@ -457,39 +467,35 @@ def tile_active_surface_link_s11_kernel(
         c_coef(5, "s")
         q_inc(2)
         q_refl(0)
-        q_outg(0, 0, 2)
         q_coef(4, 2)
-        og(2, 2)
-        og(3, 2)
+        interleave(3)
+        og(0, 3)
+        og(1, 3)
         t_coef(6)
         t_coef(7)
         c_coef(6, "s")
         c_coef(7, "s")
-        widen(3)
         q_coef(6, 2)
+        q_inc(3)
         apply_gain(1)
         og(2, 3)
         og(3, 3)
-        interleave(3)
         for t in range(4):
             field_slot(2, t)
             final_pass(0, t, 0)
             og(4 + t, 0)
         q_refl(1)
-        q_inc(3)
+        q_outg(0, 2, 2)
         apply_gain(2)
-        og(4, 1)
-        og(5, 1)
         for t in range(4):
+            og(4 + t, 1)
             field_slot(3, t)
             final_pass(0, t, 1)
-            og(*((6, 1), (7, 1), (4, 2), (5, 2))[t])
-        q_outg(0, 2, 2)
         q_refl(2)
-        apply_gain(3)
         q_outg(1, 0, 2)
-        og(6, 2)
-        og(7, 2)
+        apply_gain(3)
+        for n in range(4, 8):
+            og(n, 2)
         final(0, 2)
         q_refl(3)
         og(4, 3)

@@ -46,9 +46,8 @@ def tile_active_surface_link_s11_kernel(
         coef_scales = [kept("coef_scales%d" % n, [P, 512], U8) for n in range(N_COEF // 2)]
         resp_raw = [kept("resp_raw%d" % k, [P, 2, 1024 * w], U8) for k, (g0, w) in enumerate(RESP_LOADS)]
         resp_perm = [kept("resp_perm%d" % k, [P, 2, 1024 * w], U8) for k, (g0, w) in enumerate(RESP_LOADS)]
-        rs_raw = [kept("rs_raw0", [P, 2, 512], U8), kept("rs_raw1", [P, 2, E - 512], U8)]
-        rs_first = kept("rs_first", [P, 2, 512], U8)
-        rs_rest = kept("rs_rest", [P, 2, E - 512], U8)
+        rs_raw = [kept("rs_raw%d" % k, [P, 2, 512 * w], U8) for k, (g0, w) in enumerate(RESP_LOADS)]
+        rs_perm = [kept("rs_perm%d" % k, [P, 2, 512 * w], U8) for k, (g0, w) in enumerate(RESP_LOADS)]
         inc_b = [kept("inc_b%d" % k, [P, 4, 512 * w], U8) for k, (g0, w) in enumerate(INC_LOADS)]
         inc_sc = kept("inc_sc", [P, 4], F32)
         inc_codes = [kept("inc_codes%d" % g, [P, 512], U32) for g in range(GROUPS)]
@@ -63,8 +62,9 @@ def tile_active_surface_link_s11_kernel(
         outg_scales = [[kept("outg_scales%d_%d" % (h, k), [P, 2 * HALF_R], U8) for k in range(2)] for h in range(2)]
         ident = kept("ident", [P, P], F32)
         ident_b = kept("ident_b", [P, P], BF16)
+        vec_raw = kept("vec_raw", [P, 512], BF16)
         vec_b = kept("vec_b", [P, 512], BF16)
-        vec_t = kept("vec_t", [P, GROUPS, 8], F32)
+        vec_t = kept("vec_t", [P, 8, 4], F32)
         dummy = kept("dummy", [P, 1], F32)
         zeros = kept("zeros", [P, 512], BF16)
 
@@ -80,9 +80,9 @@ def tile_active_surface_link_s11_kernel(
         nc.vector.memset(dummy[:], 0.0)
         make_identity(nc, ident[:], nomemset=True)
         nc.vector.memset(zeros[:], 0.0)
-        nc.vector.memset(rs_raw[0][:].rearrange("p g e -> p (g e)").bitcast(I32), 0)
-        nc.vector.memset(rs_raw[1][:].rearrange("p g e -> p (g e)").bitcast(I32), 0)
-        nc.vector.memset(vec_b[:], 0.0)
+        for raw in rs_raw:
+            nc.vector.memset(raw[:].rearrange("p g e -> p (g e)").bitcast(I32), 0)
+        nc.vector.memset(vec_raw[:], 0.0)
         nc.scalar.activation(dummy[:], dummy[:], TANH)
         nc.scalar.copy(out=ident_b[:], in_=ident[:])
 
@@ -90,11 +90,12 @@ def tile_active_surface_link_s11_kernel(
             nc.sync.dma_start(out=coef_raw[n][:], in_=coef[128 * n : 128 * (n + 1), :])
 
         def load_scales(k):
-            cols = (slice(0, 512), slice(512, E))[k]
-            for q in range(4):
+            g0, w = RESP_LOADS[k]
+            cols = slice(512 * g0, 512 * (g0 + w))
+            for r in range(4):
                 nc.sync.dma_start(
-                    out=rs_raw[k][32 * q : 32 * q + 4, :, :].bitcast(I32),
-                    in_=resp_scales[:, 4 * q : 4 * q + 4, cols].rearrange("g q e -> q g e").bitcast(I32),
+                    out=rs_raw[k][r:P:32, :, :].bitcast(I32),
+                    in_=resp_scales[:, r:16:4, cols].rearrange("g q e -> q g e").bitcast(I32),
                 )
 
         def load_resp(k):
@@ -117,10 +118,13 @@ def tile_active_surface_link_s11_kernel(
 
         def load_vectors():
             for v, vec in enumerate((bias, gain)):
-                nc.sync.dma_start(
-                    out=vec_b[4 * v : 4 * v + 4, :].rearrange("t (b i) -> t b i", i=8),
-                    in_=vec.rearrange("(b t i) -> t b i", t=4, i=8),
-                )
+                nc.sync.dma_start(out=vec_raw[4 * v : 4 * v + 4, :], in_=vec.rearrange("(g e) -> g e", g=GROUPS))
+
+        def sort_vectors():
+            nc.scalar.copy(
+                out=vec_b[:].rearrange("p (t q i) -> p t q i", t=4, i=8),
+                in_=vec_raw[:].rearrange("p (q t i) -> p t q i", t=4, i=8),
+            )
 
         def warm_up(count):
             b, bank = take_bank()
@@ -190,17 +194,17 @@ def tile_active_surface_link_s11_kernel(
             )
 
         def sort_scales(k):
-            dst = (rs_first, rs_rest)[k]
+            dst = rs_perm[k]
             nc.vector.tensor_copy(
                 out=dst[:].rearrange("p g e -> p (g e)").bitcast(I32).rearrange("p (g t b w) -> p g t b w", g=2, t=4, w=2),
                 in_=rs_raw[k][:].bitcast(I32).rearrange("p g (b t w) -> p g t b w", t=4, w=2),
             )
 
         def resp_scale(grp, g, t):
-            if grp == 0:
-                return rs_first[:, g, 128 * t : 128 * (t + 1)]
-            so = 384 * t + 128 * (grp - 1)
-            return rs_rest[:, g, so : so + 128]
+            k = min(grp, len(RESP_LOADS) - 1)
+            g0, w = RESP_LOADS[k]
+            so = 128 * (w * t + grp - g0)
+            return rs_perm[k][:, g, so : so + 128]
 
         def perm_resp(k):
             nc.vector.tensor_copy(
@@ -224,7 +228,7 @@ def tile_active_surface_link_s11_kernel(
             vec_bank[0] = bank
 
         def c_vectors(engine):
-            copy(engine, vec_t[:], vec_bank[0][:, 0:GROUPS, 0:8])
+            copy(engine, vec_t[:].rearrange("p r t -> p t r"), vec_bank[0][:, 0:GROUPS, 0:8])
 
         inc_wid, inc_grp, plain = {}, {}, set()
 
@@ -345,7 +349,7 @@ def tile_active_surface_link_s11_kernel(
             nc.vector.tensor_tensor(
                 out=rf[:].rearrange("p (c i) t -> p c t i", i=4),
                 in0=refl_tanh[grp][:].rearrange("p t (c i) -> p c t i", i=4),
-                in1=vec_t[:, grp, 4:8].unsqueeze(1).unsqueeze(3).to_broadcast([P, T // 4, 4, 4]),
+                in1=vec_t[:, 4 + grp, :].unsqueeze(1).unsqueeze(3).to_broadcast([P, T // 4, 4, 4]),
                 op=MULT,
             )
 
@@ -394,15 +398,16 @@ def tile_active_surface_link_s11_kernel(
         load_scales(0)
         load_resp(0)
         load_coef(1)
+        load_inc(1)
         load_coef(2)
         load_coef(3)
         load_scales(1)
         load_resp(1)
-        load_inc(1)
-        load_sig()
         load_vectors()
-        load_resp(2)
+        load_sig()
         load_inc(2)
+        load_scales(2)
+        load_resp(2)
         load_coef(4)
         load_coef(5)
         load_coef(6)
@@ -420,7 +425,9 @@ def tile_active_surface_link_s11_kernel(
         t_coef(1)
         c_coef(1, "s")
         interleave(0, 1)
+        widen(1, "v---")
         q_coef(1)
+        widen_row(1, 1, "v")
         og(0, 0)
         t_coef(2)
         t_coef(3)
@@ -431,42 +438,46 @@ def tile_active_surface_link_s11_kernel(
         sort_scales(1)
         perm_resp(1)
         q_coef(3)
+        widen_row(1, 2, "v")
+        widen_row(1, 3, "v")
         og(1, 0)
+        sort_vectors()
         og(2, 0)
         og(0, 1)
-        og(1, 1)
-        og(3, 0)
         t_sig(0)
         t_sig(1)
         t_vectors()
         c_sig(0, "s")
         c_sig(1, "s")
         c_vectors("s")
-        widen(1)
         interleave(1)
-        perm_resp(2)
+        widen(2, "v---")
         q_sig()
+        sort_scales(2)
+        perm_resp(2)
+        q_inc(1)
+        og(1, 1)
+        og(3, 0)
         og(2, 1)
         og(3, 1)
-        og(0, 2)
         field(0)
-        widen(2, "vv--")
-        q_inc(1)
+        widen_row(2, 1, "v")
         widen_row(2, 2, "v")
         widen_row(2, 3, "v")
-        q_outg(0, 0, 2)
-        interleave(2)
+        og(0, 2)
         og(1, 2)
         og(2, 2)
         og(3, 2)
         apply_gain(0)
+        interleave(2)
+        q_refl(0)
         field(1)
         t_coef(4)
         t_coef(5)
         c_coef(4, "s")
         c_coef(5, "s")
         q_inc(2)
-        q_refl(0)
+        q_outg(0, 0, 2)
         q_coef(4, 2)
         interleave(3)
         og(0, 3)
@@ -481,9 +492,9 @@ def tile_active_surface_link_s11_kernel(
         og(2, 3)
         og(3, 3)
         for t in range(4):
+            og(4 + t, 0)
             field_slot(2, t)
             final_pass(0, t, 0)
-            og(4 + t, 0)
         q_refl(1)
         q_outg(0, 2, 2)
         apply_gain(2)

@@ -24,6 +24,7 @@ N_COEF = R // 128
 HALF_R = 512
 OUTG_BUFS = 3
 WID_BUFS = 2
+GAIN_RUN = 4
 RESP_LOADS = ((0, 1), (1, 1), (2, 2))
 INC_LOADS = ((0, 1), (1, 1), (2, 2))
 
@@ -44,6 +45,7 @@ def tile_active_surface_link_s11_kernel(
         coef_raw = [kept("coef_raw%d" % n, [P, PATHS], BF16) for n in range(N_COEF)]
         coef_codes = [kept("coef_codes%d_x" % n, [P, 512], U32) for n in range(N_COEF // 2)]
         coef_scales = [kept("coef_scales%d" % n, [P, 512], U8) for n in range(N_COEF // 2)]
+        late_grp = kept("late_grp", [P, 2, 2048], BF16)
         resp_raw = [kept("resp_raw%d" % k, [P, 2, 1024 * w], U8) for k, (g0, w) in enumerate(RESP_LOADS)]
         resp_perm = [kept("resp_perm%d" % k, [P, 2, 1024 * w], U8) for k, (g0, w) in enumerate(RESP_LOADS)]
         rs_raw = [kept("rs_raw%d" % k, [P, 2, 512 * w], U8) for k, (g0, w) in enumerate(RESP_LOADS)]
@@ -77,10 +79,11 @@ def tile_active_surface_link_s11_kernel(
             return b, psum.tile(list(shape), dtype, name="bank%d" % b, tag="bank%d" % b)
 
         nc.vector.memset(ident[:], 0.0)
+        nc.vector.memset(zeros[:], 0.0)
+        nc.vector.memset(rs_raw[0][:].rearrange("p g e -> p (g e)").bitcast(I32), 0)
         nc.vector.memset(dummy[:], 0.0)
         make_identity(nc, ident[:], nomemset=True)
-        nc.vector.memset(zeros[:], 0.0)
-        for raw in rs_raw:
+        for raw in rs_raw[1:]:
             nc.vector.memset(raw[:].rearrange("p g e -> p (g e)").bitcast(I32), 0)
         nc.vector.memset(vec_raw[:], 0.0)
         nc.scalar.activation(dummy[:], dummy[:], TANH)
@@ -139,18 +142,36 @@ def tile_active_surface_link_s11_kernel(
 
         coef_bank, coef_grp = {}, {}
 
+        coef_split = {}
+
+        def p_coef(n):
+            coef_split[n] = work.tile([P, 512], I32, name="coef_split", tag="coef_split", bufs=4, align_bytes=64)
+            nc.vector.tensor_copy(
+                out=coef_split[n][:].rearrange("p (g u m) -> p g u m", g=2, u=2),
+                in_=coef_raw[n][:].bitcast(I32).rearrange("p (g m u) -> p g u m", g=2, u=2),
+            )
+
         def t_coef(n):
             b, bank = take_bank()
-            words = coef_raw[n][:].bitcast(F32)
             for g in range(2):
                 for u in range(2):
                     j = 2 * g + u
-                    nc.tensor.transpose(
-                        bank[:, 128 * j : 128 * (j + 1)], words[:, 256 * g + u : 256 * (g + 1) : 2], ident[:]
-                    )
+                    if n in coef_split:
+                        words = coef_split[n][:].bitcast(F32)[:, 128 * j : 128 * (j + 1)]
+                    else:
+                        words = coef_raw[n][:].bitcast(F32)[:, 256 * g + u : 256 * (g + 1) : 2]
+                    nc.tensor.transpose(bank[:, 128 * j : 128 * (j + 1)], words, ident[:])
             coef_bank[n] = bank
 
         def c_coef(n, engine):
+            if n >= 4:
+                lo = 512 * (n - 4)
+                copy(
+                    engine,
+                    late_grp[:, :, lo : lo + 512].bitcast(F32).rearrange("p g (r u) -> p g r u", u=2),
+                    coef_bank[n][:].rearrange("p (g u r) -> p g r u", g=2, u=2),
+                )
+                return
             pair = n // 2
             if pair not in coef_grp:
                 coef_grp[pair] = work.tile([P, 2048], BF16, name="coef_grp", tag="coef_grp", align_bytes=64)
@@ -168,6 +189,16 @@ def tile_active_surface_link_s11_kernel(
                 scales=coef_scales[n // 2][:, cols],
                 in_=coef_grp[n // 2][:, 4 * cols.start : 4 * cols.stop],
             )
+
+        def q_late(g):
+            nc.vector.quantize_mx(out=coef_codes[2 + g][:].bitcast(FP8X4), scales=coef_scales[2 + g][:], in_=late_grp[:, g, :])
+
+        def coef_operand(n, g, count=1):
+            if n >= 4:
+                k, cols = 2 + g, slice(128 * (n - 4), 128 * (n - 4 + count))
+            else:
+                k, cols = n // 2, slice(256 * (n % 2) + 128 * g, 256 * (n % 2) + 128 * (g + 1))
+            return coef_codes[k][:, cols].bitcast(FP8X4), coef_scales[k][:, cols]
 
         sig_bank = {}
 
@@ -230,49 +261,31 @@ def tile_active_surface_link_s11_kernel(
         def c_vectors(engine):
             copy(engine, vec_t[:].rearrange("p r t -> p t r"), vec_bank[0][:, 0:GROUPS, 0:8])
 
-        inc_wid, inc_grp, plain = {}, {}, set()
+        inc_wid, inc_grp = {}, {}
 
-        def widen(grp, engines="vvvv"):
-            wid = work.tile([P, 4, 512 * INC_LOADS[grp][1]], BF16, name="inc_wid", tag="inc_wid", bufs=WID_BUFS, align_bytes=64)
-            inc_wid[grp] = wid
-            if "s" in engines:
-                plain.add(grp)
-            for j in range(4):
-                if engines[j] != "-":
-                    widen_row(grp, j, engines[j])
+        def widen_row(grp, j):
+            if grp not in inc_wid:
+                inc_wid[grp] = work.tile([P, 4, 512], BF16, name="inc_wid", tag="inc_wid", bufs=WID_BUFS, align_bytes=64)
+            k = min(grp, len(INC_LOADS) - 1)
+            lo = 512 * (grp - INC_LOADS[k][0])
+            nc.vector.tensor_scalar(
+                out=inc_wid[grp][:, j, :].rearrange("p (t q i) -> p q t i", t=4, i=8),
+                in0=inc_b[k][:, j, lo : lo + 512].bitcast(FP8).rearrange("p (q t i) -> p q t i", t=4, i=8),
+                scalar1=inc_sc[:, j : j + 1],
+                scalar2=None,
+                op0=MULT,
+            )
 
-        def widen_row(grp, j, engine):
-            src = inc_b[grp][:, j, :].bitcast(FP8)
-            dst = inc_wid[grp][:, j, :]
-            if engine == "s":
-                nc.scalar.activation(dst, src, COPY, scale=inc_sc[:, j : j + 1])
-            elif grp in plain:
-                nc.vector.tensor_scalar(out=dst, in0=src, scalar1=inc_sc[:, j : j + 1], scalar2=None, op0=MULT)
-            else:
-                nc.vector.tensor_scalar(
-                    out=dst.rearrange("p (t q i) -> p q t i", t=4, i=8),
-                    in0=src.rearrange("p (q t i) -> p q t i", t=4, i=8),
-                    scalar1=inc_sc[:, j : j + 1],
-                    scalar2=None,
-                    op0=MULT,
-                )
+        def widen(grp, rows=range(4)):
+            for j in rows:
+                widen_row(grp, j)
 
-        def interleave(grp, half=None):
-            if grp not in inc_grp:
-                inc_grp[grp] = work.tile([P, 512, 4], BF16, name="inc_grp", tag="inc_grp", align_bytes=64)
-            if grp in plain:
-                slots = slice(0, 4) if half is None else slice(2 * half, 2 * half + 2)
-                nc.vector.tensor_copy(
-                    out=inc_grp[grp][:].rearrange("p (t q i) j -> p t q i j", t=4, i=8)[:, slots],
-                    in_=inc_wid[grp][:].rearrange("p j (q t i) -> p t q i j", t=4, i=8)[:, slots],
-                )
-            else:
-                k = min(grp, len(INC_LOADS) - 1)
-                g0, w = INC_LOADS[k]
-                nc.vector.tensor_copy(
-                    out=inc_grp[grp][:].rearrange("p (t c i) j -> p t c j i", t=4, i=4),
-                    in_=inc_wid[k][:].rearrange("p j (t g c i) -> p g t c j i", t=4, g=w, i=4)[:, grp - g0],
-                )
+        def interleave(grp):
+            inc_grp[grp] = work.tile([P, 512, 4], BF16, name="inc_grp", tag="inc_grp", align_bytes=64)
+            nc.vector.tensor_copy(
+                out=inc_grp[grp][:].rearrange("p (c i) j -> p c j i", i=4),
+                in_=inc_wid[grp][:].rearrange("p j (c i) -> p c j i", i=4),
+            )
 
         def q_inc(grp):
             nc.vector.quantize_mx(
@@ -287,13 +300,13 @@ def tile_active_surface_link_s11_kernel(
             b, bank = take_bank()
             for t in range(4):
                 for g in range(2):
-                    cols = slice(256 * (n % 2) + 128 * g, 256 * (n % 2) + 128 * (g + 1))
+                    codes, scales = coef_operand(n, g)
                     nc.tensor.matmul_mx(
                         out=bank[:, 128 * t : 128 * (t + 1)],
                         lhsT=resp_slice(grp, g, t),
                         lhsT_scale=resp_scale(grp, g, t),
-                        rhs=coef_codes[n // 2][:, cols].bitcast(FP8X4),
-                        rhs_scale=coef_scales[n // 2][:, cols],
+                        rhs=codes,
+                        rhs_scale=scales,
                         start=(g == 0),
                         stop=(g == 1),
                     )
@@ -313,6 +326,35 @@ def tile_active_surface_link_s11_kernel(
         def og(n, grp, engine="s"):
             outgoing(n, grp)
             c_outg(n, grp, engine)
+
+        planes = {}
+
+        def og_wide(grp, t, engine="s"):
+            if grp not in planes:
+                planes[grp] = work.tile([P, 4, HALF_R], BF16, name="planes", tag="planes", bufs=2, align_bytes=64)
+            b, bank = take_bank()
+            for g in range(2):
+                codes, scales = coef_operand(4, g, 4)
+                nc.tensor.matmul_mx(
+                    out=bank[:],
+                    lhsT=resp_slice(grp, g, t),
+                    lhsT_scale=resp_scale(grp, g, t),
+                    rhs=codes,
+                    rhs_scale=scales,
+                    start=(g == 0),
+                    stop=(g == 1),
+                )
+            copy(engine, planes[grp][:, t, :], bank[:])
+
+        def il_outg(grp):
+            key = (1, grp // 2)
+            if key not in outg:
+                outg[key] = work.tile([P, 2 * HALF_R, 4], BF16, name="outg", tag="outg", bufs=OUTG_BUFS, align_bytes=64)
+            r0 = HALF_R * (grp % 2)
+            nc.vector.tensor_copy(
+                out=outg[key][:, r0 : r0 + HALF_R, :].rearrange("p (c i) t -> p c t i", i=4),
+                in_=planes[grp][:].rearrange("p t (c i) -> p c t i", i=4),
+            )
 
         def q_outg(h, grp, count=1):
             cols = slice(HALF_R * (grp % 2), HALF_R * (grp % 2 + count))
@@ -343,21 +385,22 @@ def tile_active_surface_link_s11_kernel(
             for t in range(4):
                 field_slot(grp, t)
 
-        def apply_gain(grp):
-            rf = work.tile([P, T, 4], BF16, name="refl", tag="refl", bufs=2, align_bytes=64)
-            refl_grp[grp] = rf
+        def apply_gain(grp, sym=slice(0, T)):
+            if grp not in refl_grp:
+                refl_grp[grp] = work.tile([P, T, 4], BF16, name="refl", tag="refl", bufs=2, align_bytes=64)
+            count = sym.stop - sym.start
             nc.vector.tensor_tensor(
-                out=rf[:].rearrange("p (c i) t -> p c t i", i=4),
-                in0=refl_tanh[grp][:].rearrange("p t (c i) -> p c t i", i=4),
-                in1=vec_t[:, 4 + grp, :].unsqueeze(1).unsqueeze(3).to_broadcast([P, T // 4, 4, 4]),
+                out=refl_grp[grp][:, sym, :].rearrange("p (c i) t -> p c t i", i=GAIN_RUN),
+                in0=refl_tanh[grp][:, :, sym].rearrange("p t (c i) -> p c t i", i=GAIN_RUN),
+                in1=vec_t[:, 4 + grp, :].unsqueeze(1).unsqueeze(3).to_broadcast([P, count // GAIN_RUN, 4, GAIN_RUN]),
                 op=MULT,
             )
 
-        def q_refl(grp):
+        def q_refl(grp, sym=slice(0, T)):
             nc.vector.quantize_mx(
-                out=refl_codes[grp][:].bitcast(FP8X4),
-                scales=refl_scales[grp][:],
-                in_=refl_grp[grp][:].rearrange("p n t -> p (n t)"),
+                out=refl_codes[grp][:, sym].bitcast(FP8X4),
+                scales=refl_scales[grp][:, sym],
+                in_=refl_grp[grp][:, sym, :].rearrange("p n t -> p (n t)"),
             )
 
         fin = {}
@@ -392,146 +435,142 @@ def tile_active_surface_link_s11_kernel(
             )
             ring.append(b)
 
-        load_inc_scale()
-        load_inc(0)
         load_coef(0)
+        load_coef(1)
+        load_coef(2)
         load_scales(0)
         load_resp(0)
-        load_coef(1)
-        load_inc(1)
-        load_coef(2)
+        load_inc_scale()
+        load_inc(0)
         load_coef(3)
-        load_scales(1)
-        load_resp(1)
         load_vectors()
         load_sig()
-        load_inc(2)
+        load_scales(1)
+        load_resp(1)
+        load_inc(1)
+        for n in range(4, 8):
+            load_coef(n)
         load_scales(2)
         load_resp(2)
-        load_coef(4)
-        load_coef(5)
-        load_coef(6)
-        load_coef(7)
+        load_inc(2)
 
-        warm_up(4)
-        t_coef(0)
         warm_up(3)
-        widen(0, "vvss")
-        c_coef(0, "s")
+        for n in range(3):
+            t_coef(n)
+        warm_up(3)
+        for n in range(3):
+            c_coef(n, "s")
         sort_scales(0)
-        interleave(0, 0)
-        perm_resp(0)
         q_coef(0)
-        t_coef(1)
-        c_coef(1, "s")
-        interleave(0, 1)
-        widen(1, "v---")
+        perm_resp(0)
         q_coef(1)
-        widen_row(1, 1, "v")
-        og(0, 0)
-        t_coef(2)
-        t_coef(3)
-        c_coef(2, "s")
-        q_inc(0)
         q_coef(2)
-        c_coef(3, "s")
-        sort_scales(1)
-        perm_resp(1)
-        q_coef(3)
-        widen_row(1, 2, "v")
-        widen_row(1, 3, "v")
-        og(1, 0)
+        for n in range(3):
+            og(n, 0)
+        widen(0)
+        t_coef(3)
         sort_vectors()
-        og(2, 0)
-        og(0, 1)
         t_sig(0)
         t_sig(1)
         t_vectors()
+        c_coef(3, "s")
         c_sig(0, "s")
         c_sig(1, "s")
         c_vectors("s")
-        interleave(1)
-        widen(2, "v---")
+        interleave(0)
+        sort_scales(1)
+        perm_resp(1)
+        q_coef(3)
+        q_inc(0)
+        widen(1, range(2))
         q_sig()
+        og(0, 1)
+        og(3, 0)
+        og(1, 1)
+        widen(1, range(2, 4))
+        p_coef(4)
+        interleave(1)
+        for n in range(5, 8):
+            p_coef(n)
+        field_slot(0, 0)
+        og(2, 1)
+        field_slot(0, 1)
+        og(3, 1)
+        field_slot(0, 2)
+        field_slot(0, 3)
+        for n in range(4, 8):
+            t_coef(n)
+        for n in range(4, 8):
+            c_coef(n, "s")
         sort_scales(2)
         perm_resp(2)
         q_inc(1)
-        og(1, 1)
-        og(3, 0)
-        og(2, 1)
-        og(3, 1)
-        field(0)
-        widen_row(2, 1, "v")
-        widen_row(2, 2, "v")
-        widen_row(2, 3, "v")
-        og(0, 2)
-        og(1, 2)
-        og(2, 2)
-        og(3, 2)
         apply_gain(0)
+        for t in range(4):
+            og(t, 2)
+            field_slot(1, t)
+        widen(2)
+        q_late(0)
+        q_late(1)
         interleave(2)
         q_refl(0)
-        field(1)
-        t_coef(4)
-        t_coef(5)
-        c_coef(4, "s")
-        c_coef(5, "s")
         q_inc(2)
-        q_outg(0, 0, 2)
-        q_coef(4, 2)
+        widen(3)
+        for n in range(4):
+            og(n, 3)
+        q_outg(0, 0)
         interleave(3)
-        og(0, 3)
-        og(1, 3)
-        t_coef(6)
-        t_coef(7)
-        c_coef(6, "s")
-        c_coef(7, "s")
-        q_coef(6, 2)
+        q_outg(0, 1)
         q_inc(3)
-        apply_gain(1)
-        og(2, 3)
-        og(3, 3)
-        for t in range(4):
-            og(4 + t, 0)
-            field_slot(2, t)
-            final_pass(0, t, 0)
-        q_refl(1)
-        q_outg(0, 2, 2)
-        apply_gain(2)
-        for t in range(4):
-            og(4 + t, 1)
-            field_slot(3, t)
-            final_pass(0, t, 1)
-        q_refl(2)
-        q_outg(1, 0, 2)
-        apply_gain(3)
         for n in range(4, 8):
+            og(n, 0)
+        apply_gain(1)
+        for t in range(4):
+            field_slot(2, t)
+            og(4 + t, 1)
+            final_pass(0, t, 0)
+        q_outg(0, 2)
+        q_refl(1)
+        apply_gain(2)
+        field_slot(3, 0)
+        og(4, 2)
+        for t in range(1, 4):
+            field_slot(3, t)
+            final_pass(0, t - 1, 1)
+        final_pass(0, 3, 1)
+        q_outg(0, 3)
+        q_refl(2)
+        for n in range(5, 8):
             og(n, 2)
-        final(0, 2)
-        q_refl(3)
-        og(4, 3)
-        og(5, 3, "v")
+        first, second = slice(0, T // 2), slice(T // 2, T)
+        apply_gain(3, first)
+        q_outg(1, 0, 2)
+        q_refl(3, first)
+        for t in range(4):
+            og(4 + t, 3)
+            final_pass(0, t, 2)
+        apply_gain(3, second)
         q_outg(1, 2)
-        og(6, 3)
-        og(7, 3, "v")
-        final(0, 3)
-        store(0, 0, "s")
-        for m in range(2):
-            for grp in range(3):
-                final_pass(1, m, grp)
+        q_refl(3, second)
         q_outg(1, 3)
-        store(0, 1, "s")
-        store(0, 2, "v")
-        store(0, 3, "s")
-
         for m in range(2):
-            final_pass(1, m, 3)
-            store(1, m, "sv"[m % 2])
+            final_pass(0, m, 3)
+            store(0, m, "s")
+        for m in range(2):
+            for grp in range(2):
+                final_pass(1, m, grp)
+        for m in range(2, 4):
+            final_pass(0, m, 3)
+            store(0, m, "s")
+        for m in range(2):
+            for grp in range(2, 4):
+                final_pass(1, m, grp)
+            store(1, m, "vs"[m % 2])
         for grp in range(GROUPS):
             final_pass(1, 2, grp)
-        store(1, 2, "s")
+        store(1, 2, "v")
         for part in range(2):
             cols = slice(256 * part, 256 * (part + 1))
             for grp in range(GROUPS):
                 final_pass(1, 3, grp, cols)
-            store(1, 3, "vs"[part], cols)
+            store(1, 3, "sv"[part], cols)

@@ -24,7 +24,7 @@ N_COEF = R // 128
 HALF_R = 512
 OUTG_BUFS = 3
 WID_BUFS = 2
-GAIN_RUN = 4
+GAIN_RUN = 2
 RESP_LOADS = ((0, 1), (1, 1), (2, 2))
 INC_LOADS = ((0, 1), (1, 1), (2, 2))
 
@@ -319,8 +319,8 @@ def tile_active_surface_link_s11_kernel(
             r0 = HALF_R * (grp % 2) + 128 * (n % 4)
             copy(
                 engine,
-                outg[key][:, r0 : r0 + 128, :].rearrange("p (c i) t -> p c t i", i=4),
-                outg_bank[(n, grp)][:].rearrange("p (t c i) -> p c t i", t=4, i=4),
+                outg[key][:, r0 : r0 + 128, :],
+                outg_bank[(n, grp)][:].rearrange("p (t r) -> p r t", t=4),
             )
 
         def og(n, grp, engine="s"):

@@ -26,6 +26,8 @@ OUTG_BUFS = 3
 WID_BUFS = 2
 GAIN_RUN = 2
 RESP_LOADS = ((0, 1), (1, 1), (2, 2))
+SCALE_LOADS = ((0, 2), (2, 2))
+COEF_LOADS = ((0, 1), (1, 1), (2, 1), (3, 3), (6, 2))
 INC_LOADS = ((0, 1), (1, 1), (2, 2))
 
 
@@ -42,14 +44,14 @@ def tile_active_surface_link_s11_kernel(
         def kept(name, shape, dtype):
             return keep.tile(shape, dtype, name=name, tag=name, align_bytes=64)
 
-        coef_raw = [kept("coef_raw%d" % n, [P, PATHS], BF16) for n in range(N_COEF)]
+        coef_in = [kept("coef_in%d" % n0, [P, w, PATHS], BF16) for n0, w in COEF_LOADS]
+        coef_raw = [coef_in[k][:, i, :] for k, (n0, w) in enumerate(COEF_LOADS) for i in range(w)]
         coef_codes = [kept("coef_codes%d_x" % n, [P, 512], U32) for n in range(N_COEF // 2)]
         coef_scales = [kept("coef_scales%d" % n, [P, 512], U8) for n in range(N_COEF // 2)]
-        late_grp = kept("late_grp", [P, 2, 2048], BF16)
         resp_raw = [kept("resp_raw%d" % k, [P, 2, 1024 * w], U8) for k, (g0, w) in enumerate(RESP_LOADS)]
         resp_perm = [kept("resp_perm%d" % k, [P, 2, 1024 * w], U8) for k, (g0, w) in enumerate(RESP_LOADS)]
-        rs_raw = [kept("rs_raw%d" % k, [P, 2, 512 * w], U8) for k, (g0, w) in enumerate(RESP_LOADS)]
-        rs_perm = [kept("rs_perm%d" % k, [P, 2, 512 * w], U8) for k, (g0, w) in enumerate(RESP_LOADS)]
+        rs_raw = [kept("rs_raw%d" % k, [P, 2, 512 * w], U8) for k, (g0, w) in enumerate(SCALE_LOADS)]
+        rs_perm = [kept("rs_perm%d" % k, [P, 2, 512 * w], U8) for k, (g0, w) in enumerate(SCALE_LOADS)]
         inc_b = [kept("inc_b%d" % k, [P, 4, 512 * w], U8) for k, (g0, w) in enumerate(INC_LOADS)]
         inc_sc = kept("inc_sc", [P, 4], F32)
         inc_codes = [kept("inc_codes%d" % g, [P, 512], U32) for g in range(GROUPS)]
@@ -90,10 +92,12 @@ def tile_active_surface_link_s11_kernel(
         nc.scalar.copy(out=ident_b[:], in_=ident[:])
 
         def load_coef(n):
-            nc.sync.dma_start(out=coef_raw[n][:], in_=coef[128 * n : 128 * (n + 1), :])
+            n0, w = COEF_LOADS[n]
+            rows = coef[128 * n0 : 128 * (n0 + w), :]
+            nc.sync.dma_start(out=coef_in[n][:], in_=rows.rearrange("(n p) k -> p n k", p=P))
 
         def load_scales(k):
-            g0, w = RESP_LOADS[k]
+            g0, w = SCALE_LOADS[k]
             cols = slice(512 * g0, 512 * (g0 + w))
             for r in range(4):
                 nc.sync.dma_start(
@@ -124,7 +128,7 @@ def tile_active_surface_link_s11_kernel(
                 nc.sync.dma_start(out=vec_raw[4 * v : 4 * v + 4, :], in_=vec.rearrange("(g e) -> g e", g=GROUPS))
 
         def sort_vectors():
-            nc.scalar.copy(
+            nc.vector.tensor_copy(
                 out=vec_b[:].rearrange("p (t q i) -> p t q i", t=4, i=8),
                 in_=vec_raw[:].rearrange("p (q t i) -> p t q i", t=4, i=8),
             )
@@ -144,12 +148,18 @@ def tile_active_surface_link_s11_kernel(
 
         coef_split = {}
 
-        def p_coef(n):
-            coef_split[n] = work.tile([P, 512], I32, name="coef_split", tag="coef_split", bufs=4, align_bytes=64)
-            nc.vector.tensor_copy(
-                out=coef_split[n][:].rearrange("p (g u m) -> p g u m", g=2, u=2),
-                in_=coef_raw[n][:].bitcast(I32).rearrange("p (g m u) -> p g u m", g=2, u=2),
+        def split_words(src, engine):
+            dtype = I32 if engine == "v" else U32
+            dst = work.tile([P, 512], F32, name="split", tag="split", bufs=4, align_bytes=64)
+            copy(
+                engine,
+                dst[:].bitcast(dtype).rearrange("p (g u m) -> p g u m", g=2, u=2),
+                src.bitcast(dtype).rearrange("p (g m u) -> p g u m", g=2, u=2),
             )
+            return dst
+
+        def p_coef(n, engine="v"):
+            coef_split[n] = split_words(coef_raw[n], engine)
 
         def t_coef(n):
             b, bank = take_bank()
@@ -157,24 +167,16 @@ def tile_active_surface_link_s11_kernel(
                 for u in range(2):
                     j = 2 * g + u
                     if n in coef_split:
-                        words = coef_split[n][:].bitcast(F32)[:, 128 * j : 128 * (j + 1)]
+                        words = coef_split[n][:, 128 * j : 128 * (j + 1)]
                     else:
-                        words = coef_raw[n][:].bitcast(F32)[:, 256 * g + u : 256 * (g + 1) : 2]
+                        words = coef_raw[n].bitcast(F32)[:, 256 * g + u : 256 * (g + 1) : 2]
                     nc.tensor.transpose(bank[:, 128 * j : 128 * (j + 1)], words, ident[:])
             coef_bank[n] = bank
 
         def c_coef(n, engine):
-            if n >= 4:
-                lo = 512 * (n - 4)
-                copy(
-                    engine,
-                    late_grp[:, :, lo : lo + 512].bitcast(F32).rearrange("p g (r u) -> p g r u", u=2),
-                    coef_bank[n][:].rearrange("p (g u r) -> p g r u", g=2, u=2),
-                )
-                return
             pair = n // 2
             if pair not in coef_grp:
-                coef_grp[pair] = work.tile([P, 2048], BF16, name="coef_grp", tag="coef_grp", align_bytes=64)
+                coef_grp[pair] = work.tile([P, 2048], BF16, name="coef_grp", tag="coef_grp", bufs=3, align_bytes=64)
             lo = 1024 * (n % 2)
             copy(
                 engine,
@@ -190,25 +192,27 @@ def tile_active_surface_link_s11_kernel(
                 in_=coef_grp[n // 2][:, 4 * cols.start : 4 * cols.stop],
             )
 
-        def q_late(g):
-            nc.vector.quantize_mx(out=coef_codes[2 + g][:].bitcast(FP8X4), scales=coef_scales[2 + g][:], in_=late_grp[:, g, :])
-
-        def coef_operand(n, g, count=1):
-            if n >= 4:
-                k, cols = 2 + g, slice(128 * (n - 4), 128 * (n - 4 + count))
-            else:
-                k, cols = n // 2, slice(256 * (n % 2) + 128 * g, 256 * (n % 2) + 128 * (g + 1))
-            return coef_codes[k][:, cols].bitcast(FP8X4), coef_scales[k][:, cols]
+        def coef_operand(n, g):
+            cols = slice(256 * (n % 2) + 128 * g, 256 * (n % 2) + 128 * (g + 1))
+            return coef_codes[n // 2][:, cols].bitcast(FP8X4), coef_scales[n // 2][:, cols]
 
         sig_bank = {}
 
+        sig_split = {}
+
+        def p_sig(pair, engine="v"):
+            rows = sig_raw[:, 2 * pair : 2 * pair + 2, :].rearrange("p i a -> p (i a)")
+            sig_split[pair] = split_words(rows, engine)
+
         def t_sig(pair):
             b, bank = take_bank()
-            for i in range(2):
-                words = sig_raw[:, 2 * pair + i, :].bitcast(F32)
-                for u in range(2):
-                    j = 2 * i + u
-                    nc.tensor.transpose(bank[:, 128 * j : 128 * (j + 1)], words[:, u:256:2], ident[:])
+            for j in range(4):
+                cols = slice(128 * j, 128 * (j + 1))
+                if pair in sig_split:
+                    words = sig_split[pair][:, cols]
+                else:
+                    words = sig_raw[:, 2 * pair + j // 2, :].bitcast(F32)[:, j % 2 : 256 : 2]
+                nc.tensor.transpose(bank[:, cols], words, ident[:])
             sig_bank[pair] = bank
 
         def c_sig(pair, engine):
@@ -232,8 +236,8 @@ def tile_active_surface_link_s11_kernel(
             )
 
         def resp_scale(grp, g, t):
-            k = min(grp, len(RESP_LOADS) - 1)
-            g0, w = RESP_LOADS[k]
+            k = max(i for i, (g0, w) in enumerate(SCALE_LOADS) if g0 <= grp)
+            g0, w = SCALE_LOADS[k]
             so = 128 * (w * t + grp - g0)
             return rs_perm[k][:, g, so : so + 128]
 
@@ -244,7 +248,7 @@ def tile_active_surface_link_s11_kernel(
             )
 
         def resp_slice(grp, g, t):
-            k = max(i for i, (g0, w) in enumerate(RESP_LOADS) if g0 <= grp)
+            k = min(grp, len(RESP_LOADS) - 1)
             g0, w = RESP_LOADS[k]
             lo = 256 * (w * t + grp - g0)
             return resp_perm[k][:, g, lo : lo + 256].bitcast(FP4X4)
@@ -263,28 +267,27 @@ def tile_active_surface_link_s11_kernel(
 
         inc_wid, inc_grp = {}, {}
 
-        def widen_row(grp, j):
-            if grp not in inc_wid:
-                inc_wid[grp] = work.tile([P, 4, 512], BF16, name="inc_wid", tag="inc_wid", bufs=WID_BUFS, align_bytes=64)
-            k = min(grp, len(INC_LOADS) - 1)
-            lo = 512 * (grp - INC_LOADS[k][0])
-            nc.vector.tensor_scalar(
-                out=inc_wid[grp][:, j, :].rearrange("p (t q i) -> p q t i", t=4, i=8),
-                in0=inc_b[k][:, j, lo : lo + 512].bitcast(FP8).rearrange("p (q t i) -> p q t i", t=4, i=8),
-                scalar1=inc_sc[:, j : j + 1],
-                scalar2=None,
-                op0=MULT,
-            )
-
-        def widen(grp, rows=range(4)):
+        def widen(k, rows=range(4)):
+            if k not in inc_wid:
+                width = 512 * INC_LOADS[k][1]
+                inc_wid[k] = work.tile([P, 4, width], BF16, name="inc_wid", tag="inc_wid", bufs=WID_BUFS, align_bytes=64)
             for j in rows:
-                widen_row(grp, j)
+                nc.vector.tensor_scalar(
+                    out=inc_wid[k][:, j, :].rearrange("p (t q i) -> p q t i", t=4, i=8),
+                    in0=inc_b[k][:, j, :].bitcast(FP8).rearrange("p (q t i) -> p q t i", t=4, i=8),
+                    scalar1=inc_sc[:, j : j + 1],
+                    scalar2=None,
+                    op0=MULT,
+                )
 
-        def interleave(grp):
-            inc_grp[grp] = work.tile([P, 512, 4], BF16, name="inc_grp", tag="inc_grp", align_bytes=64)
+        def interleave(grp, slots=slice(0, 4)):
+            if grp not in inc_grp:
+                inc_grp[grp] = work.tile([P, 512, 4], BF16, name="inc_grp", tag="inc_grp", align_bytes=64)
+            k = min(grp, len(INC_LOADS) - 1)
+            g0, w = INC_LOADS[k]
             nc.vector.tensor_copy(
-                out=inc_grp[grp][:].rearrange("p (c i) j -> p c j i", i=4),
-                in_=inc_wid[grp][:].rearrange("p j (c i) -> p c j i", i=4),
+                out=inc_grp[grp][:].rearrange("p (t c i) j -> p t c j i", t=4, i=4)[:, slots],
+                in_=inc_wid[k][:].rearrange("p j (t g c i) -> p g t c j i", t=4, g=w, i=4)[:, grp - g0, slots],
             )
 
         def q_inc(grp):
@@ -326,35 +329,6 @@ def tile_active_surface_link_s11_kernel(
         def og(n, grp, engine="s"):
             outgoing(n, grp)
             c_outg(n, grp, engine)
-
-        planes = {}
-
-        def og_wide(grp, t, engine="s"):
-            if grp not in planes:
-                planes[grp] = work.tile([P, 4, HALF_R], BF16, name="planes", tag="planes", bufs=2, align_bytes=64)
-            b, bank = take_bank()
-            for g in range(2):
-                codes, scales = coef_operand(4, g, 4)
-                nc.tensor.matmul_mx(
-                    out=bank[:],
-                    lhsT=resp_slice(grp, g, t),
-                    lhsT_scale=resp_scale(grp, g, t),
-                    rhs=codes,
-                    rhs_scale=scales,
-                    start=(g == 0),
-                    stop=(g == 1),
-                )
-            copy(engine, planes[grp][:, t, :], bank[:])
-
-        def il_outg(grp):
-            key = (1, grp // 2)
-            if key not in outg:
-                outg[key] = work.tile([P, 2 * HALF_R, 4], BF16, name="outg", tag="outg", bufs=OUTG_BUFS, align_bytes=64)
-            r0 = HALF_R * (grp % 2)
-            nc.vector.tensor_copy(
-                out=outg[key][:, r0 : r0 + HALF_R, :].rearrange("p (c i) t -> p c t i", i=4),
-                in_=planes[grp][:].rearrange("p t (c i) -> p c t i", i=4),
-            )
 
         def q_outg(h, grp, count=1):
             cols = slice(HALF_R * (grp % 2), HALF_R * (grp % 2 + count))
@@ -437,118 +411,119 @@ def tile_active_surface_link_s11_kernel(
 
         load_coef(0)
         load_coef(1)
-        load_coef(2)
         load_scales(0)
         load_resp(0)
-        load_inc_scale()
         load_inc(0)
-        load_coef(3)
+        load_inc_scale()
+        load_coef(2)
         load_vectors()
         load_sig()
-        load_scales(1)
         load_resp(1)
         load_inc(1)
-        for n in range(4, 8):
-            load_coef(n)
-        load_scales(2)
+        load_coef(3)
+        load_scales(1)
         load_resp(2)
         load_inc(2)
+        load_coef(4)
 
         warm_up(3)
-        for n in range(3):
-            t_coef(n)
+        t_coef(0)
+        t_coef(1)
         warm_up(3)
-        for n in range(3):
-            c_coef(n, "s")
+        c_coef(0, "s")
+        c_coef(1, "s")
         sort_scales(0)
-        q_coef(0)
         perm_resp(0)
+        q_coef(0)
         q_coef(1)
-        q_coef(2)
-        for n in range(3):
-            og(n, 0)
+        og(0, 0)
+        og(1, 0)
         widen(0)
-        t_coef(3)
         sort_vectors()
+        t_coef(2)
         t_sig(0)
         t_sig(1)
         t_vectors()
-        c_coef(3, "s")
+        c_coef(2, "s")
         c_sig(0, "s")
         c_sig(1, "s")
         c_vectors("s")
-        interleave(0)
-        sort_scales(1)
+        interleave(0, slice(0, 2))
         perm_resp(1)
-        q_coef(3)
-        q_inc(0)
-        widen(1, range(2))
+        q_coef(2)
+        interleave(0, slice(2, 4))
         q_sig()
+        q_inc(0)
+        widen(1)
         og(0, 1)
-        og(3, 0)
         og(1, 1)
-        widen(1, range(2, 4))
-        p_coef(4)
-        interleave(1)
-        for n in range(5, 8):
-            p_coef(n)
-        field_slot(0, 0)
+        og(2, 0)
         og(2, 1)
-        field_slot(0, 1)
-        og(3, 1)
-        field_slot(0, 2)
-        field_slot(0, 3)
-        for n in range(4, 8):
+        field(0)
+        for n in range(3, 6):
             t_coef(n)
-        for n in range(4, 8):
+        for n in range(3, 6):
             c_coef(n, "s")
-        sort_scales(2)
+        sort_scales(1)
         perm_resp(2)
+        interleave(1)
+        widen(2, range(1))
         q_inc(1)
+        q_coef(3)
         apply_gain(0)
-        for t in range(4):
-            og(t, 2)
-            field_slot(1, t)
-        widen(2)
-        q_late(0)
-        q_late(1)
+        for n in range(3):
+            og(n, 2)
+        field_slot(1, 0)
+        for grp in range(3):
+            field_slot(1, 1 + grp)
+            og(3, grp)
+        widen(2, range(1, 4))
+        q_coef(4, 2)
+        t_coef(6)
+        t_coef(7)
+        c_coef(6, "s")
+        c_coef(7, "s")
         interleave(2)
         q_refl(0)
-        q_inc(2)
-        widen(3)
         for n in range(4):
             og(n, 3)
-        q_outg(0, 0)
-        interleave(3)
-        q_outg(0, 1)
-        q_inc(3)
-        for n in range(4, 8):
-            og(n, 0)
-        apply_gain(1)
-        for t in range(4):
-            field_slot(2, t)
-            og(4 + t, 1)
-            final_pass(0, t, 0)
-        q_outg(0, 2)
-        q_refl(1)
-        apply_gain(2)
-        field_slot(3, 0)
-        og(4, 2)
+        q_inc(2)
+        q_outg(0, 0, 2)
+        q_coef(6, 2)
+        og(4, 0, "v")
+        og(5, 0)
+        field_slot(2, 0)
         for t in range(1, 4):
+            field_slot(2, t)
+            final_pass(0, t - 1, 0)
+        final_pass(0, 3, 0)
+        apply_gain(1)
+        for n in range(6, 8):
+            og(n, 0)
+        for n in range(4, 8):
+            og(n, 1)
+        interleave(3)
+        q_refl(1)
+        q_inc(3)
+        q_outg(0, 2, 2)
+        og(4, 2)
+        for t in range(4):
+            final_pass(0, t, 1)
             field_slot(3, t)
-            final_pass(0, t - 1, 1)
-        final_pass(0, 3, 1)
-        q_outg(0, 3)
+        apply_gain(2)
+        q_outg(1, 0)
         q_refl(2)
         for n in range(5, 8):
             og(n, 2)
         first, second = slice(0, T // 2), slice(T // 2, T)
         apply_gain(3, first)
-        q_outg(1, 0, 2)
+        q_outg(1, 1)
         q_refl(3, first)
-        for t in range(4):
+        og(4, 3)
+        for t in range(1, 4):
             og(4 + t, 3)
-            final_pass(0, t, 2)
+            final_pass(0, t - 1, 2)
+        final_pass(0, 3, 2)
         apply_gain(3, second)
         q_outg(1, 2)
         q_refl(3, second)

@@ -229,9 +229,8 @@ def tile_active_surface_link_s11_kernel(
             )
 
         def sort_scales(k):
-            dst = rs_perm[k]
             nc.vector.tensor_copy(
-                out=dst[:].rearrange("p g e -> p (g e)").bitcast(I32).rearrange("p (g t b w) -> p g t b w", g=2, t=4, w=2),
+                out=rs_perm[k][:].bitcast(I32).rearrange("p g (t b w) -> p g t b w", t=4, w=2),
                 in_=rs_raw[k][:].bitcast(I32).rearrange("p g (b t w) -> p g t b w", t=4, w=2),
             )
 
@@ -267,28 +266,33 @@ def tile_active_surface_link_s11_kernel(
 
         inc_wid, inc_grp = {}, {}
 
-        def widen(k, rows=range(4)):
+        def widen(k, rows=range(4), engine="v"):
             if k not in inc_wid:
                 width = 512 * INC_LOADS[k][1]
                 inc_wid[k] = work.tile([P, 4, width], BF16, name="inc_wid", tag="inc_wid", bufs=WID_BUFS, align_bytes=64)
             for j in rows:
-                nc.vector.tensor_scalar(
-                    out=inc_wid[k][:, j, :].rearrange("p (t q i) -> p q t i", t=4, i=8),
-                    in0=inc_b[k][:, j, :].bitcast(FP8).rearrange("p (q t i) -> p q t i", t=4, i=8),
-                    scalar1=inc_sc[:, j : j + 1],
-                    scalar2=None,
-                    op0=MULT,
-                )
+                src = inc_b[k][:, j, :].bitcast(FP8)
+                dst = inc_wid[k][:, j, :]
+                if engine == "s":
+                    nc.scalar.activation(dst, src, COPY, scale=inc_sc[:, j : j + 1])
+                    continue
+                if k > 0:
+                    src = src.rearrange("p (q t i) -> p q t i", t=4, i=8)
+                    dst = dst.rearrange("p (t q i) -> p q t i", t=4, i=8)
+                nc.vector.tensor_scalar(out=dst, in0=src, scalar1=inc_sc[:, j : j + 1], scalar2=None, op0=MULT)
 
         def interleave(grp, slots=slice(0, 4)):
             if grp not in inc_grp:
                 inc_grp[grp] = work.tile([P, 512, 4], BF16, name="inc_grp", tag="inc_grp", align_bytes=64)
-            k = min(grp, len(INC_LOADS) - 1)
-            g0, w = INC_LOADS[k]
-            nc.vector.tensor_copy(
-                out=inc_grp[grp][:].rearrange("p (t c i) j -> p t c j i", t=4, i=4)[:, slots],
-                in_=inc_wid[k][:].rearrange("p j (t g c i) -> p g t c j i", t=4, g=w, i=4)[:, grp - g0, slots],
-            )
+            if grp == 0:
+                dst = inc_grp[grp][:].rearrange("p (t q i) j -> p t q j i", t=4, i=8)
+                src = inc_wid[grp][:].rearrange("p j (q t i) -> p t q j i", t=4, i=8)
+            else:
+                k = min(grp, len(INC_LOADS) - 1)
+                g0, w = INC_LOADS[k]
+                dst = inc_grp[grp][:].rearrange("p (t c i) j -> p t c j i", t=4, i=4)
+                src = inc_wid[k][:].rearrange("p j (t g c i) -> p g t c j i", t=4, g=w, i=4)[:, grp - g0]
+            nc.vector.tensor_copy(out=dst[:, slots], in_=src[:, slots])
 
         def q_inc(grp):
             nc.vector.quantize_mx(
@@ -340,9 +344,9 @@ def tile_active_surface_link_s11_kernel(
 
         refl_tanh, refl_grp = {}, {}
 
-        def field_slot(grp, t):
-            if grp not in refl_tanh:
-                refl_tanh[grp] = work.tile([P, 4, T], F32, name="th", tag="th", bufs=3, align_bytes=64)
+        field_bank = {}
+
+        def field_pass(grp, t):
             b, bank = take_bank()
             nc.tensor.matmul_mx(
                 out=bank[:],
@@ -353,11 +357,36 @@ def tile_active_surface_link_s11_kernel(
                 start=True,
                 stop=True,
             )
-            nc.scalar.activation(refl_tanh[grp][:, t, :], bank[:], TANH, bias=vec_t[:, grp, t : t + 1])
+            field_bank[(grp, t)] = bank
 
-        def field(grp):
-            for t in range(4):
-                field_slot(grp, t)
+        def c_field(grp, t):
+            if grp not in refl_tanh:
+                refl_tanh[grp] = work.tile([P, 4, T], F32, name="th", tag="th", bufs=3, align_bytes=64)
+            nc.scalar.activation(refl_tanh[grp][:, t, :], field_bank[(grp, t)][:], TANH, bias=vec_t[:, grp, t : t + 1])
+
+        def field_slot(grp, t):
+            field_pass(grp, t)
+            c_field(grp, t)
+
+        fill = {"o": outgoing, "f": field_pass, "c": t_coef, "s": t_sig}
+        empty = {
+            "o": lambda n, grp: c_outg(n, grp, "s"),
+            "f": c_field,
+            "c": lambda n: c_coef(n, "s"),
+            "s": lambda pair: c_sig(pair, "s"),
+        }
+
+        def batch(*steps):
+            filled = []
+            for kind, *where in steps:
+                if kind == "F":
+                    final_pass(*where)
+                else:
+                    fill[kind](*where)
+                    filled.append((kind, where))
+            for kind, where in reversed(filled):
+                empty[kind](*where)
+            ring[-len(filled) :] = list(reversed(ring[-len(filled) :]))
 
         def apply_gain(grp, sym=slice(0, T)):
             if grp not in refl_grp:
@@ -411,8 +440,8 @@ def tile_active_surface_link_s11_kernel(
 
         load_coef(0)
         load_coef(1)
-        load_scales(0)
         load_resp(0)
+        load_scales(0)
         load_inc(0)
         load_inc_scale()
         load_coef(2)
@@ -432,23 +461,24 @@ def tile_active_surface_link_s11_kernel(
         warm_up(3)
         c_coef(0, "s")
         c_coef(1, "s")
-        sort_scales(0)
         perm_resp(0)
+        sort_scales(0)
         q_coef(0)
         q_coef(1)
+        widen(0, range(2), "s")
         og(0, 0)
         og(1, 0)
-        widen(0)
+        widen(0, range(2, 4))
         sort_vectors()
         t_coef(2)
         t_sig(0)
         t_sig(1)
         t_vectors()
-        c_coef(2, "s")
         c_sig(0, "s")
         c_sig(1, "s")
         c_vectors("s")
         interleave(0, slice(0, 2))
+        c_coef(2, "v")
         perm_resp(1)
         q_coef(2)
         interleave(0, slice(2, 4))
@@ -458,75 +488,67 @@ def tile_active_surface_link_s11_kernel(
         og(0, 1)
         og(1, 1)
         og(2, 0)
-        og(2, 1)
-        field(0)
-        for n in range(3, 6):
-            t_coef(n)
-        for n in range(3, 6):
-            c_coef(n, "s")
+        batch(("o", 2, 1), ("f", 0, 0))
+        batch(("f", 0, 1), ("f", 0, 2), ("f", 0, 3))
+        batch(("c", 4), ("c", 3))
         sort_scales(1)
         perm_resp(2)
+        batch(("c", 5), ("o", 0, 2))
         interleave(1)
         widen(2, range(1))
         q_inc(1)
         q_coef(3)
         apply_gain(0)
-        for n in range(3):
-            og(n, 2)
-        field_slot(1, 0)
-        for grp in range(3):
-            field_slot(1, 1 + grp)
-            og(3, grp)
+        batch(("o", 1, 2), ("o", 2, 2))
+        batch(("f", 1, 0), ("f", 1, 1), ("o", 3, 0))
+        batch(("f", 1, 2), ("o", 3, 1), ("f", 1, 3))
         widen(2, range(1, 4))
-        q_coef(4, 2)
+        og(3, 2)
         t_coef(6)
         t_coef(7)
-        c_coef(6, "s")
-        c_coef(7, "s")
-        interleave(2)
+        q_coef(4, 2)
+        c_coef(7, "v")
+        c_coef(6, "v")
         q_refl(0)
-        for n in range(4):
-            og(n, 3)
-        q_inc(2)
-        q_outg(0, 0, 2)
         q_coef(6, 2)
-        og(4, 0, "v")
-        og(5, 0)
-        field_slot(2, 0)
-        for t in range(1, 4):
-            field_slot(2, t)
-            final_pass(0, t - 1, 0)
-        final_pass(0, 3, 0)
+        interleave(2)
+        batch(("o", 0, 3), ("o", 1, 3))
+        batch(("o", 2, 3), ("o", 3, 3))
+        q_outg(0, 0, 2)
+        q_inc(2)
+        batch(("o", 4, 0), ("o", 5, 0))
+        batch(("o", 6, 0), ("o", 7, 0))
+        batch(("o", 4, 1), ("o", 5, 1))
+        for t in range(0, 4, 2):
+            batch(("F", 0, t, 0), ("f", 2, t), ("F", 0, t + 1, 0), ("f", 2, t + 1))
         apply_gain(1)
-        for n in range(6, 8):
-            og(n, 0)
-        for n in range(4, 8):
-            og(n, 1)
+        batch(("o", 6, 1), ("o", 7, 1))
         interleave(3)
         q_refl(1)
         q_inc(3)
         q_outg(0, 2, 2)
-        og(4, 2)
-        for t in range(4):
-            final_pass(0, t, 1)
-            field_slot(3, t)
+        batch(("o", 4, 2), ("o", 5, 2))
+        for t in range(0, 4, 2):
+            batch(("F", 0, t, 1), ("f", 3, t), ("F", 0, t + 1, 1), ("f", 3, t + 1))
         apply_gain(2)
         q_outg(1, 0)
         q_refl(2)
-        for n in range(5, 8):
-            og(n, 2)
+        batch(("o", 6, 2), ("o", 7, 2))
+        og(4, 3)
         first, second = slice(0, T // 2), slice(T // 2, T)
         apply_gain(3, first)
         q_outg(1, 1)
         q_refl(3, first)
-        og(4, 3)
-        for t in range(1, 4):
-            og(4 + t, 3)
-            final_pass(0, t - 1, 2)
+        og(5, 3)
+        final_pass(0, 0, 2)
+        og(6, 3)
+        final_pass(0, 1, 2)
+        og(7, 3)
+        final_pass(0, 2, 2)
         final_pass(0, 3, 2)
         apply_gain(3, second)
-        q_outg(1, 2)
         q_refl(3, second)
+        q_outg(1, 2)
         q_outg(1, 3)
         for m in range(2):
             final_pass(0, m, 3)
@@ -538,8 +560,9 @@ def tile_active_surface_link_s11_kernel(
             final_pass(0, m, 3)
             store(0, m, "s")
         for m in range(2):
-            for grp in range(2, 4):
-                final_pass(1, m, grp)
+            final_pass(1, m, 2)
+        for m in range(2):
+            final_pass(1, m, 3)
             store(1, m, "vs"[m % 2])
         for grp in range(GROUPS):
             final_pass(1, 2, grp)

@@ -344,9 +344,9 @@ def tile_active_surface_link_s11_kernel(
 
         refl_tanh, refl_grp = {}, {}
 
-        field_bank = {}
-
-        def field_pass(grp, t):
+        def field_slot(grp, t):
+            if grp not in refl_tanh:
+                refl_tanh[grp] = work.tile([P, 4, T], F32, name="th", tag="th", bufs=3, align_bytes=64)
             b, bank = take_bank()
             nc.tensor.matmul_mx(
                 out=bank[:],
@@ -357,36 +357,11 @@ def tile_active_surface_link_s11_kernel(
                 start=True,
                 stop=True,
             )
-            field_bank[(grp, t)] = bank
+            nc.scalar.activation(refl_tanh[grp][:, t, :], bank[:], TANH, bias=vec_t[:, grp, t : t + 1])
 
-        def c_field(grp, t):
-            if grp not in refl_tanh:
-                refl_tanh[grp] = work.tile([P, 4, T], F32, name="th", tag="th", bufs=3, align_bytes=64)
-            nc.scalar.activation(refl_tanh[grp][:, t, :], field_bank[(grp, t)][:], TANH, bias=vec_t[:, grp, t : t + 1])
-
-        def field_slot(grp, t):
-            field_pass(grp, t)
-            c_field(grp, t)
-
-        fill = {"o": outgoing, "f": field_pass, "c": t_coef, "s": t_sig}
-        empty = {
-            "o": lambda n, grp: c_outg(n, grp, "s"),
-            "f": c_field,
-            "c": lambda n: c_coef(n, "s"),
-            "s": lambda pair: c_sig(pair, "s"),
-        }
-
-        def batch(*steps):
-            filled = []
-            for kind, *where in steps:
-                if kind == "F":
-                    final_pass(*where)
-                else:
-                    fill[kind](*where)
-                    filled.append((kind, where))
-            for kind, where in reversed(filled):
-                empty[kind](*where)
-            ring[-len(filled) :] = list(reversed(ring[-len(filled) :]))
+        def field(grp):
+            for t in range(4):
+                field_slot(grp, t)
 
         def apply_gain(grp, sym=slice(0, T)):
             if grp not in refl_grp:
@@ -440,13 +415,13 @@ def tile_active_surface_link_s11_kernel(
 
         load_coef(0)
         load_coef(1)
+        load_coef(2)
         load_resp(0)
         load_scales(0)
         load_inc(0)
         load_inc_scale()
-        load_coef(2)
-        load_vectors()
         load_sig()
+        load_vectors()
         load_resp(1)
         load_inc(1)
         load_coef(3)
@@ -456,21 +431,22 @@ def tile_active_surface_link_s11_kernel(
         load_coef(4)
 
         warm_up(3)
-        t_coef(0)
-        t_coef(1)
-        warm_up(3)
-        c_coef(0, "s")
-        c_coef(1, "s")
+        for n in range(3):
+            t_coef(n)
+        warm_up(2)
+        for n in range(3):
+            c_coef(n, "s")
+        q_coef(0)
         perm_resp(0)
         sort_scales(0)
-        q_coef(0)
         q_coef(1)
+        q_coef(2)
         widen(0, range(2), "s")
-        og(0, 0)
-        og(1, 0)
         widen(0, range(2, 4))
+        og(0, 0, "v")
+        og(1, 0)
+        og(2, 0)
         sort_vectors()
-        t_coef(2)
         t_sig(0)
         t_sig(1)
         t_vectors()
@@ -478,73 +454,81 @@ def tile_active_surface_link_s11_kernel(
         c_sig(1, "s")
         c_vectors("s")
         interleave(0, slice(0, 2))
-        c_coef(2, "v")
         perm_resp(1)
-        q_coef(2)
         interleave(0, slice(2, 4))
-        q_sig()
+        widen(1, range(1))
         q_inc(0)
-        widen(1)
-        og(0, 1)
-        og(1, 1)
-        og(2, 0)
-        batch(("o", 2, 1), ("f", 0, 0))
-        batch(("f", 0, 1), ("f", 0, 2), ("f", 0, 3))
-        batch(("c", 4), ("c", 3))
+        q_sig()
+        widen(1, range(1, 4))
+        for n in range(3):
+            og(n, 1)
+        field(0)
+        for n in range(3, 6):
+            t_coef(n)
+        for n in range(3, 6):
+            c_coef(n, "s")
         sort_scales(1)
         perm_resp(2)
-        batch(("c", 5), ("o", 0, 2))
         interleave(1)
         widen(2, range(1))
         q_inc(1)
         q_coef(3)
         apply_gain(0)
-        batch(("o", 1, 2), ("o", 2, 2))
-        batch(("f", 1, 0), ("f", 1, 1), ("o", 3, 0))
-        batch(("f", 1, 2), ("o", 3, 1), ("f", 1, 3))
+        for n in range(3):
+            og(n, 2)
+        field_slot(1, 0)
+        for grp in range(3):
+            field_slot(1, 1 + grp)
+            og(3, grp)
         widen(2, range(1, 4))
-        og(3, 2)
         t_coef(6)
         t_coef(7)
+        c_coef(6, "v")
         q_coef(4, 2)
         c_coef(7, "v")
-        c_coef(6, "v")
         q_refl(0)
         q_coef(6, 2)
         interleave(2)
-        batch(("o", 0, 3), ("o", 1, 3))
-        batch(("o", 2, 3), ("o", 3, 3))
         q_outg(0, 0, 2)
         q_inc(2)
-        batch(("o", 4, 0), ("o", 5, 0))
-        batch(("o", 6, 0), ("o", 7, 0))
-        batch(("o", 4, 1), ("o", 5, 1))
-        for t in range(0, 4, 2):
-            batch(("F", 0, t, 0), ("f", 2, t), ("F", 0, t + 1, 0), ("f", 2, t + 1))
+        for n in range(4):
+            og(n, 3)
+        for n in range(4, 8):
+            og(n, 0)
+        og(4, 1)
+        og(5, 1)
+        final_pass(0, 0, 0)
+        for t in range(1, 4):
+            final_pass(0, t, 0)
+            field_slot(2, t - 1)
+        field_slot(2, 3)
         apply_gain(1)
-        batch(("o", 6, 1), ("o", 7, 1))
+        og(6, 1)
+        og(7, 1)
         interleave(3)
         q_refl(1)
         q_inc(3)
         q_outg(0, 2, 2)
-        batch(("o", 4, 2), ("o", 5, 2))
-        for t in range(0, 4, 2):
-            batch(("F", 0, t, 1), ("f", 3, t), ("F", 0, t + 1, 1), ("f", 3, t + 1))
+        og(4, 2)
+        og(5, 2)
+        final_pass(0, 0, 1)
+        for t in range(1, 4):
+            final_pass(0, t, 1)
+            field_slot(3, t - 1)
+        field_slot(3, 3)
         apply_gain(2)
         q_outg(1, 0)
         q_refl(2)
-        batch(("o", 6, 2), ("o", 7, 2))
-        og(4, 3)
+        og(6, 2)
+        og(7, 2)
         first, second = slice(0, T // 2), slice(T // 2, T)
         apply_gain(3, first)
         q_outg(1, 1)
         q_refl(3, first)
-        og(5, 3)
-        final_pass(0, 0, 2)
-        og(6, 3)
-        final_pass(0, 1, 2)
-        og(7, 3)
-        final_pass(0, 2, 2)
+        og(4, 3)
+        for t in range(1, 4):
+            og(4 + t, 3)
+            final_pass(0, t - 1, 2)
         final_pass(0, 3, 2)
         apply_gain(3, second)
         q_refl(3, second)

@@ -285,8 +285,11 @@ def tile_active_surface_link_s11_kernel(
             if grp not in inc_grp:
                 inc_grp[grp] = work.tile([P, 512, 4], BF16, name="inc_grp", tag="inc_grp", align_bytes=64)
             if grp == 0:
-                dst = inc_grp[grp][:].rearrange("p (t q i) j -> p t q j i", t=4, i=8)
-                src = inc_wid[grp][:].rearrange("p j (q t i) -> p t q j i", t=4, i=8)
+                dst = inc_grp[grp][:].rearrange("p (t q h i) j -> p t q h j i", t=4, h=2, i=4)
+                src = inc_wid[grp][:].rearrange("p j (q t h i) -> p t q h j i", t=4, h=2, i=4)
+                for t in range(slots.start, slots.stop):
+                    nc.vector.tensor_copy(out=dst[:, t], in_=src[:, t])
+                return
             else:
                 k = min(grp, len(INC_LOADS) - 1)
                 g0, w = INC_LOADS[k]
@@ -525,11 +528,12 @@ def tile_active_surface_link_s11_kernel(
         apply_gain(3, first)
         q_outg(1, 1)
         q_refl(3, first)
-        og(4, 3)
-        for t in range(1, 4):
-            og(4 + t, 3)
-            final_pass(0, t - 1, 2)
-        final_pass(0, 3, 2)
+        for n in range(4, 7):
+            og(n, 3)
+        final_pass(0, 0, 2)
+        og(7, 3)
+        for m in range(1, 4):
+            final_pass(0, m, 2)
         apply_gain(3, second)
         q_refl(3, second)
         q_outg(1, 2)

@@ -19,16 +19,28 @@ COPY = mybir.ActivationFunctionType.Copy
 TANH = mybir.ActivationFunctionType.Tanh
 
 P = 128
+SLOTS = 4
 GROUPS = E // 512
-N_COEF = R // 128
+RECV_TILES = R // 128
 HALF_R = 512
-OUTG_BUFS = 3
-WID_BUFS = 2
-GAIN_RUN = 2
+SCALAR, VECTOR = "scalar", "vector"
+
+COEF_LOADS = ((0, 1), (1, 1), (2, 1), (3, 3), (6, 2))
 RESP_LOADS = ((0, 1), (1, 1), (2, 2))
 SCALE_LOADS = ((0, 2), (2, 2))
-COEF_LOADS = ((0, 1), (1, 1), (2, 1), (3, 3), (6, 2))
 INC_LOADS = ((0, 1), (1, 1), (2, 2))
+
+COEF_BUFS = 3
+OUTG_BUFS = 3
+TANH_BUFS = 3
+RES_BUFS = 8
+GAIN_RUN = 2
+COPY_RUN = 4
+
+
+def load_of(loads, piece):
+    k = max(i for i, (start, count) in enumerate(loads) if start <= piece)
+    return k, loads[k][0], loads[k][1]
 
 
 def tile_active_surface_link_s11_kernel(
@@ -45,19 +57,18 @@ def tile_active_surface_link_s11_kernel(
             return keep.tile(shape, dtype, name=name, tag=name, align_bytes=64)
 
         coef_in = [kept("coef_in%d" % n0, [P, w, PATHS], BF16) for n0, w in COEF_LOADS]
-        coef_raw = [coef_in[k][:, i, :] for k, (n0, w) in enumerate(COEF_LOADS) for i in range(w)]
-        coef_codes = [kept("coef_codes%d_x" % n, [P, 512], U32) for n in range(N_COEF // 2)]
-        coef_scales = [kept("coef_scales%d" % n, [P, 512], U8) for n in range(N_COEF // 2)]
+        coef_codes = [kept("coef_codes%d_x" % n, [P, 512], U32) for n in range(RECV_TILES // 2)]
+        coef_scales = [kept("coef_scales%d" % n, [P, 512], U8) for n in range(RECV_TILES // 2)]
         resp_raw = [kept("resp_raw%d" % k, [P, 2, 1024 * w], U8) for k, (g0, w) in enumerate(RESP_LOADS)]
         resp_perm = [kept("resp_perm%d" % k, [P, 2, 1024 * w], U8) for k, (g0, w) in enumerate(RESP_LOADS)]
         rs_raw = [kept("rs_raw%d" % k, [P, 2, 512 * w], U8) for k, (g0, w) in enumerate(SCALE_LOADS)]
         rs_perm = [kept("rs_perm%d" % k, [P, 2, 512 * w], U8) for k, (g0, w) in enumerate(SCALE_LOADS)]
-        inc_b = [kept("inc_b%d" % k, [P, 4, 512 * w], U8) for k, (g0, w) in enumerate(INC_LOADS)]
-        inc_sc = kept("inc_sc", [P, 4], F32)
+        inc_b = [kept("inc_b%d" % k, [P, SLOTS, 512 * w], U8) for k, (g0, w) in enumerate(INC_LOADS)]
+        inc_sc = kept("inc_sc", [P, SLOTS], F32)
         inc_codes = [kept("inc_codes%d" % g, [P, 512], U32) for g in range(GROUPS)]
         inc_scales = [kept("inc_scales%d" % g, [P, 512], U8) for g in range(GROUPS)]
         sig_raw = kept("sig_raw", [P, 4, A], BF16)
-        sig_grp = kept("sig_grp", [P, T, 4], BF16)
+        sig_grp = kept("sig_grp", [P, T, SLOTS], BF16)
         sig_codes = kept("sig_codes", [P, T], U32)
         sig_scales = kept("sig_scales", [P, T], U8)
         refl_codes = [kept("refl_codes%d" % g, [P, T], U32) for g in range(GROUPS)]
@@ -68,7 +79,7 @@ def tile_active_surface_link_s11_kernel(
         ident_b = kept("ident_b", [P, P], BF16)
         vec_raw = kept("vec_raw", [P, 512], BF16)
         vec_b = kept("vec_b", [P, 512], BF16)
-        vec_t = kept("vec_t", [P, 8, 4], F32)
+        vec_t = kept("vec_t", [P, 2 * GROUPS, SLOTS], F32)
         dummy = kept("dummy", [P, 1], F32)
         zeros = kept("zeros", [P, 512], BF16)
 
@@ -80,21 +91,38 @@ def tile_active_surface_link_s11_kernel(
                 ring.append(b)
             return b, psum.tile(list(shape), dtype, name="bank%d" % b, tag="bank%d" % b)
 
+        def clear_scale_rows(k):
+            nc.vector.memset(rs_raw[k][:].rearrange("p g e -> p (g e)").bitcast(I32), 0)
+
         nc.vector.memset(ident[:], 0.0)
         nc.vector.memset(zeros[:], 0.0)
-        nc.vector.memset(rs_raw[0][:].rearrange("p g e -> p (g e)").bitcast(I32), 0)
+        clear_scale_rows(0)
         nc.vector.memset(dummy[:], 0.0)
         make_identity(nc, ident[:], nomemset=True)
-        for raw in rs_raw[1:]:
-            nc.vector.memset(raw[:].rearrange("p g e -> p (g e)").bitcast(I32), 0)
+        clear_scale_rows(1)
         nc.vector.memset(vec_raw[:], 0.0)
         nc.scalar.activation(dummy[:], dummy[:], TANH)
         nc.scalar.copy(out=ident_b[:], in_=ident[:])
 
-        def load_coef(n):
-            n0, w = COEF_LOADS[n]
+        def warm_up(count):
+            b, bank = take_bank()
+            for i in range(count):
+                nc.tensor.matmul(bank[:], lhsT=zeros[:, 0:P], rhs=zeros[:], start=True, stop=True)
+
+        def copy(engine, dst, src):
+            if engine == VECTOR:
+                nc.vector.tensor_copy(out=dst, in_=src)
+            else:
+                nc.scalar.copy(out=dst, in_=src)
+
+        def quantize(codes, scales, values):
+            nc.vector.quantize_mx(out=codes.bitcast(FP8X4), scales=scales, in_=values)
+
+
+        def load_coef(k):
+            n0, w = COEF_LOADS[k]
             rows = coef[128 * n0 : 128 * (n0 + w), :]
-            nc.sync.dma_start(out=coef_in[n][:], in_=rows.rearrange("(n p) k -> p n k", p=P))
+            nc.sync.dma_start(out=coef_in[k][:], in_=rows.rearrange("(n p) k -> p n k", p=P))
 
         def load_scales(k):
             g0, w = SCALE_LOADS[k]
@@ -115,286 +143,256 @@ def tile_active_surface_link_s11_kernel(
         def load_inc(k):
             g0, w = INC_LOADS[k]
             cols = slice(512 * g0, 512 * (g0 + w))
-            nc.sync.dma_start(out=inc_b[k][:], in_=inc_bytes[:, cols].rearrange("(p j) e -> p j e", j=4))
+            nc.sync.dma_start(out=inc_b[k][:], in_=inc_bytes[:, cols].rearrange("(p j) e -> p j e", j=SLOTS))
 
         def load_inc_scale():
-            nc.sync.dma_start(out=inc_sc[:], in_=inc_scale.rearrange("(p j) o -> p (j o)", j=4))
+            nc.sync.dma_start(out=inc_sc[:], in_=inc_scale.rearrange("(p j) o -> p (j o)", j=SLOTS))
 
         def load_sig():
-            nc.sync.dma_start(out=sig_raw[:], in_=sig.rearrange("(p n) a -> p n a", n=4))
+            nc.sync.dma_start(out=sig_raw[:], in_=sig.rearrange("(p m) a -> p m a", m=4))
 
         def load_vectors():
             for v, vec in enumerate((bias, gain)):
-                nc.sync.dma_start(out=vec_raw[4 * v : 4 * v + 4, :], in_=vec.rearrange("(g e) -> g e", g=GROUPS))
+                rows = slice(GROUPS * v, GROUPS * (v + 1))
+                nc.sync.dma_start(out=vec_raw[rows, :], in_=vec.rearrange("(g e) -> g e", g=GROUPS))
 
-        def sort_vectors():
-            nc.vector.tensor_copy(
-                out=vec_b[:].rearrange("p (t q i) -> p t q i", t=4, i=8),
-                in_=vec_raw[:].rearrange("p (q t i) -> p t q i", t=4, i=8),
-            )
 
-        def warm_up(count):
-            b, bank = take_bank()
-            for i in range(count):
-                nc.tensor.matmul(bank[:], lhsT=zeros[:, 0:P], rhs=zeros[:], start=True, stop=True)
+        coef_bank, coef_grp, sig_bank = {}, {}, {}
 
-        def copy(engine, dst, src):
-            if engine == "v":
-                nc.vector.tensor_copy(out=dst, in_=src)
-            else:
-                nc.scalar.copy(out=dst, in_=src)
+        def turn_words(bank, passes):
+            for j, words in enumerate(passes):
+                for u in range(2):
+                    lo = 128 * (2 * j + u)
+                    nc.tensor.transpose(bank[:, lo : lo + 128], words[:, u:256:2], ident[:])
 
-        coef_bank, coef_grp = {}, {}
-
-        coef_split = {}
-
-        def split_words(src, engine):
-            dtype = I32 if engine == "v" else U32
-            dst = work.tile([P, 512], F32, name="split", tag="split", bufs=4, align_bytes=64)
+        def empty_words(engine, dst, bank):
             copy(
                 engine,
-                dst[:].bitcast(dtype).rearrange("p (g u m) -> p g u m", g=2, u=2),
-                src.bitcast(dtype).rearrange("p (g m u) -> p g u m", g=2, u=2),
+                dst.bitcast(F32).rearrange("p (j r u) -> p j r u", j=2, u=2),
+                bank[:].rearrange("p (j u r) -> p j r u", j=2, u=2),
             )
-            return dst
 
-        def p_coef(n, engine="v"):
-            coef_split[n] = split_words(coef_raw[n], engine)
+        def turn_coef(n):
+            k, n0, w = load_of(COEF_LOADS, n)
+            words = coef_in[k][:, n - n0, :].bitcast(F32)
+            b, coef_bank[n] = take_bank()
+            turn_words(coef_bank[n], [words[:, 256 * g : 256 * (g + 1)] for g in range(2)])
 
-        def t_coef(n):
-            b, bank = take_bank()
-            for g in range(2):
-                for u in range(2):
-                    j = 2 * g + u
-                    if n in coef_split:
-                        words = coef_split[n][:, 128 * j : 128 * (j + 1)]
-                    else:
-                        words = coef_raw[n].bitcast(F32)[:, 256 * g + u : 256 * (g + 1) : 2]
-                    nc.tensor.transpose(bank[:, 128 * j : 128 * (j + 1)], words, ident[:])
-            coef_bank[n] = bank
-
-        def c_coef(n, engine):
+        def empty_coef(n, engine=SCALAR):
             pair = n // 2
             if pair not in coef_grp:
-                coef_grp[pair] = work.tile([P, 2048], BF16, name="coef_grp", tag="coef_grp", bufs=3, align_bytes=64)
+                coef_grp[pair] = work.tile(
+                    [P, 2048], BF16, name="coef_grp", tag="coef_grp", bufs=COEF_BUFS, align_bytes=64
+                )
             lo = 1024 * (n % 2)
-            copy(
-                engine,
-                coef_grp[pair][:, lo : lo + 1024].bitcast(F32).rearrange("p (g r u) -> p g r u", g=2, u=2),
-                coef_bank[n][:].rearrange("p (g u r) -> p g r u", g=2, u=2),
-            )
+            empty_words(engine, coef_grp[pair][:, lo : lo + 1024], coef_bank[n])
 
-        def q_coef(n, count=1):
+        def quant_coef(n, count=1):
             cols = slice(256 * (n % 2), 256 * (n % 2 + count))
-            nc.vector.quantize_mx(
-                out=coef_codes[n // 2][:, cols].bitcast(FP8X4),
-                scales=coef_scales[n // 2][:, cols],
-                in_=coef_grp[n // 2][:, 4 * cols.start : 4 * cols.stop],
-            )
+            values = coef_grp[n // 2][:, SLOTS * cols.start : SLOTS * cols.stop]
+            quantize(coef_codes[n // 2][:, cols], coef_scales[n // 2][:, cols], values)
 
-        def coef_operand(n, g):
-            cols = slice(256 * (n % 2) + 128 * g, 256 * (n % 2) + 128 * (g + 1))
-            return coef_codes[n // 2][:, cols].bitcast(FP8X4), coef_scales[n // 2][:, cols]
+        def turn_sig(pair):
+            b, sig_bank[pair] = take_bank()
+            turn_words(sig_bank[pair], [sig_raw[:, 2 * pair + i, :].bitcast(F32) for i in range(2)])
 
-        sig_bank = {}
+        def empty_sig(pair):
+            dst = sig_grp[:, 256 * pair : 256 * (pair + 1), :].rearrange("p r t -> p (r t)")
+            empty_words(SCALAR, dst, sig_bank[pair])
 
-        sig_split = {}
+        def quant_sig():
+            quantize(sig_codes[:], sig_scales[:], sig_grp[:].rearrange("p r t -> p (r t)"))
 
-        def p_sig(pair, engine="v"):
-            rows = sig_raw[:, 2 * pair : 2 * pair + 2, :].rearrange("p i a -> p (i a)")
-            sig_split[pair] = split_words(rows, engine)
 
-        def t_sig(pair):
-            b, bank = take_bank()
-            for j in range(4):
-                cols = slice(128 * j, 128 * (j + 1))
-                if pair in sig_split:
-                    words = sig_split[pair][:, cols]
-                else:
-                    words = sig_raw[:, 2 * pair + j // 2, :].bitcast(F32)[:, j % 2 : 256 : 2]
-                nc.tensor.transpose(bank[:, cols], words, ident[:])
-            sig_bank[pair] = bank
-
-        def c_sig(pair, engine):
-            dst = sig_grp[:, 256 * pair : 256 * (pair + 1), :].rearrange("p r t -> p (r t)").bitcast(F32)
-            copy(
-                engine,
-                dst.rearrange("p (i r u) -> p i r u", i=2, u=2),
-                sig_bank[pair][:].rearrange("p (i u r) -> p i r u", i=2, u=2),
-            )
-
-        def q_sig():
-            nc.vector.quantize_mx(
-                out=sig_codes[:].bitcast(FP8X4), scales=sig_scales[:], in_=sig_grp[:].rearrange("p r t -> p (r t)")
+        def sort_resp(k):
+            nc.vector.tensor_copy(
+                out=resp_perm[k][:].bitcast(I32).rearrange("p g (t b w) -> p g t b w", t=SLOTS, w=4),
+                in_=resp_raw[k][:].bitcast(I32).rearrange("p g (b t w) -> p g t b w", t=SLOTS, w=4),
             )
 
         def sort_scales(k):
             nc.vector.tensor_copy(
-                out=rs_perm[k][:].bitcast(I32).rearrange("p g (t b w) -> p g t b w", t=4, w=2),
-                in_=rs_raw[k][:].bitcast(I32).rearrange("p g (b t w) -> p g t b w", t=4, w=2),
+                out=rs_perm[k][:].bitcast(I32).rearrange("p g (t b w) -> p g t b w", t=SLOTS, w=2),
+                in_=rs_raw[k][:].bitcast(I32).rearrange("p g (b t w) -> p g t b w", t=SLOTS, w=2),
             )
 
-        def resp_scale(grp, g, t):
-            k = max(i for i, (g0, w) in enumerate(SCALE_LOADS) if g0 <= grp)
-            g0, w = SCALE_LOADS[k]
-            so = 128 * (w * t + grp - g0)
-            return rs_perm[k][:, g, so : so + 128]
-
-        def perm_resp(k):
-            nc.vector.tensor_copy(
-                out=resp_perm[k][:].bitcast(I32).rearrange("p g (t b w) -> p g t b w", t=4, w=4),
-                in_=resp_raw[k][:].bitcast(I32).rearrange("p g (b t w) -> p g t b w", t=4, w=4),
-            )
-
-        def resp_slice(grp, g, t):
-            k = min(grp, len(RESP_LOADS) - 1)
-            g0, w = RESP_LOADS[k]
+        def resp_operand(grp, g, t):
+            k, g0, w = load_of(RESP_LOADS, grp)
             lo = 256 * (w * t + grp - g0)
-            return resp_perm[k][:, g, lo : lo + 256].bitcast(FP4X4)
+            words = resp_perm[k][:, g, lo : lo + 256].bitcast(FP4X4)
+            k, g0, w = load_of(SCALE_LOADS, grp)
+            lo = 128 * (w * t + grp - g0)
+            return words, rs_perm[k][:, g, lo : lo + 128]
 
-        vec_bank = {}
+        vec_bank = []
 
-        def t_vectors():
+        def sort_vectors():
+            nc.vector.tensor_copy(
+                out=vec_b[:].rearrange("p (t q i) -> p t q i", t=SLOTS, i=8),
+                in_=vec_raw[:].rearrange("p (q t i) -> p t q i", t=SLOTS, i=8),
+            )
+
+        def turn_vectors():
             b, bank = take_bank((P, 8, P), BF16)
-            for grp in range(GROUPS):
-                cols = slice(128 * grp, 128 * (grp + 1))
-                nc.tensor.transpose(bank[:, grp, :], vec_b[:, cols], ident_b[:])
-            vec_bank[0] = bank
+            for t in range(SLOTS):
+                nc.tensor.transpose(bank[:, t, :], vec_b[:, 128 * t : 128 * (t + 1)], ident_b[:])
+            vec_bank.append(bank)
 
-        def c_vectors(engine):
-            copy(engine, vec_t[:].rearrange("p r t -> p t r"), vec_bank[0][:, 0:GROUPS, 0:8])
+        def empty_vectors():
+            nc.scalar.copy(out=vec_t[:].rearrange("p r t -> p t r"), in_=vec_bank[0][:, 0:SLOTS, 0 : 2 * GROUPS])
+
 
         inc_wid, inc_grp = {}, {}
 
-        def widen(k, rows=range(4), engine="v"):
+        def widen(k, rows, engine=VECTOR):
             if k not in inc_wid:
                 width = 512 * INC_LOADS[k][1]
-                inc_wid[k] = work.tile([P, 4, width], BF16, name="inc_wid", tag="inc_wid", bufs=WID_BUFS, align_bytes=64)
+                inc_wid[k] = work.tile([P, SLOTS, width], BF16, name="inc_wid", tag="inc_wid", align_bytes=64)
             for j in rows:
                 src = inc_b[k][:, j, :].bitcast(FP8)
                 dst = inc_wid[k][:, j, :]
-                if engine == "s":
-                    nc.scalar.activation(dst, src, COPY, scale=inc_sc[:, j : j + 1])
-                    continue
-                if k > 0:
-                    src = src.rearrange("p (q t i) -> p q t i", t=4, i=8)
-                    dst = dst.rearrange("p (t q i) -> p q t i", t=4, i=8)
-                nc.vector.tensor_scalar(out=dst, in0=src, scalar1=inc_sc[:, j : j + 1], scalar2=None, op0=MULT)
+                scale = inc_sc[:, j : j + 1]
+                if engine == SCALAR:
+                    nc.scalar.activation(dst, src, COPY, scale=scale)
+                elif k == 0:
+                    nc.vector.tensor_scalar(out=dst, in0=src, scalar1=scale, scalar2=None, op0=MULT)
+                else:
+                    nc.vector.tensor_scalar(
+                        out=dst.rearrange("p (t q i) -> p q t i", t=SLOTS, i=8),
+                        in0=src.rearrange("p (q t i) -> p q t i", t=SLOTS, i=8),
+                        scalar1=scale,
+                        scalar2=None,
+                        op0=MULT,
+                    )
 
-        def interleave(grp, slots=slice(0, 4)):
+        def grouped_inc(grp):
             if grp not in inc_grp:
-                inc_grp[grp] = work.tile([P, 512, 4], BF16, name="inc_grp", tag="inc_grp", align_bytes=64)
-            if grp == 0:
-                dst = inc_grp[grp][:].rearrange("p (t q h i) j -> p t q h j i", t=4, h=2, i=4)
-                src = inc_wid[grp][:].rearrange("p j (q t h i) -> p t q h j i", t=4, h=2, i=4)
-                for t in range(slots.start, slots.stop):
-                    nc.vector.tensor_copy(out=dst[:, t], in_=src[:, t])
-                return
-            else:
-                k = min(grp, len(INC_LOADS) - 1)
-                g0, w = INC_LOADS[k]
-                dst = inc_grp[grp][:].rearrange("p (t c i) j -> p t c j i", t=4, i=4)
-                src = inc_wid[k][:].rearrange("p j (t g c i) -> p g t c j i", t=4, g=w, i=4)[:, grp - g0]
-            nc.vector.tensor_copy(out=dst[:, slots], in_=src[:, slots])
+                inc_grp[grp] = work.tile([P, 512, SLOTS], BF16, name="inc_grp", tag="inc_grp", align_bytes=64)
+            return inc_grp[grp]
 
-        def q_inc(grp):
-            nc.vector.quantize_mx(
-                out=inc_codes[grp][:].bitcast(FP8X4),
-                scales=inc_scales[grp][:],
-                in_=inc_grp[grp][:].rearrange("p c j -> p (c j)"),
+        def interleave_first(slots):
+            dst = grouped_inc(0)[:].rearrange("p (t q h i) j -> p t q h j i", t=SLOTS, h=2, i=COPY_RUN)
+            src = inc_wid[0][:].rearrange("p j (q t h i) -> p t q h j i", t=SLOTS, h=2, i=COPY_RUN)
+            for t in slots:
+                nc.vector.tensor_copy(out=dst[:, t], in_=src[:, t])
+
+        def interleave(grp):
+            k, g0, w = load_of(INC_LOADS, grp)
+            src = inc_wid[k][:].rearrange("p j (t g c i) -> p g t c j i", t=SLOTS, g=w, i=COPY_RUN)
+            nc.vector.tensor_copy(
+                out=grouped_inc(grp)[:].rearrange("p (t c i) j -> p t c j i", t=SLOTS, i=COPY_RUN),
+                in_=src[:, grp - g0],
             )
+
+        def quant_inc(grp):
+            quantize(inc_codes[grp][:], inc_scales[grp][:], inc_grp[grp][:].rearrange("p c j -> p (c j)"))
+
 
         outg, outg_bank = {}, {}
 
-        def outgoing(n, grp):
+        def fill_outg(n, grp):
             b, bank = take_bank()
-            for t in range(4):
+            for t in range(SLOTS):
                 for g in range(2):
-                    codes, scales = coef_operand(n, g)
+                    words, word_scales = resp_operand(grp, g, t)
+                    cols = slice(256 * (n % 2) + 128 * g, 256 * (n % 2) + 128 * (g + 1))
                     nc.tensor.matmul_mx(
                         out=bank[:, 128 * t : 128 * (t + 1)],
-                        lhsT=resp_slice(grp, g, t),
-                        lhsT_scale=resp_scale(grp, g, t),
-                        rhs=codes,
-                        rhs_scale=scales,
+                        lhsT=words,
+                        lhsT_scale=word_scales,
+                        rhs=coef_codes[n // 2][:, cols].bitcast(FP8X4),
+                        rhs_scale=coef_scales[n // 2][:, cols],
                         start=(g == 0),
                         stop=(g == 1),
                     )
             outg_bank[(n, grp)] = bank
 
-        def c_outg(n, grp, engine):
+        def empty_outg(n, grp, engine=SCALAR):
             key = (n // 4, grp // 2)
             if key not in outg:
-                outg[key] = work.tile([P, 2 * HALF_R, 4], BF16, name="outg", tag="outg", bufs=OUTG_BUFS, align_bytes=64)
+                outg[key] = work.tile(
+                    [P, 2 * HALF_R, SLOTS], BF16, name="outg", tag="outg", bufs=OUTG_BUFS, align_bytes=64
+                )
             r0 = HALF_R * (grp % 2) + 128 * (n % 4)
-            copy(
-                engine,
-                outg[key][:, r0 : r0 + 128, :],
-                outg_bank[(n, grp)][:].rearrange("p (t r) -> p r t", t=4),
-            )
+            copy(engine, outg[key][:, r0 : r0 + 128, :], outg_bank[(n, grp)][:].rearrange("p (t r) -> p r t", t=SLOTS))
 
-        def og(n, grp, engine="s"):
-            outgoing(n, grp)
-            c_outg(n, grp, engine)
+        def outgoing(n, grp, engine=SCALAR):
+            fill_outg(n, grp)
+            empty_outg(n, grp, engine)
 
-        def q_outg(h, grp, count=1):
+        def quant_outg(h, grp, count=1):
             cols = slice(HALF_R * (grp % 2), HALF_R * (grp % 2 + count))
-            nc.vector.quantize_mx(
-                out=outg_codes[h][grp // 2][:, cols].bitcast(FP8X4),
-                scales=outg_scales[h][grp // 2][:, cols],
-                in_=outg[(h, grp // 2)][:, cols, :].rearrange("p r t -> p (r t)"),
-            )
+            values = outg[(h, grp // 2)][:, cols, :].rearrange("p r t -> p (r t)")
+            quantize(outg_codes[h][grp // 2][:, cols], outg_scales[h][grp // 2][:, cols], values)
 
-        refl_tanh, refl_grp = {}, {}
 
-        def field_slot(grp, t):
-            if grp not in refl_tanh:
-                refl_tanh[grp] = work.tile([P, 4, T], F32, name="th", tag="th", bufs=3, align_bytes=64)
+        field_bank, refl_tanh, refl_grp = {}, {}, {}
+
+        def fill_field(grp, t):
             b, bank = take_bank()
+            cols = slice(128 * t, 128 * (t + 1))
             nc.tensor.matmul_mx(
                 out=bank[:],
-                lhsT=inc_codes[grp][:, 128 * t : 128 * (t + 1)].bitcast(FP8X4),
-                lhsT_scale=inc_scales[grp][:, 128 * t : 128 * (t + 1)],
+                lhsT=inc_codes[grp][:, cols].bitcast(FP8X4),
+                lhsT_scale=inc_scales[grp][:, cols],
                 rhs=sig_codes[:].bitcast(FP8X4),
                 rhs_scale=sig_scales[:],
                 start=True,
                 stop=True,
             )
-            nc.scalar.activation(refl_tanh[grp][:, t, :], bank[:], TANH, bias=vec_t[:, grp, t : t + 1])
+            field_bank[(grp, t)] = bank
 
-        def field(grp):
-            for t in range(4):
-                field_slot(grp, t)
+        def empty_field(grp, t):
+            if grp not in refl_tanh:
+                refl_tanh[grp] = work.tile([P, SLOTS, T], F32, name="th", tag="th", bufs=TANH_BUFS, align_bytes=64)
+            nc.scalar.activation(refl_tanh[grp][:, t, :], field_bank[(grp, t)][:], TANH, bias=vec_t[:, grp, t : t + 1])
+
+        def field(grp, t):
+            fill_field(grp, t)
+            empty_field(grp, t)
 
         def apply_gain(grp, sym=slice(0, T)):
             if grp not in refl_grp:
-                refl_grp[grp] = work.tile([P, T, 4], BF16, name="refl", tag="refl", bufs=2, align_bytes=64)
-            count = sym.stop - sym.start
+                refl_grp[grp] = work.tile([P, T, SLOTS], BF16, name="refl", tag="refl", align_bytes=64)
+            runs = (sym.stop - sym.start) // GAIN_RUN
             nc.vector.tensor_tensor(
                 out=refl_grp[grp][:, sym, :].rearrange("p (c i) t -> p c t i", i=GAIN_RUN),
                 in0=refl_tanh[grp][:, :, sym].rearrange("p t (c i) -> p c t i", i=GAIN_RUN),
-                in1=vec_t[:, 4 + grp, :].unsqueeze(1).unsqueeze(3).to_broadcast([P, count // GAIN_RUN, 4, GAIN_RUN]),
+                in1=vec_t[:, GROUPS + grp, :].unsqueeze(1).unsqueeze(3).to_broadcast([P, runs, SLOTS, GAIN_RUN]),
                 op=MULT,
             )
 
-        def q_refl(grp, sym=slice(0, T)):
-            nc.vector.quantize_mx(
-                out=refl_codes[grp][:, sym].bitcast(FP8X4),
-                scales=refl_scales[grp][:, sym],
-                in_=refl_grp[grp][:, sym, :].rearrange("p n t -> p (n t)"),
-            )
+        def quant_refl(grp, sym=slice(0, T)):
+            values = refl_grp[grp][:, sym, :].rearrange("p n t -> p (n t)")
+            quantize(refl_codes[grp][:, sym], refl_scales[grp][:, sym], values)
 
-        fin = {}
-        out_rows = out.rearrange("(p n) r -> n p r", n=4)
+        def coef_step(n):
+            return lambda: turn_coef(n), lambda: empty_coef(n)
 
-        def final_pass(h, m, grp, recv=slice(0, HALF_R)):
+        def outg_step(n, grp):
+            return lambda: fill_outg(n, grp), lambda: empty_outg(n, grp)
+
+        def field_step(grp, t):
+            return lambda: fill_field(grp, t), lambda: empty_field(grp, t)
+
+        def pair_of(earlier, later):
+            earlier[0]()
+            later[0]()
+            later[1]()
+            earlier[1]()
+
+
+        out_bank = {}
+        out_rows = out.rearrange("(p m) r -> m p r", m=4)
+
+        def out_pass(h, m, grp, recv=slice(0, HALF_R)):
             key = (h, m, recv.start)
-            if key not in fin:
-                fin[key] = take_bank(hold=True)
+            if key not in out_bank:
+                out_bank[key] = take_bank(hold=True)
             cols = slice(128 * m, 128 * (m + 1))
             moving = slice(HALF_R * (grp % 2) + recv.start, HALF_R * (grp % 2) + recv.stop)
             nc.tensor.matmul_mx(
-                out=fin[key][1][:, recv],
+                out=out_bank[key][1][:, recv],
                 lhsT=refl_codes[grp][:, cols].bitcast(FP8X4),
                 lhsT_scale=refl_scales[grp][:, cols],
                 rhs=outg_codes[h][grp // 2][:, moving].bitcast(FP8X4),
@@ -403,22 +401,23 @@ def tile_active_surface_link_s11_kernel(
                 stop=(grp == GROUPS - 1),
             )
 
-        def final(h, grp):
-            for m in range(4):
-                final_pass(h, m, grp)
-
-        def store(h, m, engine, recv=slice(0, HALF_R)):
-            b, bank = fin[(h, m, recv.start)]
-            res = work.tile([P, HALF_R], F32, name="res", tag="res", bufs=8, align_bytes=64)
+        def store(h, m, engine=SCALAR, recv=slice(0, HALF_R)):
+            b, bank = out_bank[(h, m, recv.start)]
+            res = work.tile([P, HALF_R], F32, name="res", tag="res", bufs=RES_BUFS, align_bytes=64)
             copy(engine, res[:, recv], bank[:, recv])
-            nc.sync.dma_start(
-                out=out_rows[m][:, HALF_R * h + recv.start : HALF_R * h + recv.stop], in_=res[:, recv]
-            )
+            nc.sync.dma_start(out=out_rows[m][:, HALF_R * h + recv.start : HALF_R * h + recv.stop], in_=res[:, recv])
             ring.append(b)
 
-        load_coef(0)
-        load_coef(1)
-        load_coef(2)
+        def out_with_field(grp_out, grp_field):
+            out_pass(0, 0, grp_out)
+            for t in range(1, SLOTS):
+                out_pass(0, t, grp_out)
+                field(grp_field, t - 1)
+            field(grp_field, SLOTS - 1)
+
+
+        for k in range(3):
+            load_coef(k)
         load_resp(0)
         load_scales(0)
         load_inc(0)
@@ -435,128 +434,123 @@ def tile_active_surface_link_s11_kernel(
 
         warm_up(3)
         for n in range(3):
-            t_coef(n)
+            turn_coef(n)
         warm_up(2)
         for n in range(3):
-            c_coef(n, "s")
-        q_coef(0)
-        perm_resp(0)
+            empty_coef(n)
+        quant_coef(0)
+        sort_resp(0)
         sort_scales(0)
-        q_coef(1)
-        q_coef(2)
-        widen(0, range(2), "s")
+        quant_coef(1)
+        quant_coef(2)
+
+        widen(0, range(2), SCALAR)
         widen(0, range(2, 4))
-        og(0, 0, "v")
-        og(1, 0)
-        og(2, 0)
+        outgoing(0, 0, VECTOR)
+        outgoing(1, 0)
+        outgoing(2, 0)
         sort_vectors()
-        t_sig(0)
-        t_sig(1)
-        t_vectors()
-        c_sig(0, "s")
-        c_sig(1, "s")
-        c_vectors("s")
-        interleave(0, slice(0, 2))
-        perm_resp(1)
-        interleave(0, slice(2, 4))
+        turn_sig(0)
+        turn_sig(1)
+        turn_vectors()
+        empty_sig(0)
+        empty_sig(1)
+        empty_vectors()
+        interleave_first(range(2))
+        sort_resp(1)
+        interleave_first(range(2, 4))
         widen(1, range(1))
-        q_inc(0)
-        q_sig()
+        quant_inc(0)
+        quant_sig()
         widen(1, range(1, 4))
         for n in range(3):
-            og(n, 1)
-        field(0)
-        for n in range(3, 6):
-            t_coef(n)
-        for n in range(3, 6):
-            c_coef(n, "s")
+            outgoing(n, 1)
+
+        pair_of(field_step(0, 0), field_step(0, 1))
+        pair_of(field_step(0, 2), field_step(0, 3))
+        pair_of(coef_step(4), coef_step(3))
         sort_scales(1)
-        perm_resp(2)
+        sort_resp(2)
+        pair_of(coef_step(5), outg_step(0, 2))
         interleave(1)
         widen(2, range(1))
-        q_inc(1)
-        q_coef(3)
+        quant_inc(1)
+        quant_coef(3)
         apply_gain(0)
-        for n in range(3):
-            og(n, 2)
-        field_slot(1, 0)
-        for grp in range(3):
-            field_slot(1, 1 + grp)
-            og(3, grp)
+        pair_of(outg_step(1, 2), outg_step(2, 2))
+        pair_of(field_step(1, 0), field_step(1, 1))
+        for grp in range(2):
+            pair_of(outg_step(3, grp), field_step(1, 2 + grp))
+        outgoing(3, 2)
         widen(2, range(1, 4))
-        t_coef(6)
-        t_coef(7)
-        c_coef(6, "v")
-        q_coef(4, 2)
-        c_coef(7, "v")
-        q_refl(0)
-        q_coef(6, 2)
+        turn_coef(6)
+        turn_coef(7)
+        quant_coef(4, 2)
+        empty_coef(7, VECTOR)
+        empty_coef(6, VECTOR)
+        quant_refl(0)
+        quant_coef(6, 2)
         interleave(2)
-        q_outg(0, 0, 2)
-        q_inc(2)
-        for n in range(4):
-            og(n, 3)
-        for n in range(4, 8):
-            og(n, 0)
-        og(4, 1)
-        og(5, 1)
-        final_pass(0, 0, 0)
-        for t in range(1, 4):
-            final_pass(0, t, 0)
-            field_slot(2, t - 1)
-        field_slot(2, 3)
+        quant_outg(0, 0, 2)
+        quant_inc(2)
+
+        for n in range(0, 4, 2):
+            pair_of(outg_step(n, 3), outg_step(n + 1, 3))
+        for n in range(4, 8, 2):
+            pair_of(outg_step(n, 0), outg_step(n + 1, 0))
+        pair_of(outg_step(4, 1), outg_step(5, 1))
+
+        out_with_field(0, 2)
         apply_gain(1)
-        og(6, 1)
-        og(7, 1)
+        outgoing(6, 1)
+        outgoing(7, 1)
         interleave(3)
-        q_refl(1)
-        q_inc(3)
-        q_outg(0, 2, 2)
-        og(4, 2)
-        og(5, 2)
-        final_pass(0, 0, 1)
-        for t in range(1, 4):
-            final_pass(0, t, 1)
-            field_slot(3, t - 1)
-        field_slot(3, 3)
+        quant_refl(1)
+        quant_inc(3)
+        quant_outg(0, 2, 2)
+        outgoing(4, 2)
+        outgoing(5, 2)
+        out_with_field(1, 3)
         apply_gain(2)
-        q_outg(1, 0)
-        q_refl(2)
-        og(6, 2)
-        og(7, 2)
-        first, second = slice(0, T // 2), slice(T // 2, T)
-        apply_gain(3, first)
-        q_outg(1, 1)
-        q_refl(3, first)
+        quant_outg(1, 0)
+        quant_refl(2)
+        outgoing(6, 2)
+        outgoing(7, 2)
+
+        early, late = slice(0, T // 2), slice(T // 2, T)
+        apply_gain(3, early)
+        quant_outg(1, 1)
+        quant_refl(3, early)
         for n in range(4, 7):
-            og(n, 3)
-        final_pass(0, 0, 2)
-        og(7, 3)
+            outgoing(n, 3)
+        out_pass(0, 0, 2)
+        outgoing(7, 3)
         for m in range(1, 4):
-            final_pass(0, m, 2)
-        apply_gain(3, second)
-        q_refl(3, second)
-        q_outg(1, 2)
-        q_outg(1, 3)
+            out_pass(0, m, 2)
+        apply_gain(3, late)
+        quant_refl(3, late)
+        quant_outg(1, 2)
+        quant_outg(1, 3)
+
         for m in range(2):
-            final_pass(0, m, 3)
-            store(0, m, "s")
+            out_pass(0, m, 3)
+            store(0, m)
         for m in range(2):
             for grp in range(2):
-                final_pass(1, m, grp)
+                out_pass(1, m, grp)
         for m in range(2, 4):
-            final_pass(0, m, 3)
-            store(0, m, "s")
+            out_pass(0, m, 3)
+            store(0, m)
         for m in range(2):
-            final_pass(1, m, 2)
-        for m in range(2):
-            final_pass(1, m, 3)
-            store(1, m, "vs"[m % 2])
+            out_pass(1, m, 2)
+        for m, engine in enumerate((VECTOR, SCALAR)):
+            out_pass(1, m, 3)
+            store(1, m, engine)
         for grp in range(GROUPS):
-            final_pass(1, 2, grp)
-        store(1, 2, "v")
-        for part in range(2):
-            cols = slice(256 * part, 256 * (part + 1))
+            out_pass(1, 2, grp)
+        store(1, 2, VECTOR)
+        for part, engine in enumerate((SCALAR, VECTOR)):
+            recv = slice(HALF_R // 2 * part, HALF_R // 2 * (part + 1))
             for grp in range(GROUPS):
-                final_pass(1, 3, grp, cols)
-            store(1, 3, "sv"[part], cols)
+                out_pass(1, 3, grp, recv)
+            store(1, 3, engine, recv)

@@ -84,12 +84,25 @@ def tile_active_surface_link_s11_kernel(
         zeros = kept("zeros", [P, 512], BF16)
 
         ring = list(range(8))
+        bank_of = {}
+        emptied = list(range(8))
 
         def take_bank(shape=(P, 512), dtype=F32, hold=False):
             b = ring.pop(0)
             if not hold:
                 ring.append(b)
             return b, psum.tile(list(shape), dtype, name="bank%d" % b, tag="bank%d" % b)
+
+        def note_emptied(b):
+            emptied.remove(b)
+            emptied.append(b)
+
+        def last_emptied_first(count):
+            head = sorted(ring[:count], key=emptied.index, reverse=True)
+            for b in head:
+                ring.remove(b)
+            for b in reversed(head):
+                ring.insert(0, b)
 
         def clear_scale_rows(k):
             nc.vector.memset(rs_raw[k][:].rearrange("p g e -> p (g e)").bitcast(I32), 0)
@@ -175,7 +188,7 @@ def tile_active_surface_link_s11_kernel(
         def turn_coef(n):
             k, n0, w = load_of(COEF_LOADS, n)
             words = coef_in[k][:, n - n0, :].bitcast(F32)
-            b, coef_bank[n] = take_bank()
+            bank_of[("coef", n)], coef_bank[n] = take_bank()
             turn_words(coef_bank[n], [words[:, 256 * g : 256 * (g + 1)] for g in range(2)])
 
         def empty_coef(n, engine=SCALAR):
@@ -186,6 +199,7 @@ def tile_active_surface_link_s11_kernel(
                 )
             lo = 1024 * (n % 2)
             empty_words(engine, coef_grp[pair][:, lo : lo + 1024], coef_bank[n])
+            note_emptied(bank_of[("coef", n)])
 
         def quant_coef(n, count=1):
             cols = slice(256 * (n % 2), 256 * (n % 2 + count))
@@ -193,12 +207,13 @@ def tile_active_surface_link_s11_kernel(
             quantize(coef_codes[n // 2][:, cols], coef_scales[n // 2][:, cols], values)
 
         def turn_sig(pair):
-            b, sig_bank[pair] = take_bank()
+            bank_of[("sig", pair)], sig_bank[pair] = take_bank()
             turn_words(sig_bank[pair], [sig_raw[:, 2 * pair + i, :].bitcast(F32) for i in range(2)])
 
         def empty_sig(pair):
             dst = sig_grp[:, 256 * pair : 256 * (pair + 1), :].rearrange("p r t -> p (r t)")
             empty_words(SCALAR, dst, sig_bank[pair])
+            note_emptied(bank_of[("sig", pair)])
 
         def quant_sig():
             quantize(sig_codes[:], sig_scales[:], sig_grp[:].rearrange("p r t -> p (r t)"))
@@ -233,13 +248,14 @@ def tile_active_surface_link_s11_kernel(
             )
 
         def turn_vectors():
-            b, bank = take_bank((P, 8, P), BF16)
+            bank_of["vectors"], bank = take_bank((P, 8, P), BF16)
             for t in range(SLOTS):
                 nc.tensor.transpose(bank[:, t, :], vec_b[:, 128 * t : 128 * (t + 1)], ident_b[:])
             vec_bank.append(bank)
 
         def empty_vectors():
             nc.scalar.copy(out=vec_t[:].rearrange("p r t -> p t r"), in_=vec_bank[0][:, 0:SLOTS, 0 : 2 * GROUPS])
+            note_emptied(bank_of["vectors"])
 
 
         inc_wid, inc_grp = {}, {}
@@ -291,7 +307,7 @@ def tile_active_surface_link_s11_kernel(
         outg, outg_bank = {}, {}
 
         def fill_outg(n, grp):
-            b, bank = take_bank()
+            bank_of[("outg", n, grp)], bank = take_bank()
             for t in range(SLOTS):
                 for g in range(2):
                     words, word_scales = resp_operand(grp, g, t)
@@ -315,6 +331,7 @@ def tile_active_surface_link_s11_kernel(
                 )
             r0 = HALF_R * (grp % 2) + 128 * (n % 4)
             copy(engine, outg[key][:, r0 : r0 + 128, :], outg_bank[(n, grp)][:].rearrange("p (t r) -> p r t", t=SLOTS))
+            note_emptied(bank_of[("outg", n, grp)])
 
         def outgoing(n, grp, engine=SCALAR):
             fill_outg(n, grp)
@@ -329,7 +346,7 @@ def tile_active_surface_link_s11_kernel(
         field_bank, refl_tanh, refl_grp = {}, {}, {}
 
         def fill_field(grp, t):
-            b, bank = take_bank()
+            bank_of[("field", grp, t)], bank = take_bank()
             cols = slice(128 * t, 128 * (t + 1))
             nc.tensor.matmul_mx(
                 out=bank[:],
@@ -346,6 +363,7 @@ def tile_active_surface_link_s11_kernel(
             if grp not in refl_tanh:
                 refl_tanh[grp] = work.tile([P, SLOTS, T], F32, name="th", tag="th", bufs=TANH_BUFS, align_bytes=64)
             nc.scalar.activation(refl_tanh[grp][:, t, :], field_bank[(grp, t)][:], TANH, bias=vec_t[:, grp, t : t + 1])
+            note_emptied(bank_of[("field", grp, t)])
 
         def field(grp, t):
             fill_field(grp, t)
@@ -407,6 +425,7 @@ def tile_active_surface_link_s11_kernel(
             copy(engine, res[:, recv], bank[:, recv])
             nc.sync.dma_start(out=out_rows[m][:, HALF_R * h + recv.start : HALF_R * h + recv.stop], in_=res[:, recv])
             ring.append(b)
+            note_emptied(b)
 
         def out_with_field(grp_out, grp_field):
             out_pass(0, 0, grp_out)
@@ -463,50 +482,78 @@ def tile_active_surface_link_s11_kernel(
         quant_inc(0)
         quant_sig()
         widen(1, range(1, 4))
-        for n in range(3):
-            outgoing(n, 1)
-
+        outgoing(0, 1)
+        outgoing(1, 1)
+        last_emptied_first(6)
+        outgoing(2, 1)
         pair_of(field_step(0, 0), field_step(0, 1))
         pair_of(field_step(0, 2), field_step(0, 3))
-        pair_of(coef_step(4), coef_step(3))
+        turn_coef(4)
+        last_emptied_first(3)
+        turn_coef(3)
+        empty_coef(4)
         sort_scales(1)
         sort_resp(2)
         pair_of(coef_step(5), outg_step(0, 2))
         interleave(1)
+        empty_coef(3, VECTOR)
         widen(2, range(1))
-        quant_inc(1)
         quant_coef(3)
+        quant_inc(1)
         apply_gain(0)
-        pair_of(outg_step(1, 2), outg_step(2, 2))
-        pair_of(field_step(1, 0), field_step(1, 1))
-        for grp in range(2):
-            pair_of(outg_step(3, grp), field_step(1, 2 + grp))
-        outgoing(3, 2)
+        fill_outg(1, 2)
+        ring.insert(0, ring.pop(1))
+        fill_outg(2, 2)
+        empty_outg(2, 2)
+        empty_outg(1, 2)
+        pair_of(outg_step(3, 0), field_step(1, 0))
+        pair_of(field_step(1, 1), outg_step(3, 1))
+        pair_of(field_step(1, 2), outg_step(3, 2))
+        field(1, 3)
         widen(2, range(1, 4))
         turn_coef(6)
         turn_coef(7)
         quant_coef(4, 2)
         empty_coef(7, VECTOR)
-        empty_coef(6, VECTOR)
+        empty_coef(6)
         quant_refl(0)
         quant_coef(6, 2)
         interleave(2)
         quant_outg(0, 0, 2)
         quant_inc(2)
-
-        for n in range(0, 4, 2):
-            pair_of(outg_step(n, 3), outg_step(n + 1, 3))
-        for n in range(4, 8, 2):
-            pair_of(outg_step(n, 0), outg_step(n + 1, 0))
-        pair_of(outg_step(4, 1), outg_step(5, 1))
-
-        out_with_field(0, 2)
+        pair_of(outg_step(0, 3), outg_step(1, 3))
+        fill_outg(2, 3)
+        last_emptied_first(2)
+        fill_outg(3, 3)
+        empty_outg(3, 3)
+        empty_outg(2, 3)
+        fill_outg(4, 0)
+        last_emptied_first(2)
+        fill_outg(5, 0)
+        empty_outg(5, 0)
+        empty_outg(4, 0)
+        pair_of(outg_step(6, 0), outg_step(7, 0))
+        fill_outg(4, 1)
+        last_emptied_first(5)
+        fill_outg(5, 1)
+        empty_outg(5, 1)
+        empty_outg(4, 1)
+        out_pass(0, 0, 0)
+        out_pass(0, 1, 0)
+        field(2, 0)
+        out_pass(0, 2, 0)
+        last_emptied_first(2)
+        field(2, 1)
+        out_pass(0, 3, 0)
+        last_emptied_first(2)
+        field(2, 2)
+        field(2, 3)
+        interleave(3)
         apply_gain(1)
         outgoing(6, 1)
         outgoing(7, 1)
-        interleave(3)
-        quant_refl(1)
         quant_inc(3)
+        quant_refl(1)
         quant_outg(0, 2, 2)
         outgoing(4, 2)
         outgoing(5, 2)
@@ -516,7 +563,6 @@ def tile_active_surface_link_s11_kernel(
         quant_refl(2)
         outgoing(6, 2)
         outgoing(7, 2)
-
         early, late = slice(0, T // 2), slice(T // 2, T)
         apply_gain(3, early)
         quant_outg(1, 1)
@@ -531,7 +577,7 @@ def tile_active_surface_link_s11_kernel(
         quant_refl(3, late)
         quant_outg(1, 2)
         quant_outg(1, 3)
-
+        last_emptied_first(2)
         for m in range(2):
             out_pass(0, m, 3)
             store(0, m)

@@ -15,7 +15,6 @@ FP8 = mybir.dt.float8_e4m3fn
 FP8X4 = mybir.dt.float8_e4m3fn_x4
 FP4X4 = mybir.dt.float4_e2m1fn_x4
 MULT = mybir.AluOpType.mult
-COPY = mybir.ActivationFunctionType.Copy
 TANH = mybir.ActivationFunctionType.Tanh
 
 P = 128
@@ -260,44 +259,30 @@ def tile_active_surface_link_s11_kernel(
 
         inc_wid, inc_grp = {}, {}
 
-        def widen(k, rows, engine=VECTOR):
+        def widen(k, rows):
             if k not in inc_wid:
                 width = 512 * INC_LOADS[k][1]
                 inc_wid[k] = work.tile([P, SLOTS, width], BF16, name="inc_wid", tag="inc_wid", align_bytes=64)
             for j in rows:
-                src = inc_b[k][:, j, :].bitcast(FP8)
-                dst = inc_wid[k][:, j, :]
-                scale = inc_sc[:, j : j + 1]
-                if engine == SCALAR:
-                    nc.scalar.activation(dst, src, COPY, scale=scale)
-                elif k == 0:
-                    nc.vector.tensor_scalar(out=dst, in0=src, scalar1=scale, scalar2=None, op0=MULT)
-                else:
-                    nc.vector.tensor_scalar(
-                        out=dst.rearrange("p (t q i) -> p q t i", t=SLOTS, i=8),
-                        in0=src.rearrange("p (q t i) -> p q t i", t=SLOTS, i=8),
-                        scalar1=scale,
-                        scalar2=None,
-                        op0=MULT,
-                    )
+                nc.vector.tensor_scalar(
+                    out=inc_wid[k][:, j, :].rearrange("p (t q i) -> p q t i", t=SLOTS, i=8),
+                    in0=inc_b[k][:, j, :].bitcast(FP8).rearrange("p (q t i) -> p q t i", t=SLOTS, i=8),
+                    scalar1=inc_sc[:, j : j + 1],
+                    scalar2=None,
+                    op0=MULT,
+                )
 
         def grouped_inc(grp):
             if grp not in inc_grp:
                 inc_grp[grp] = work.tile([P, 512, SLOTS], BF16, name="inc_grp", tag="inc_grp", align_bytes=64)
             return inc_grp[grp]
 
-        def interleave_first(slots):
-            dst = grouped_inc(0)[:].rearrange("p (t q h i) j -> p t q h j i", t=SLOTS, h=2, i=COPY_RUN)
-            src = inc_wid[0][:].rearrange("p j (q t h i) -> p t q h j i", t=SLOTS, h=2, i=COPY_RUN)
-            for t in slots:
-                nc.vector.tensor_copy(out=dst[:, t], in_=src[:, t])
-
-        def interleave(grp):
+        def interleave(grp, slots=slice(0, SLOTS)):
             k, g0, w = load_of(INC_LOADS, grp)
             src = inc_wid[k][:].rearrange("p j (t g c i) -> p g t c j i", t=SLOTS, g=w, i=COPY_RUN)
             nc.vector.tensor_copy(
-                out=grouped_inc(grp)[:].rearrange("p (t c i) j -> p t c j i", t=SLOTS, i=COPY_RUN),
-                in_=src[:, grp - g0],
+                out=grouped_inc(grp)[:].rearrange("p (t c i) j -> p t c j i", t=SLOTS, i=COPY_RUN)[:, slots],
+                in_=src[:, grp - g0, slots],
             )
 
         def quant_inc(grp):
@@ -435,10 +420,11 @@ def tile_active_surface_link_s11_kernel(
             field(grp_field, SLOTS - 1)
 
 
-        for k in range(3):
-            load_coef(k)
+        load_coef(0)
+        load_coef(1)
         load_resp(0)
         load_scales(0)
+        load_coef(2)
         load_inc(0)
         load_inc_scale()
         load_sig()
@@ -450,24 +436,21 @@ def tile_active_surface_link_s11_kernel(
         load_resp(2)
         load_inc(2)
         load_coef(4)
-
         warm_up(3)
-        for n in range(3):
-            turn_coef(n)
+        turn_coef(0)
+        turn_coef(1)
         warm_up(2)
+        turn_coef(2)
         for n in range(3):
             empty_coef(n)
-        quant_coef(0)
         sort_resp(0)
         sort_scales(0)
+        quant_coef(0)
         quant_coef(1)
+        widen(0, range(4))
         quant_coef(2)
-
-        widen(0, range(2), SCALAR)
-        widen(0, range(2, 4))
-        outgoing(0, 0, VECTOR)
+        outgoing(0, 0)
         outgoing(1, 0)
-        outgoing(2, 0)
         sort_vectors()
         turn_sig(0)
         turn_sig(1)
@@ -475,19 +458,24 @@ def tile_active_surface_link_s11_kernel(
         empty_sig(0)
         empty_sig(1)
         empty_vectors()
-        interleave_first(range(2))
+        outgoing(2, 0)
+        interleave(0, slice(0, 2))
         sort_resp(1)
-        interleave_first(range(2, 4))
+        interleave(0, slice(2, 4))
         widen(1, range(1))
         quant_inc(0)
         quant_sig()
         widen(1, range(1, 4))
         outgoing(0, 1)
         outgoing(1, 1)
-        last_emptied_first(6)
+        last_emptied_first(5)
         outgoing(2, 1)
         pair_of(field_step(0, 0), field_step(0, 1))
-        pair_of(field_step(0, 2), field_step(0, 3))
+        fill_field(0, 2)
+        last_emptied_first(2)
+        fill_field(0, 3)
+        empty_field(0, 3)
+        empty_field(0, 2)
         turn_coef(4)
         last_emptied_first(3)
         turn_coef(3)

@@ -24,14 +24,14 @@ RECV_TILES = R // 128
 HALF_R = 512
 SCALAR, VECTOR = "scalar", "vector"
 
-COEF_LOADS = ((0, 1), (1, 1), (2, 1), (3, 3), (6, 2))
+COEF_LOADS = ((0, 1), (1, 1), (2, 2), (4, 2), (6, 2))
 RESP_LOADS = ((0, 1), (1, 1), (2, 2))
-SCALE_LOADS = ((0, 2), (2, 2))
+SCALE_LOADS = ((0, 1), (1, 3))
 INC_LOADS = ((0, 1), (1, 1), (2, 2))
 
 COEF_BUFS = 3
-OUTG_BUFS = 3
-TANH_BUFS = 3
+OUTG_BUFS = 4
+TANH_BUFS = 2
 RES_BUFS = 8
 GAIN_RUN = 2
 COPY_RUN = 4
@@ -106,10 +106,10 @@ def tile_active_surface_link_s11_kernel(
         def clear_scale_rows(k):
             nc.vector.memset(rs_raw[k][:].rearrange("p g e -> p (g e)").bitcast(I32), 0)
 
+        nc.vector.memset(dummy[:], 0.0)
         nc.vector.memset(ident[:], 0.0)
         nc.vector.memset(zeros[:], 0.0)
         clear_scale_rows(0)
-        nc.vector.memset(dummy[:], 0.0)
         make_identity(nc, ident[:], nomemset=True)
         clear_scale_rows(1)
         nc.vector.memset(vec_raw[:], 0.0)
@@ -171,11 +171,22 @@ def tile_active_surface_link_s11_kernel(
 
         coef_bank, coef_grp, sig_bank = {}, {}, {}
 
-        def turn_words(bank, passes):
+        def turn_words(bank, passes, is_split=False):
             for j, words in enumerate(passes):
                 for u in range(2):
                     lo = 128 * (2 * j + u)
-                    nc.tensor.transpose(bank[:, lo : lo + 128], words[:, u:256:2], ident[:])
+                    picked = words[:, 128 * u : 128 * (u + 1)] if is_split else words[:, u:256:2]
+                    nc.tensor.transpose(bank[:, lo : lo + 128], picked, ident[:])
+
+        coef_split = {}
+
+        def split_coef(k):
+            w = COEF_LOADS[k][1]
+            coef_split[k] = kept("coef_split%d" % k, [P, w, PATHS // 2], F32)
+            nc.vector.tensor_copy(
+                out=coef_split[k][:].rearrange("p n (g u c i) -> p (n g) c u i", g=2, u=2, i=4),
+                in_=coef_in[k][:].bitcast(F32).rearrange("p n (g c i u) -> p (n g) c u i", g=2, u=2, i=4),
+            )
 
         def empty_words(engine, dst, bank):
             copy(
@@ -186,9 +197,9 @@ def tile_active_surface_link_s11_kernel(
 
         def turn_coef(n):
             k, n0, w = load_of(COEF_LOADS, n)
-            words = coef_in[k][:, n - n0, :].bitcast(F32)
+            words = coef_split[k][:, n - n0, :] if k in coef_split else coef_in[k][:, n - n0, :].bitcast(F32)
             bank_of[("coef", n)], coef_bank[n] = take_bank()
-            turn_words(coef_bank[n], [words[:, 256 * g : 256 * (g + 1)] for g in range(2)])
+            turn_words(coef_bank[n], [words[:, 256 * g : 256 * (g + 1)] for g in range(2)], k in coef_split)
 
         def empty_coef(n, engine=SCALAR):
             pair = n // 2
@@ -247,13 +258,16 @@ def tile_active_surface_link_s11_kernel(
             )
 
         def turn_vectors():
-            bank_of["vectors"], bank = take_bank((P, 8, P), BF16)
+            bank_of["vectors"], bank = take_bank((P, 8, P), BF16, hold=True)
             for t in range(SLOTS):
                 nc.tensor.transpose(bank[:, t, :], vec_b[:, 128 * t : 128 * (t + 1)], ident_b[:])
             vec_bank.append(bank)
 
         def empty_vectors():
             nc.scalar.copy(out=vec_t[:].rearrange("p r t -> p t r"), in_=vec_bank[0][:, 0:SLOTS, 0 : 2 * GROUPS])
+
+        def release_vectors():
+            ring.append(bank_of["vectors"])
             note_emptied(bank_of["vectors"])
 
 
@@ -274,15 +288,28 @@ def tile_active_surface_link_s11_kernel(
 
         def grouped_inc(grp):
             if grp not in inc_grp:
-                inc_grp[grp] = work.tile([P, 512, SLOTS], BF16, name="inc_grp", tag="inc_grp", align_bytes=64)
+                inc_grp[grp] = work.tile([P, 512, SLOTS], BF16, name="inc_grp", tag="inc_grp", bufs=1, align_bytes=64)
             return inc_grp[grp]
 
-        def interleave(grp, slots=slice(0, SLOTS)):
+        def interleave(grp, slots=slice(0, SLOTS), cols=slice(0, 128)):
             k, g0, w = load_of(INC_LOADS, grp)
-            src = inc_wid[k][:].rearrange("p j (t g c i) -> p g t c j i", t=SLOTS, g=w, i=COPY_RUN)
+            src = inc_wid[k][:].rearrange("p j (t g c) -> p g t c j", t=SLOTS, g=w)[:, grp - g0, slots, cols]
+            dst = grouped_inc(grp)[:].rearrange("p (t c) j -> p t c j", t=SLOTS)[:, slots, cols]
             nc.vector.tensor_copy(
-                out=grouped_inc(grp)[:].rearrange("p (t c i) j -> p t c j i", t=SLOTS, i=COPY_RUN)[:, slots],
-                in_=src[:, grp - g0, slots],
+                out=dst.rearrange("p t (c i) j -> p t c j i", i=COPY_RUN),
+                in_=src.rearrange("p t (c i) j -> p t c j i", i=COPY_RUN),
+            )
+
+        def interleave_on_gpsimd(grp, cols):
+            k, g0, w = load_of(INC_LOADS, grp)
+            src = inc_wid[k][:].rearrange("p j (t g c) -> p g t c j", t=SLOTS, g=w)
+            nc.gpsimd.tensor_scalar(
+                out=grouped_inc(grp)[:].rearrange("p (t c) j -> p t c j", t=SLOTS)[:, :, cols],
+                in0=src[:, grp - g0, :, cols],
+                scalar1=1.0,
+                scalar2=1.0,
+                op0=MULT,
+                op1=MULT,
             )
 
         def quant_inc(grp):
@@ -354,14 +381,15 @@ def tile_active_surface_link_s11_kernel(
             fill_field(grp, t)
             empty_field(grp, t)
 
-        def apply_gain(grp, sym=slice(0, T)):
+        def apply_gain(grp, sym=slice(0, T), from_psum=False):
             if grp not in refl_grp:
                 refl_grp[grp] = work.tile([P, T, SLOTS], BF16, name="refl", tag="refl", align_bytes=64)
             runs = (sym.stop - sym.start) // GAIN_RUN
+            gains = vec_bank[0][:, 0:SLOTS, GROUPS + grp] if from_psum else vec_t[:, GROUPS + grp, :]
             nc.vector.tensor_tensor(
                 out=refl_grp[grp][:, sym, :].rearrange("p (c i) t -> p c t i", i=GAIN_RUN),
                 in0=refl_tanh[grp][:, :, sym].rearrange("p t (c i) -> p c t i", i=GAIN_RUN),
-                in1=vec_t[:, GROUPS + grp, :].unsqueeze(1).unsqueeze(3).to_broadcast([P, runs, SLOTS, GAIN_RUN]),
+                in1=gains.unsqueeze(1).unsqueeze(3).to_broadcast([P, runs, SLOTS, GAIN_RUN]),
                 op=MULT,
             )
 
@@ -422,166 +450,155 @@ def tile_active_surface_link_s11_kernel(
 
         load_coef(0)
         load_coef(1)
+        load_coef(2)
         load_resp(0)
         load_scales(0)
-        load_coef(2)
         load_inc(0)
         load_inc_scale()
         load_sig()
         load_vectors()
         load_resp(1)
-        load_inc(1)
-        load_coef(3)
         load_scales(1)
+        load_inc(1)
         load_resp(2)
-        load_inc(2)
+        load_coef(3)
         load_coef(4)
+        load_inc(2)
         warm_up(3)
         turn_coef(0)
         turn_coef(1)
-        warm_up(2)
+        warm_up(1)
         turn_coef(2)
-        for n in range(3):
+        turn_coef(3)
+        warm_up(1)
+        for n in range(4):
             empty_coef(n)
+        quant_coef(0)
         sort_resp(0)
         sort_scales(0)
-        quant_coef(0)
         quant_coef(1)
-        widen(0, range(4))
         quant_coef(2)
-        outgoing(0, 0)
-        outgoing(1, 0)
+        widen(0, range(2))
+        quant_coef(3)
+        widen(0, range(2, 4))
         sort_vectors()
+        for n in range(4):
+            outgoing(n, 0)
         turn_sig(0)
         turn_sig(1)
         turn_vectors()
         empty_sig(0)
         empty_sig(1)
         empty_vectors()
-        outgoing(2, 0)
-        interleave(0, slice(0, 2))
         sort_resp(1)
-        interleave(0, slice(2, 4))
+        interleave(0, slice(0, 1))
+        sort_scales(1)
+        interleave(0, slice(1, 4))
         widen(1, range(1))
         quant_inc(0)
         quant_sig()
-        widen(1, range(1, 4))
-        outgoing(0, 1)
-        outgoing(1, 1)
-        last_emptied_first(5)
-        outgoing(2, 1)
+        widen(1, range(1, 3))
+        sort_resp(2)
+        widen(1, range(3, 4))
+        split_coef(3)
+        interleave(1)
+        split_coef(4)
+        quant_inc(1)
+        for n in range(3):
+            outgoing(n, 1)
+        last_emptied_first(2)
+        outgoing(3, 1)
         pair_of(field_step(0, 0), field_step(0, 1))
         fill_field(0, 2)
         last_emptied_first(2)
         fill_field(0, 3)
         empty_field(0, 3)
         empty_field(0, 2)
-        turn_coef(4)
-        last_emptied_first(3)
-        turn_coef(3)
-        empty_coef(4)
-        sort_scales(1)
-        sort_resp(2)
-        pair_of(coef_step(5), outg_step(0, 2))
-        interleave(1)
-        empty_coef(3, VECTOR)
-        widen(2, range(1))
-        quant_coef(3)
-        quant_inc(1)
-        apply_gain(0)
-        fill_outg(1, 2)
-        ring.insert(0, ring.pop(1))
+        pair_of(outg_step(0, 2), outg_step(1, 2))
         fill_outg(2, 2)
+        fill_outg(3, 2)
+        for n in range(4, 8):
+            turn_coef(n)
+        empty_outg(3, 2)
         empty_outg(2, 2)
-        empty_outg(1, 2)
-        pair_of(outg_step(3, 0), field_step(1, 0))
-        pair_of(field_step(1, 1), outg_step(3, 1))
-        pair_of(field_step(1, 2), outg_step(3, 2))
-        field(1, 3)
-        widen(2, range(1, 4))
-        turn_coef(6)
-        turn_coef(7)
-        quant_coef(4, 2)
-        empty_coef(7, VECTOR)
+        widen(2, range(2))
+        empty_coef(4, VECTOR)
+        empty_coef(5)
+        empty_coef(7)
         empty_coef(6)
-        quant_refl(0)
+        widen(2, range(2, 3))
+        quant_coef(4, 2)
+        widen(2, range(3, 4))
+        interleave_on_gpsimd(2, slice(0, 96))
+        apply_gain(0, from_psum=True)
+        for t in range(4):
+            pair_of(outg_step(t, 3), field_step(1, t))
+        outgoing(4, 0, VECTOR)
         quant_coef(6, 2)
-        interleave(2)
-        quant_outg(0, 0, 2)
+        interleave(2, cols=slice(96, 128))
+        quant_refl(0)
+        quant_outg(0, 0)
         quant_inc(2)
-        pair_of(outg_step(0, 3), outg_step(1, 3))
-        fill_outg(2, 3)
-        last_emptied_first(2)
-        fill_outg(3, 3)
-        empty_outg(3, 3)
-        empty_outg(2, 3)
-        fill_outg(4, 0)
-        last_emptied_first(2)
-        fill_outg(5, 0)
-        empty_outg(5, 0)
-        empty_outg(4, 0)
+        interleave_on_gpsimd(3, slice(0, 96))
+        apply_gain(1, from_psum=True)
+        outgoing(5, 0)
+        pair_of(outg_step(4, 1), outg_step(5, 1))
         pair_of(outg_step(6, 0), outg_step(7, 0))
-        fill_outg(4, 1)
-        last_emptied_first(5)
-        fill_outg(5, 1)
-        empty_outg(5, 1)
-        empty_outg(4, 1)
-        out_pass(0, 0, 0)
-        out_pass(0, 1, 0)
-        field(2, 0)
-        out_pass(0, 2, 0)
-        last_emptied_first(2)
-        field(2, 1)
-        out_pass(0, 3, 0)
-        last_emptied_first(2)
-        field(2, 2)
-        field(2, 3)
-        interleave(3)
-        apply_gain(1)
         outgoing(6, 1)
-        outgoing(7, 1)
-        quant_inc(3)
+        last_emptied_first(2)
+        outgoing(7, 1, VECTOR)
+        interleave(3, cols=slice(96, 128))
         quant_refl(1)
-        quant_outg(0, 2, 2)
+        quant_inc(3)
+        quant_outg(0, 1)
+        field(2, 0)
+        field(2, 1)
+        out_pass(0, 0, 0)
         outgoing(4, 2)
+        field(2, 2)
+        out_pass(0, 1, 0)
+        release_vectors()
         outgoing(5, 2)
-        out_with_field(1, 3)
-        apply_gain(2)
-        quant_outg(1, 0)
-        quant_refl(2)
+        field(2, 3)
+        out_pass(0, 2, 0)
         outgoing(6, 2)
+        out_pass(0, 3, 0)
         outgoing(7, 2)
+        out_with_field(1, 3)
         early, late = slice(0, T // 2), slice(T // 2, T)
-        apply_gain(3, early)
-        quant_outg(1, 1)
-        quant_refl(3, early)
-        for n in range(4, 7):
-            outgoing(n, 3)
+        quant_outg(0, 2, 2)
+        apply_gain(2, early)
+        apply_gain(2, late)
+        quant_refl(2, early)
+        quant_refl(2, late)
+        outgoing(4, 3)
+        outgoing(5, 3)
+        outgoing(6, 3)
         out_pass(0, 0, 2)
         outgoing(7, 3)
         for m in range(1, 4):
             out_pass(0, m, 2)
-        apply_gain(3, late)
-        quant_refl(3, late)
+        tiles = [slice(128 * m, 128 * (m + 1)) for m in range(4)]
+        quant_outg(1, 0, 2)
+        apply_gain(3, tiles[0])
+        for m in range(1, 4):
+            apply_gain(3, tiles[m])
+            quant_refl(3, tiles[m - 1])
         quant_outg(1, 2)
+        quant_refl(3, tiles[3])
         quant_outg(1, 3)
-        last_emptied_first(2)
-        for m in range(2):
+        fillers = [(m, grp) for grp in range(2) for m in range(3)] + [(0, 2), (1, 2)]
+        out_pass(1, *fillers.pop(0))
+        for m in range(4):
             out_pass(0, m, 3)
             store(0, m)
-        for m in range(2):
-            for grp in range(2):
-                out_pass(1, m, grp)
-        for m in range(2, 4):
-            out_pass(0, m, 3)
-            store(0, m)
-        for m in range(2):
-            out_pass(1, m, 2)
+            for step in fillers[2 * m : 2 * m + 2]:
+                out_pass(1, *step)
         for m, engine in enumerate((VECTOR, SCALAR)):
             out_pass(1, m, 3)
             store(1, m, engine)
-        for grp in range(GROUPS):
-            out_pass(1, 2, grp)
+        out_pass(1, 2, 2)
+        out_pass(1, 2, 3)
         store(1, 2, VECTOR)
         for part, engine in enumerate((SCALAR, VECTOR)):
             recv = slice(HALF_R // 2 * part, HALF_R // 2 * (part + 1))

@@ -82,26 +82,30 @@ def tile_active_surface_link_s11_kernel(
         dummy = kept("dummy", [P, 1], F32)
         zeros = kept("zeros", [P, 512], BF16)
 
-        ring = list(range(8))
+        free = [(b, None) for b in range(8)]
         bank_of = {}
-        emptied = list(range(8))
 
-        def take_bank(shape=(P, 512), dtype=F32, hold=False):
-            b = ring.pop(0)
-            if not hold:
-                ring.append(b)
+        def take_bank(shape=(P, 512), dtype=F32):
+            pick = 0
+            waits = [i for i in range(len(free)) if free[i][1] is not None]
+            if waits and waits[0] <= len(early_wait):
+                engine = free[waits[0]][1]
+                ahead = max(2 if len(free) > 4 else 1, 2 * len(early_wait))
+                pick = max(i for i in waits if i < ahead and free[i][1] == engine)
+                for i in range(pick):
+                    if free[i][1] == engine:
+                        free[i] = (free[i][0], None)
+            early_wait.clear()
+            b = free.pop(pick)[0]
             return b, psum.tile(list(shape), dtype, name="bank%d" % b, tag="bank%d" % b)
 
-        def note_emptied(b):
-            emptied.remove(b)
-            emptied.append(b)
+        early_wait = []
 
-        def last_emptied_first(count):
-            head = sorted(ring[:count], key=emptied.index, reverse=True)
-            for b in head:
-                ring.remove(b)
-            for b in reversed(head):
-                ring.insert(0, b)
+        def wait_a_step_early():
+            early_wait.append(True)
+
+        def note_emptied(b, engine=SCALAR):
+            free.append((b, engine))
 
         def clear_scale_rows(k):
             nc.vector.memset(rs_raw[k][:].rearrange("p g e -> p (g e)").bitcast(I32), 0)
@@ -120,6 +124,7 @@ def tile_active_surface_link_s11_kernel(
             b, bank = take_bank()
             for i in range(count):
                 nc.tensor.matmul(bank[:], lhsT=zeros[:, 0:P], rhs=zeros[:], start=True, stop=True)
+            free.append((b, None))
 
         def copy(engine, dst, src):
             if engine == VECTOR:
@@ -209,7 +214,7 @@ def tile_active_surface_link_s11_kernel(
                 )
             lo = 1024 * (n % 2)
             empty_words(engine, coef_grp[pair][:, lo : lo + 1024], coef_bank[n])
-            note_emptied(bank_of[("coef", n)])
+            note_emptied(bank_of[("coef", n)], engine)
 
         def quant_coef(n, count=1):
             cols = slice(256 * (n % 2), 256 * (n % 2 + count))
@@ -220,10 +225,10 @@ def tile_active_surface_link_s11_kernel(
             bank_of[("sig", pair)], sig_bank[pair] = take_bank()
             turn_words(sig_bank[pair], [sig_raw[:, 2 * pair + i, :].bitcast(F32) for i in range(2)])
 
-        def empty_sig(pair):
+        def empty_sig(pair, engine=SCALAR):
             dst = sig_grp[:, 256 * pair : 256 * (pair + 1), :].rearrange("p r t -> p (r t)")
-            empty_words(SCALAR, dst, sig_bank[pair])
-            note_emptied(bank_of[("sig", pair)])
+            empty_words(engine, dst, sig_bank[pair])
+            note_emptied(bank_of[("sig", pair)], engine)
 
         def quant_sig():
             quantize(sig_codes[:], sig_scales[:], sig_grp[:].rearrange("p r t -> p (r t)"))
@@ -258,7 +263,7 @@ def tile_active_surface_link_s11_kernel(
             )
 
         def turn_vectors():
-            bank_of["vectors"], bank = take_bank((P, 8, P), BF16, hold=True)
+            bank_of["vectors"], bank = take_bank((P, 8, P), BF16)
             for t in range(SLOTS):
                 nc.tensor.transpose(bank[:, t, :], vec_b[:, 128 * t : 128 * (t + 1)], ident_b[:])
             vec_bank.append(bank)
@@ -267,8 +272,7 @@ def tile_active_surface_link_s11_kernel(
             nc.scalar.copy(out=vec_t[:].rearrange("p r t -> p t r"), in_=vec_bank[0][:, 0:SLOTS, 0 : 2 * GROUPS])
 
         def release_vectors():
-            ring.append(bank_of["vectors"])
-            note_emptied(bank_of["vectors"])
+            note_emptied(bank_of["vectors"], VECTOR)
 
 
         inc_wid, inc_grp = {}, {}
@@ -343,7 +347,7 @@ def tile_active_surface_link_s11_kernel(
                 )
             r0 = HALF_R * (grp % 2) + 128 * (n % 4)
             copy(engine, outg[key][:, r0 : r0 + 128, :], outg_bank[(n, grp)][:].rearrange("p (t r) -> p r t", t=SLOTS))
-            note_emptied(bank_of[("outg", n, grp)])
+            note_emptied(bank_of[("outg", n, grp)], engine)
 
         def outgoing(n, grp, engine=SCALAR):
             fill_outg(n, grp)
@@ -419,7 +423,7 @@ def tile_active_surface_link_s11_kernel(
         def out_pass(h, m, grp, recv=slice(0, HALF_R)):
             key = (h, m, recv.start)
             if key not in out_bank:
-                out_bank[key] = take_bank(hold=True)
+                out_bank[key] = take_bank()
             cols = slice(128 * m, 128 * (m + 1))
             moving = slice(HALF_R * (grp % 2) + recv.start, HALF_R * (grp % 2) + recv.stop)
             nc.tensor.matmul_mx(
@@ -437,8 +441,7 @@ def tile_active_surface_link_s11_kernel(
             res = work.tile([P, HALF_R], F32, name="res", tag="res", bufs=RES_BUFS, align_bytes=64)
             copy(engine, res[:, recv], bank[:, recv])
             nc.sync.dma_start(out=out_rows[m][:, HALF_R * h + recv.start : HALF_R * h + recv.stop], in_=res[:, recv])
-            ring.append(b)
-            note_emptied(b)
+            note_emptied(b, engine)
 
         def out_with_field(grp_out, grp_field):
             out_pass(0, 0, grp_out)
@@ -506,18 +509,21 @@ def tile_active_surface_link_s11_kernel(
         quant_inc(1)
         for n in range(3):
             outgoing(n, 1)
-        last_emptied_first(2)
+        wait_a_step_early()
         outgoing(3, 1)
         pair_of(field_step(0, 0), field_step(0, 1))
         fill_field(0, 2)
-        last_emptied_first(2)
+        wait_a_step_early()
         fill_field(0, 3)
         empty_field(0, 3)
         empty_field(0, 2)
         pair_of(outg_step(0, 2), outg_step(1, 2))
         fill_outg(2, 2)
+        wait_a_step_early()
         fill_outg(3, 2)
         for n in range(4, 8):
+            if n == 5:
+                wait_a_step_early()
             turn_coef(n)
         empty_outg(3, 2)
         empty_outg(2, 2)
@@ -529,25 +535,35 @@ def tile_active_surface_link_s11_kernel(
         widen(2, range(2, 3))
         quant_coef(4, 2)
         widen(2, range(3, 4))
-        interleave_on_gpsimd(2, slice(0, 96))
+        interleave_on_gpsimd(2, slice(0, 88))
+        wait_a_step_early()
+        pair_of(outg_step(0, 3), field_step(1, 0))
+        outgoing(1, 3, VECTOR)
+        field(1, 1)
         apply_gain(0, from_psum=True)
-        for t in range(4):
-            pair_of(outg_step(t, 3), field_step(1, t))
-        outgoing(4, 0, VECTOR)
+        pair_of(outg_step(2, 3), field_step(1, 2))
+        fill_outg(3, 3)
+        wait_a_step_early()
+        field(1, 3)
+        empty_outg(3, 3)
+        outgoing(4, 0)
         quant_coef(6, 2)
-        interleave(2, cols=slice(96, 128))
+        interleave(2, cols=slice(88, 128))
         quant_refl(0)
         quant_outg(0, 0)
         quant_inc(2)
-        interleave_on_gpsimd(3, slice(0, 96))
-        apply_gain(1, from_psum=True)
+        interleave_on_gpsimd(3, slice(0, 88))
         outgoing(5, 0)
-        pair_of(outg_step(4, 1), outg_step(5, 1))
-        pair_of(outg_step(6, 0), outg_step(7, 0))
+        fill_outg(4, 1)
+        wait_a_step_early()
+        outgoing(5, 1)
+        empty_outg(4, 1)
+        outgoing(6, 0)
+        outgoing(7, 0, VECTOR)
+        apply_gain(1, from_psum=True)
         outgoing(6, 1)
-        last_emptied_first(2)
-        outgoing(7, 1, VECTOR)
-        interleave(3, cols=slice(96, 128))
+        outgoing(7, 1)
+        interleave(3, cols=slice(88, 128))
         quant_refl(1)
         quant_inc(3)
         quant_outg(0, 1)
@@ -587,18 +603,18 @@ def tile_active_surface_link_s11_kernel(
         quant_outg(1, 2)
         quant_refl(3, tiles[3])
         quant_outg(1, 3)
-        fillers = [(m, grp) for grp in range(2) for m in range(3)] + [(0, 2), (1, 2)]
-        out_pass(1, *fillers.pop(0))
-        for m in range(4):
+        for m, between in enumerate((((0, 0),), ((0, 1),), ((1, 0), (1, 1)), ((0, 2),))):
             out_pass(0, m, 3)
             store(0, m)
-            for step in fillers[2 * m : 2 * m + 2]:
+            for step in between:
                 out_pass(1, *step)
-        for m, engine in enumerate((VECTOR, SCALAR)):
-            out_pass(1, m, 3)
-            store(1, m, engine)
-        out_pass(1, 2, 2)
-        out_pass(1, 2, 3)
+        out_pass(1, 0, 3)
+        store(1, 0, VECTOR)
+        out_pass(1, 1, 2)
+        out_pass(1, 1, 3)
+        store(1, 1)
+        for grp in range(GROUPS):
+            out_pass(1, 2, grp)
         store(1, 2, VECTOR)
         for part, engine in enumerate((SCALAR, VECTOR)):
             recv = slice(HALF_R // 2 * part, HALF_R // 2 * (part + 1))

@@ -90,7 +90,7 @@ def tile_active_surface_link_s11_kernel(
             waits = [i for i in range(len(free)) if free[i][1] is not None]
             if waits and waits[0] <= len(early_wait):
                 engine = free[waits[0]][1]
-                ahead = max(2 if len(free) > 4 else 1, 2 * len(early_wait))
+                ahead = max(2 if len(free) > 5 else 1, 2 * len(early_wait))
                 pick = max(i for i in waits if i < ahead and free[i][1] == engine)
                 for i in range(pick):
                     if free[i][1] == engine:
@@ -460,8 +460,8 @@ def tile_active_surface_link_s11_kernel(
         load_inc_scale()
         load_sig()
         load_vectors()
-        load_resp(1)
         load_scales(1)
+        load_resp(1)
         load_inc(1)
         load_resp(2)
         load_coef(3)
@@ -493,9 +493,9 @@ def tile_active_surface_link_s11_kernel(
         empty_sig(0)
         empty_sig(1)
         empty_vectors()
-        sort_resp(1)
         interleave(0, slice(0, 1))
         sort_scales(1)
+        sort_resp(1)
         interleave(0, slice(1, 4))
         widen(1, range(1))
         quant_inc(0)
@@ -567,24 +567,19 @@ def tile_active_surface_link_s11_kernel(
         quant_refl(1)
         quant_inc(3)
         quant_outg(0, 1)
-        field(2, 0)
-        field(2, 1)
-        out_pass(0, 0, 0)
-        outgoing(4, 2)
-        field(2, 2)
-        out_pass(0, 1, 0)
-        release_vectors()
-        outgoing(5, 2)
-        field(2, 3)
-        out_pass(0, 2, 0)
-        outgoing(6, 2)
-        out_pass(0, 3, 0)
-        outgoing(7, 2)
-        out_with_field(1, 3)
+        for half in range(2):
+            for t in (2 * half, 2 * half + 1):
+                field(2, t)
+                out_pass(0, t, 0)
+            outgoing(4 + 2 * half, 2)
+            outgoing(5 + 2 * half, 2)
+        for t in range(SLOTS):
+            field(3, t)
+            out_pass(0, t, 1)
         early, late = slice(0, T // 2), slice(T // 2, T)
         quant_outg(0, 2, 2)
-        apply_gain(2, early)
-        apply_gain(2, late)
+        apply_gain(2, early, from_psum=True)
+        apply_gain(2, late, from_psum=True)
         quant_refl(2, early)
         quant_refl(2, late)
         outgoing(4, 3)
@@ -596,10 +591,11 @@ def tile_active_surface_link_s11_kernel(
             out_pass(0, m, 2)
         tiles = [slice(128 * m, 128 * (m + 1)) for m in range(4)]
         quant_outg(1, 0, 2)
-        apply_gain(3, tiles[0])
+        apply_gain(3, tiles[0], from_psum=True)
         for m in range(1, 4):
-            apply_gain(3, tiles[m])
+            apply_gain(3, tiles[m], from_psum=True)
             quant_refl(3, tiles[m - 1])
+        release_vectors()
         quant_outg(1, 2)
         quant_refl(3, tiles[3])
         quant_outg(1, 3)

from contextlib import ExitStack

import concourse.mybir as mybir
from concourse.masks import make_identity

T, A, E, PATHS, R = 512, 512, 2048, 1024, 1024
FLOPS = 2 * (T * A * E + R * PATHS * E + T * E * R)

F32 = mybir.dt.float32
BF16 = mybir.dt.bfloat16
I32 = mybir.dt.int32
U32 = mybir.dt.uint32
U8 = mybir.dt.uint8
FP8 = mybir.dt.float8_e4m3fn
FP8X4 = mybir.dt.float8_e4m3fn_x4
FP4X4 = mybir.dt.float4_e2m1fn_x4
MULT = mybir.AluOpType.mult
TANH = mybir.ActivationFunctionType.Tanh

P = 128
SLOTS = 4
GROUPS = E // 512
RECV_TILES = R // 128
HALF_R = 512
SCALAR, VECTOR = "scalar", "vector"

COEF_LOADS = ((0, 1), (1, 1), (2, 2), (4, 2), (6, 2))
RESP_LOADS = ((0, 1), (1, 1), (2, 2))
SCALE_LOADS = ((0, 1), (1, 3))
INC_LOADS = ((0, 1), (1, 1), (2, 2))

COEF_BUFS = 3
OUTG_BUFS = 4
TANH_BUFS = 2
RES_BUFS = 8
GAIN_RUN = 2
COPY_RUN = 4


def load_of(loads, piece):
    k = max(i for i, (start, count) in enumerate(loads) if start <= piece)
    return k, loads[k][0], loads[k][1]


def tile_active_surface_link_s11_kernel(
    tc, sig, inc_bytes, inc_scale, bias, gain, coef, resp_words, resp_scales, out
):
    nc = tc.nc
    with ExitStack() as ctx:
        keep = ctx.enter_context(tc.tile_pool(name="keep", bufs=1))
        work = ctx.enter_context(tc.tile_pool(name="work", bufs=2))
        psum = ctx.enter_context(tc.psum_pool(name="psum", bufs=1))
        ctx.enter_context(tc.manual_schedule())

        def kept(name, shape, dtype):
            return keep.tile(shape, dtype, name=name, tag=name, align_bytes=64)

        coef_in = [kept("coef_in%d" % n0, [P, w, PATHS], BF16) for n0, w in COEF_LOADS]
        coef_codes = [kept("coef_codes%d_x" % n, [P, 512], U32) for n in range(RECV_TILES // 2)]
        coef_scales = [kept("coef_scales%d" % n, [P, 512], U8) for n in range(RECV_TILES // 2)]
        resp_raw = [kept("resp_raw%d" % k, [P, 2, 1024 * w], U8) for k, (g0, w) in enumerate(RESP_LOADS)]
        resp_perm = [kept("resp_perm%d" % k, [P, 2, 1024 * w], U8) for k, (g0, w) in enumerate(RESP_LOADS)]
        rs_raw = [kept("rs_raw%d" % k, [P, 2, 512 * w], U8) for k, (g0, w) in enumerate(SCALE_LOADS)]
        rs_perm = [kept("rs_perm%d" % k, [P, 2, 512 * w], U8) for k, (g0, w) in enumerate(SCALE_LOADS)]
        inc_b = [kept("inc_b%d" % k, [P, SLOTS, 512 * w], U8) for k, (g0, w) in enumerate(INC_LOADS)]
        inc_sc = kept("inc_sc", [P, SLOTS], F32)
        inc_codes = [kept("inc_codes%d" % g, [P, 512], U32) for g in range(GROUPS)]
        inc_scales = [kept("inc_scales%d" % g, [P, 512], U8) for g in range(GROUPS)]
        sig_raw = kept("sig_raw", [P, 4, A], BF16)
        sig_grp = kept("sig_grp", [P, T, SLOTS], BF16)
        sig_codes = kept("sig_codes", [P, T], U32)
        sig_scales = kept("sig_scales", [P, T], U8)
        refl_codes = [kept("refl_codes%d" % g, [P, T], U32) for g in range(GROUPS)]
        refl_scales = [kept("refl_scales%d" % g, [P, T], U8) for g in range(GROUPS)]
        outg_codes = [[kept("outg_codes%d_%d" % (h, k), [P, 2 * HALF_R], U32) for k in range(2)] for h in range(2)]
        outg_scales = [[kept("outg_scales%d_%d" % (h, k), [P, 2 * HALF_R], U8) for k in range(2)] for h in range(2)]
        ident = kept("ident", [P, P], F32)
        ident_b = kept("ident_b", [P, P], BF16)
        vec_raw = kept("vec_raw", [P, 512], BF16)
        vec_b = kept("vec_b", [P, 512], BF16)
        vec_t = kept("vec_t", [P, 2 * GROUPS, SLOTS], F32)
        dummy = kept("dummy", [P, 1], F32)
        zeros = kept("zeros", [P, 512], BF16)

        free = [(b, None) for b in range(8)]
        bank_of = {}

        def take_bank(shape=(P, 512), dtype=F32):
            pick = 0
            waits = [i for i in range(len(free)) if free[i][1] is not None]
            if waits and waits[0] <= len(early_wait):
                engine = free[waits[0]][1]
                ahead = max(2 if len(free) > 5 else 1, 2 * len(early_wait))
                pick = max(i for i in waits if i < ahead and free[i][1] == engine)
                for i in range(pick):
                    if free[i][1] == engine:
                        free[i] = (free[i][0], None)
            early_wait.clear()
            b = free.pop(pick)[0]
            return b, psum.tile(list(shape), dtype, name="bank%d" % b, tag="bank%d" % b)

        early_wait = []

        def wait_a_step_early():
            early_wait.append(True)

        def note_emptied(b, engine=SCALAR):
            free.append((b, engine))

        def clear_scale_rows(k):
            nc.vector.memset(rs_raw[k][:].rearrange("p g e -> p (g e)").bitcast(I32), 0)

        nc.vector.memset(dummy[:], 0.0)
        nc.vector.memset(ident[:], 0.0)
        nc.vector.memset(zeros[:], 0.0)
        clear_scale_rows(0)
        make_identity(nc, ident[:], nomemset=True)
        clear_scale_rows(1)
        nc.vector.memset(vec_raw[:], 0.0)
        nc.scalar.activation(dummy[:], dummy[:], TANH)
        nc.scalar.copy(out=ident_b[:], in_=ident[:])

        def warm_up(count):
            b, bank = take_bank()
            for i in range(count):
                nc.tensor.matmul(bank[:], lhsT=zeros[:, 0:P], rhs=zeros[:], start=True, stop=True)
            free.append((b, None))

        def copy(engine, dst, src):
            if engine == VECTOR:
                nc.vector.tensor_copy(out=dst, in_=src)
            else:
                nc.scalar.copy(out=dst, in_=src)

        def quantize(codes, scales, values):
            nc.vector.quantize_mx(out=codes.bitcast(FP8X4), scales=scales, in_=values)


        def load_coef(k):
            n0, w = COEF_LOADS[k]
            rows = coef[128 * n0 : 128 * (n0 + w), :]
            nc.sync.dma_start(out=coef_in[k][:], in_=rows.rearrange("(n p) k -> p n k", p=P))

        def load_scales(k):
            g0, w = SCALE_LOADS[k]
            cols = slice(512 * g0, 512 * (g0 + w))
            for r in range(4):
                nc.sync.dma_start(
                    out=rs_raw[k][r:P:32, :, :].bitcast(I32),
                    in_=resp_scales[:, r:16:4, cols].rearrange("g q e -> q g e").bitcast(I32),
                )

        def load_resp(k):
            g0, w = RESP_LOADS[k]
            nc.sync.dma_start(
                out=resp_raw[k][:].bitcast(I32),
                in_=resp_words[:, :, 1024 * g0 : 1024 * (g0 + w)].rearrange("g p b -> p g b").bitcast(I32),
            )

        def load_inc(k):
            g0, w = INC_LOADS[k]
            cols = slice(512 * g0, 512 * (g0 + w))
            nc.sync.dma_start(out=inc_b[k][:], in_=inc_bytes[:, cols].rearrange("(p j) e -> p j e", j=SLOTS))

        def load_inc_scale():
            nc.sync.dma_start(out=inc_sc[:], in_=inc_scale.rearrange("(p j) o -> p (j o)", j=SLOTS))

        def load_sig():
            nc.sync.dma_start(out=sig_raw[:], in_=sig.rearrange("(p m) a -> p m a", m=4))

        def load_vectors():
            for v, vec in enumerate((bias, gain)):
                rows = slice(GROUPS * v, GROUPS * (v + 1))
                nc.sync.dma_start(out=vec_raw[rows, :], in_=vec.rearrange("(g e) -> g e", g=GROUPS))


        coef_bank, coef_grp, sig_bank = {}, {}, {}

        def turn_words(bank, passes, is_split=False):
            for j, words in enumerate(passes):
                for u in range(2):
                    lo = 128 * (2 * j + u)
                    picked = words[:, 128 * u : 128 * (u + 1)] if is_split else words[:, u:256:2]
                    nc.tensor.transpose(bank[:, lo : lo + 128], picked, ident[:])

        coef_split = {}

        def split_coef(k):
            w = COEF_LOADS[k][1]
            coef_split[k] = kept("coef_split%d" % k, [P, w, PATHS // 2], F32)
            nc.vector.tensor_copy(
                out=coef_split[k][:].rearrange("p n (g u c i) -> p (n g) c u i", g=2, u=2, i=4),
                in_=coef_in[k][:].bitcast(F32).rearrange("p n (g c i u) -> p (n g) c u i", g=2, u=2, i=4),
            )

        def empty_words(engine, dst, bank):
            copy(
                engine,
                dst.bitcast(F32).rearrange("p (j r u) -> p j r u", j=2, u=2),
                bank[:].rearrange("p (j u r) -> p j r u", j=2, u=2),
            )

        def turn_coef(n):
            k, n0, w = load_of(COEF_LOADS, n)
            words = coef_split[k][:, n - n0, :] if k in coef_split else coef_in[k][:, n - n0, :].bitcast(F32)
            bank_of[("coef", n)], coef_bank[n] = take_bank()
            turn_words(coef_bank[n], [words[:, 256 * g : 256 * (g + 1)] for g in range(2)], k in coef_split)

        def empty_coef(n, engine=SCALAR):
            pair = n // 2
            if pair not in coef_grp:
                coef_grp[pair] = work.tile(
                    [P, 2048], BF16, name="coef_grp", tag="coef_grp", bufs=COEF_BUFS, align_bytes=64
                )
            lo = 1024 * (n % 2)
            empty_words(engine, coef_grp[pair][:, lo : lo + 1024], coef_bank[n])
            note_emptied(bank_of[("coef", n)], engine)

        def quant_coef(n, count=1):
            cols = slice(256 * (n % 2), 256 * (n % 2 + count))
            values = coef_grp[n // 2][:, SLOTS * cols.start : SLOTS * cols.stop]
            quantize(coef_codes[n // 2][:, cols], coef_scales[n // 2][:, cols], values)

        def turn_sig(pair):
            bank_of[("sig", pair)], sig_bank[pair] = take_bank()
            turn_words(sig_bank[pair], [sig_raw[:, 2 * pair + i, :].bitcast(F32) for i in range(2)])

        def empty_sig(pair, engine=SCALAR):
            dst = sig_grp[:, 256 * pair : 256 * (pair + 1), :].rearrange("p r t -> p (r t)")
            empty_words(engine, dst, sig_bank[pair])
            note_emptied(bank_of[("sig", pair)], engine)

        def quant_sig():
            quantize(sig_codes[:], sig_scales[:], sig_grp[:].rearrange("p r t -> p (r t)"))


        def sort_resp(k):
            nc.vector.tensor_copy(
                out=resp_perm[k][:].bitcast(I32).rearrange("p g (t b w) -> p g t b w", t=SLOTS, w=4),
                in_=resp_raw[k][:].bitcast(I32).rearrange("p g (b t w) -> p g t b w", t=SLOTS, w=4),
            )

        def sort_scales(k):
            nc.vector.tensor_copy(
                out=rs_perm[k][:].bitcast(I32).rearrange("p g (t b w) -> p g t b w", t=SLOTS, w=2),
                in_=rs_raw[k][:].bitcast(I32).rearrange("p g (b t w) -> p g t b w", t=SLOTS, w=2),
            )

        def resp_operand(grp, g, t):
            k, g0, w = load_of(RESP_LOADS, grp)
            lo = 256 * (w * t + grp - g0)
            words = resp_perm[k][:, g, lo : lo + 256].bitcast(FP4X4)
            k, g0, w = load_of(SCALE_LOADS, grp)
            lo = 128 * (w * t + grp - g0)
            return words, rs_perm[k][:, g, lo : lo + 128]

        vec_bank = []

        def sort_vectors():
            nc.vector.tensor_copy(
                out=vec_b[:].rearrange("p (t q i) -> p t q i", t=SLOTS, i=8),
                in_=vec_raw[:].rearrange("p (q t i) -> p t q i", t=SLOTS, i=8),
            )

        def turn_vectors():
            bank_of["vectors"], bank = take_bank((P, 8, P), BF16)
            for t in range(SLOTS):
                nc.tensor.transpose(bank[:, t, :], vec_b[:, 128 * t : 128 * (t + 1)], ident_b[:])
            vec_bank.append(bank)

        def empty_vectors():
            nc.scalar.copy(out=vec_t[:].rearrange("p r t -> p t r"), in_=vec_bank[0][:, 0:SLOTS, 0 : 2 * GROUPS])

        def release_vectors():
            note_emptied(bank_of["vectors"], VECTOR)


        inc_wid, inc_grp = {}, {}

        def widen(k, rows):
            if k not in inc_wid:
                width = 512 * INC_LOADS[k][1]
                inc_wid[k] = work.tile([P, SLOTS, width], BF16, name="inc_wid", tag="inc_wid", align_bytes=64)
            for j in rows:
                nc.vector.tensor_scalar(
                    out=inc_wid[k][:, j, :].rearrange("p (t q i) -> p q t i", t=SLOTS, i=8),
                    in0=inc_b[k][:, j, :].bitcast(FP8).rearrange("p (q t i) -> p q t i", t=SLOTS, i=8),
                    scalar1=inc_sc[:, j : j + 1],
                    scalar2=None,
                    op0=MULT,
                )

        def grouped_inc(grp):
            if grp not in inc_grp:
                inc_grp[grp] = work.tile([P, 512, SLOTS], BF16, name="inc_grp", tag="inc_grp", bufs=1, align_bytes=64)
            return inc_grp[grp]

        def interleave(grp, slots=slice(0, SLOTS), cols=slice(0, 128)):
            k, g0, w = load_of(INC_LOADS, grp)
            src = inc_wid[k][:].rearrange("p j (t g c) -> p g t c j", t=SLOTS, g=w)[:, grp - g0, slots, cols]
            dst = grouped_inc(grp)[:].rearrange("p (t c) j -> p t c j", t=SLOTS)[:, slots, cols]
            nc.vector.tensor_copy(
                out=dst.rearrange("p t (c i) j -> p t c j i", i=COPY_RUN),
                in_=src.rearrange("p t (c i) j -> p t c j i", i=COPY_RUN),
            )

        def interleave_on_gpsimd(grp, cols):
            k, g0, w = load_of(INC_LOADS, grp)
            src = inc_wid[k][:].rearrange("p j (t g c) -> p g t c j", t=SLOTS, g=w)
            nc.gpsimd.tensor_scalar(
                out=grouped_inc(grp)[:].rearrange("p (t c) j -> p t c j", t=SLOTS)[:, :, cols],
                in0=src[:, grp - g0, :, cols],
                scalar1=1.0,
                scalar2=1.0,
                op0=MULT,
                op1=MULT,
            )

        def quant_inc(grp):
            quantize(inc_codes[grp][:], inc_scales[grp][:], inc_grp[grp][:].rearrange("p c j -> p (c j)"))


        outg, outg_bank = {}, {}

        def fill_outg(n, grp):
            bank_of[("outg", n, grp)], bank = take_bank()
            for t in range(SLOTS):
                for g in range(2):
                    words, word_scales = resp_operand(grp, g, t)
                    cols = slice(256 * (n % 2) + 128 * g, 256 * (n % 2) + 128 * (g + 1))
                    nc.tensor.matmul_mx(
                        out=bank[:, 128 * t : 128 * (t + 1)],
                        lhsT=words,
                        lhsT_scale=word_scales,
                        rhs=coef_codes[n // 2][:, cols].bitcast(FP8X4),
                        rhs_scale=coef_scales[n // 2][:, cols],
                        start=(g == 0),
                        stop=(g == 1),
                    )
            outg_bank[(n, grp)] = bank

        def empty_outg(n, grp, engine=SCALAR):
            key = (n // 4, grp // 2)
            if key not in outg:
                outg[key] = work.tile(
                    [P, 2 * HALF_R, SLOTS], BF16, name="outg", tag="outg", bufs=OUTG_BUFS, align_bytes=64
                )
            r0 = HALF_R * (grp % 2) + 128 * (n % 4)
            copy(engine, outg[key][:, r0 : r0 + 128, :], outg_bank[(n, grp)][:].rearrange("p (t r) -> p r t", t=SLOTS))
            note_emptied(bank_of[("outg", n, grp)], engine)

        def outgoing(n, grp, engine=SCALAR):
            fill_outg(n, grp)
            empty_outg(n, grp, engine)

        def quant_outg(h, grp, count=1):
            cols = slice(HALF_R * (grp % 2), HALF_R * (grp % 2 + count))
            values = outg[(h, grp // 2)][:, cols, :].rearrange("p r t -> p (r t)")
            quantize(outg_codes[h][grp // 2][:, cols], outg_scales[h][grp // 2][:, cols], values)


        field_bank, refl_tanh, refl_grp = {}, {}, {}

        def fill_field(grp, t):
            bank_of[("field", grp, t)], bank = take_bank()
            cols = slice(128 * t, 128 * (t + 1))
            nc.tensor.matmul_mx(
                out=bank[:],
                lhsT=inc_codes[grp][:, cols].bitcast(FP8X4),
                lhsT_scale=inc_scales[grp][:, cols],
                rhs=sig_codes[:].bitcast(FP8X4),
                rhs_scale=sig_scales[:],
                start=True,
                stop=True,
            )
            field_bank[(grp, t)] = bank

        def empty_field(grp, t):
            if grp not in refl_tanh:
                refl_tanh[grp] = work.tile([P, SLOTS, T], F32, name="th", tag="th", bufs=TANH_BUFS, align_bytes=64)
            nc.scalar.activation(refl_tanh[grp][:, t, :], field_bank[(grp, t)][:], TANH, bias=vec_t[:, grp, t : t + 1])
            note_emptied(bank_of[("field", grp, t)])

        def field(grp, t):
            fill_field(grp, t)
            empty_field(grp, t)

        def apply_gain(grp, sym=slice(0, T), from_psum=False):
            if grp not in refl_grp:
                refl_grp[grp] = work.tile([P, T, SLOTS], BF16, name="refl", tag="refl", align_bytes=64)
            runs = (sym.stop - sym.start) // GAIN_RUN
            gains = vec_bank[0][:, 0:SLOTS, GROUPS + grp] if from_psum else vec_t[:, GROUPS + grp, :]
            nc.vector.tensor_tensor(
                out=refl_grp[grp][:, sym, :].rearrange("p (c i) t -> p c t i", i=GAIN_RUN),
                in0=refl_tanh[grp][:, :, sym].rearrange("p t (c i) -> p c t i", i=GAIN_RUN),
                in1=gains.unsqueeze(1).unsqueeze(3).to_broadcast([P, runs, SLOTS, GAIN_RUN]),
                op=MULT,
            )

        def quant_refl(grp, sym=slice(0, T)):
            values = refl_grp[grp][:, sym, :].rearrange("p n t -> p (n t)")
            quantize(refl_codes[grp][:, sym], refl_scales[grp][:, sym], values)

        def coef_step(n):
            return lambda: turn_coef(n), lambda: empty_coef(n)

        def outg_step(n, grp):
            return lambda: fill_outg(n, grp), lambda: empty_outg(n, grp)

        def field_step(grp, t):
            return lambda: fill_field(grp, t), lambda: empty_field(grp, t)

        def pair_of(earlier, later):
            earlier[0]()
            later[0]()
            later[1]()
            earlier[1]()


        out_bank = {}
        out_rows = out.rearrange("(p m) r -> m p r", m=4)

        def out_pass(h, m, grp, recv=slice(0, HALF_R)):
            key = (h, m, recv.start)
            if key not in out_bank:
                out_bank[key] = take_bank()
            cols = slice(128 * m, 128 * (m + 1))
            moving = slice(HALF_R * (grp % 2) + recv.start, HALF_R * (grp % 2) + recv.stop)
            nc.tensor.matmul_mx(
                out=out_bank[key][1][:, recv],
                lhsT=refl_codes[grp][:, cols].bitcast(FP8X4),
                lhsT_scale=refl_scales[grp][:, cols],
                rhs=outg_codes[h][grp // 2][:, moving].bitcast(FP8X4),
                rhs_scale=outg_scales[h][grp // 2][:, moving],
                start=(grp == 0),
                stop=(grp == GROUPS - 1),
            )

        def store(h, m, engine=SCALAR, recv=slice(0, HALF_R)):
            b, bank = out_bank[(h, m, recv.start)]
            res = work.tile([P, HALF_R], F32, name="res", tag="res", bufs=RES_BUFS, align_bytes=64)
            copy(engine, res[:, recv], bank[:, recv])
            nc.sync.dma_start(out=out_rows[m][:, HALF_R * h + recv.start : HALF_R * h + recv.stop], in_=res[:, recv])
            note_emptied(b, engine)

        def out_with_field(grp_out, grp_field):
            out_pass(0, 0, grp_out)
            for t in range(1, SLOTS):
                out_pass(0, t, grp_out)
                field(grp_field, t - 1)
            field(grp_field, SLOTS - 1)


        load_coef(0)
        load_coef(1)
        load_coef(2)
        load_resp(0)
        load_scales(0)
        load_inc(0)
        load_inc_scale()
        load_sig()
        load_vectors()
        load_scales(1)
        load_resp(1)
        load_inc(1)
        load_resp(2)
        load_coef(3)
        load_coef(4)
        load_inc(2)
        warm_up(3)
        turn_coef(0)
        turn_coef(1)
        warm_up(1)
        turn_coef(2)
        turn_coef(3)
        warm_up(1)
        for n in range(4):
            empty_coef(n)
        quant_coef(0)
        sort_resp(0)
        sort_scales(0)
        quant_coef(1)
        quant_coef(2)
        widen(0, range(2))
        quant_coef(3)
        widen(0, range(2, 4))
        sort_vectors()
        for n in range(4):
            outgoing(n, 0)
        turn_sig(0)
        turn_sig(1)
        turn_vectors()
        empty_sig(0)
        empty_sig(1)
        empty_vectors()
        interleave(0, slice(0, 1))
        sort_scales(1)
        sort_resp(1)
        interleave(0, slice(1, 4))
        widen(1, range(1))
        quant_inc(0)
        quant_sig()
        widen(1, range(1, 3))
        sort_resp(2)
        widen(1, range(3, 4))
        split_coef(3)
        interleave(1)
        split_coef(4)
        quant_inc(1)
        for n in range(3):
            outgoing(n, 1)
        wait_a_step_early()
        outgoing(3, 1)
        pair_of(field_step(0, 0), field_step(0, 1))
        fill_field(0, 2)
        wait_a_step_early()
        fill_field(0, 3)
        empty_field(0, 3)
        empty_field(0, 2)
        pair_of(outg_step(0, 2), outg_step(1, 2))
        fill_outg(2, 2)
        wait_a_step_early()
        fill_outg(3, 2)
        for n in range(4, 8):
            if n == 5:
                wait_a_step_early()
            turn_coef(n)
        empty_outg(3, 2)
        empty_outg(2, 2)
        widen(2, range(2))
        empty_coef(4, VECTOR)
        empty_coef(5)
        empty_coef(7)
        empty_coef(6)
        widen(2, range(2, 3))
        quant_coef(4, 2)
        widen(2, range(3, 4))
        interleave_on_gpsimd(2, slice(0, 88))
        wait_a_step_early()
        pair_of(outg_step(0, 3), field_step(1, 0))
        outgoing(1, 3, VECTOR)
        field(1, 1)
        apply_gain(0, from_psum=True)
        pair_of(outg_step(2, 3), field_step(1, 2))
        fill_outg(3, 3)
        wait_a_step_early()
        field(1, 3)
        empty_outg(3, 3)
        outgoing(4, 0)
        quant_coef(6, 2)
        interleave(2, cols=slice(88, 128))
        quant_refl(0)
        quant_outg(0, 0)
        quant_inc(2)
        interleave_on_gpsimd(3, slice(0, 88))
        outgoing(5, 0)
        fill_outg(4, 1)
        wait_a_step_early()
        outgoing(5, 1)
        empty_outg(4, 1)
        outgoing(6, 0)
        outgoing(7, 0, VECTOR)
        apply_gain(1, from_psum=True)
        outgoing(6, 1)
        outgoing(7, 1)
        interleave(3, cols=slice(88, 128))
        quant_refl(1)
        quant_inc(3)
        quant_outg(0, 1)
        for half in range(2):
            for t in (2 * half, 2 * half + 1):
                field(2, t)
                out_pass(0, t, 0)
            outgoing(4 + 2 * half, 2)
            outgoing(5 + 2 * half, 2)
        for t in range(SLOTS):
            field(3, t)
            out_pass(0, t, 1)
        early, late = slice(0, T // 2), slice(T // 2, T)
        quant_outg(0, 2, 2)
        apply_gain(2, early, from_psum=True)
        apply_gain(2, late, from_psum=True)
        quant_refl(2, early)
        quant_refl(2, late)
        outgoing(4, 3)
        outgoing(5, 3)
        outgoing(6, 3)
        out_pass(0, 0, 2)
        outgoing(7, 3)
        for m in range(1, 4):
            out_pass(0, m, 2)
        tiles = [slice(128 * m, 128 * (m + 1)) for m in range(4)]
        quant_outg(1, 0, 2)
        apply_gain(3, tiles[0], from_psum=True)
        for m in range(1, 4):
            apply_gain(3, tiles[m], from_psum=True)
            quant_refl(3, tiles[m - 1])
        release_vectors()
        quant_outg(1, 2)
        quant_refl(3, tiles[3])
        quant_outg(1, 3)
        for m, between in enumerate((((0, 0),), ((0, 1),), ((1, 0), (1, 1)), ((0, 2),))):
            out_pass(0, m, 3)
            store(0, m)
            for step in between:
                out_pass(1, *step)
        out_pass(1, 0, 3)
        store(1, 0, VECTOR)
        out_pass(1, 1, 2)
        out_pass(1, 1, 3)
        store(1, 1)
        for grp in range(GROUPS):
            out_pass(1, 2, grp)
        store(1, 2, VECTOR)
        for part, engine in enumerate((SCALAR, VECTOR)):
            recv = slice(HALF_R // 2 * part, HALF_R // 2 * (part + 1))
            for grp in range(GROUPS):
                out_pass(1, 3, grp, recv)
            store(1, 3, engine, recv)
